import numpy as np, ml_dtypes
CORES = [66,74,82,90,194,202,210,218]
N = 8
import mx_ref
BF = ml_dtypes.bfloat16
def gcols(t, e):
    v = np.concatenate([t.reshape(8, 16, -1, 4), np.zeros((8, 16, 1, 4), BF)], axis=2)
    return np.ascontiguousarray(np.stack([v[g][:, e[g]] for g in range(8)])).reshape(128, -1)
def tile(rs):
    return np.stack(rs, axis=2).reshape(128, -1).astype(BF)
def pick(q, e):
    c = np.concatenate([q[0].reshape(128, -1, 4), np.zeros((128, 1, 4), np.uint8)], axis=1); s = np.concatenate([q[1], np.ones((16, 1), np.uint8)], axis=1)
    return (np.ascontiguousarray(c[:, e].reshape(128, -1)), np.ascontiguousarray(s[:, e]))
def join(*qs):
    return (np.concatenate([q[0] for q in qs], axis=1), np.concatenate([q[1] for q in qs], axis=1))
def put(q, e, v):
    c, s = q[0].reshape(128, -1, 4).copy(), q[1].copy(); c[:, e] = v[0].reshape(128, -1, 4); s[:, e] = v[1]
    return (c.reshape(128, -1), s)
def pk(c, s):
    return (np.ascontiguousarray(c), mx_ref.live(s))
def emit(q):
    return q[0], q[1]
def packed(v, rng):
    q = [mx_ref.quantize(np.ascontiguousarray(v[r])) for r in range(N)]
    return np.stack([a for a, b in q]), np.stack([mx_ref.plane(b, rng) for a, b in q])
def values_of_codes():
    e, c = np.zeros((128, 128, 4), np.float32), np.zeros((128, 2, 4), np.uint8)
    e[np.arange(128), np.arange(128), 0] = 1
    c[:127, :, 0] = np.arange(256).reshape(2, 128).T[:127]
    return mx_ref.matmul(mx_ref.quantize(e.reshape(128, 512).astype(BF)), (c.reshape(128, 8), np.full((16, 2), 127, np.uint8))).T.reshape(-1).astype(np.float64)
CODE_VALUE, SCALE_VALUE = values_of_codes(), 2.0 ** (np.arange(256) - 127.0)
def decode(q):
    return (CODE_VALUE[q[0]].reshape(16, 8, -1, 4) * SCALE_VALUE[q[1]][:, None, :, None] + 0.0).reshape(128, -1).astype(np.float32)
def f(rng, *shape):
    return mx_ref.flush((rng.standard_normal(shape, dtype=np.float32) * np.exp2(rng.integers(-2, 3, shape[:-1] + (1,)))).astype(BF))
def wide(rng, *shape, cols=0):
    v = rng.standard_normal(shape, dtype=np.float32) * np.exp2(rng.integers(-12, 13, shape)).astype(np.float32)
    if cols: v *= np.repeat(np.exp2(rng.integers(-cols, cols + 1, shape[:-2] + (1, shape[-1] // 4))) * (rng.random(shape[:-2] + (1, shape[-1] // 4)) > 0.0625), 4, axis=-1).astype(np.float32)
    return mx_ref.flush(v.astype(BF))
C, A, B, E, F, R = 352, 160, 64, 32, 11, 3
STEP = [3, 2]
def order(p):
    return np.argsort(-(p[::16] + np.float32(0.0)), axis=1, kind="stable")
def gput(t, e, h):
    a, b = t.reshape(8, 16, -1, 4).copy(), h.reshape(8, 16, -1, 4)
    for g in range(8): a[g][:, e[g]] = b[g]
    return a.reshape(128, -1)
def big(v):
    v = v.astype(np.float32)
    v[np.abs(v) < np.float32(2.0 ** -16)] = 0
    return v.astype(BF)
def numbers_of(rng):
    return {"x": big(f(rng, N, 128, 4 * C)), "u": np.array(f(rng, N, 128, 512)), "v": np.array(f(rng, N, 128, 512))}
def layers(rng):
    return big(f(rng, N, 128, 2048)).reshape(N, 8, 16, 4, 8, 16, 4)
def apart(w, k):
    w[:, :, :k] = 0
    w[:, :, :, :, :, :k] = 0
    return w
def holding(w, k):
    w = apart(w, k).reshape(N, 128, 4, 128, 4)
    i = np.flatnonzero(np.arange(128) % 16 < k)
    for b in range(4): w[:, i, b, i, b] = 32
    return w
def weights(rng, w):
    c, p = packed(np.ascontiguousarray(w).reshape(N, 128, 2048), rng)
    return {"wc": c, "ws": p}
def signs(rng):
    return np.stack([rng.permutation(8) % 2 * 2.0 - 1.0 for r in range(N)])
def setup_inputs(rng):
    return {**numbers_of(rng), **weights(rng, layers(rng))}
def setup_inputs_ties(rng):
    d = numbers_of(rng)
    e = rng.permutation(N)
    x = d["x"].reshape(N, 8, 16, C, 4)
    for r in range(N):
        k = np.zeros(C, int) if r == e[0] else rng.permutation(C) % 3
        a = x[r][:, :8, :3].copy()
        a[:, :, 2] = 0
        x[r][:, :8] = a[:, :, k]
    x[e[1]] = 0
    u = d["u"].reshape(N, 8, 16, 128, 4)
    u[:, :, 8:, ::16] = 0
    return {"x": x.reshape(N, 128, 4 * C), "u": u.reshape(N, 128, 512), "v": d["v"], **weights(rng, holding(layers(rng), 8))}
def setup_inputs_near(rng):
    d = numbers_of(rng)
    x = np.zeros((N, 8, 16, C, 4), np.float32)
    u = d["u"].reshape(N, 128, 128, 4)
    u[:, :, ::16] = 0
    o, c = rng.permutation(N) % 4, signs(rng)
    upper = np.arange(C) // (C // 2)
    for r in range(N):
        i = (np.arange(C) + rng.integers(0, C, (8, 1))) % C
        if o[r] == 3: i = i % (C // 2) * 2 + upper
        s = (i + 1) // 2
        size = 1.0 if o[r] < 2 else 2.0 ** -4
        g = ((s[:, :, None] >> np.arange(8)) & 1) * np.exp2(np.arange(8) - 23.0) * size
        if o[r] < 2: x[r, :, 0, :, 0] = c[r][:, None]
        if o[r] == 3: x[r, :, 0, :, 0] = (8 + upper) * 2.0 ** -30
        x[r, :, 8] = g[:, :, :4]
        x[r, :, 9] = g[:, :, 4:]
        x[r, :, 10:] = rng.integers(4, 8, (8, 6, C, 4)) * 2.0 ** -20 * size
        k = 1.0 if o[r] == 0 else 2.0 ** -30
        for h in range(0, 128, 16):
            u[r, h, h, 0] = k
            u[r, h + 8:h + 10, h] = k
    w = (np.abs(layers(rng).astype(np.float32)) * np.float32(0.125)).astype(BF)
    return {"x": x.reshape(N, 128, 4 * C).astype(BF), "u": u.reshape(N, 128, 512), "v": d["v"], **weights(rng, holding(w, 10))}
def setup_inputs_huge(rng):
    d = numbers_of(rng)
    c = np.stack([rng.permutation(C) % 2 * 2.0 - 1.0 for r in range(N)])
    c[rng.permutation(N) < N // 2] = -1
    x = (0.6 + 0.2 * rng.random((N, 128, C, 4))) * np.where(c < 0, -2.0 ** 30, 2.0 ** 28)[:, None, :, None]
    u = d["u"].reshape(N, 128, 128, 4)
    a = 2.0 ** 30 * (1 - 0.25 * rng.random((N, 128, 8, 4))) * signs(rng)[:, None, :, None]
    u[:, :, ::16] = a.astype(np.float32).astype(BF)
    return {"x": x.astype(np.float32).reshape(N, 128, 4 * C).astype(BF), "u": u.reshape(N, 128, 512), "v": d["v"], **weights(rng, holding(layers(rng), 16))}
def setup_inputs_levels(rng):
    d = numbers_of(rng)
    x = d["x"].reshape(N, 8, 16, C, 4)
    x[:, :, :8] = 0
    x[:, :, 1, :, 0] = 1
    for r in range(N):
        n = rng.permutation(np.array([0, 1, B - 1, B, B + 1, C - A - B, C - A - max(B, A // 2), rng.integers(0, C - A - B + 1)]))
        way = rng.permutation(8)
        for g in range(8):
            k = rng.permutation(C)[:A]
            if way[g] == 0: k = np.arange(A)
            if way[g] == 1: k = np.arange(C - A, C)
            s = rng.integers(1, 8, C)
            s[k] = rng.integers(8, 16, A)
            rest = np.setdiff1d(np.arange(C), k)[B:]
            e = rng.permutation(rest)[:n[g]]
            s[e] = -s[e]
            x[r, g, 0, :, 0] = (s * 0.125).astype(np.float32).astype(BF)
    u = d["u"].reshape(N, 128, 128, 4)
    u[:, :, ::16] = 0
    for h in range(0, 128, 16): u[:, h, h, 0] = 1
    w = apart(layers(rng), 8)
    half = rng.permutation(N)[:N // 2]
    for g in range(8):
        w[:, g, 1, 0, g, 1, 0] = 64
        for r in half: w[r, g, 1, 0, g, 0, 0] = -0.5
    return {"x": x.reshape(N, 128, 4 * C), "u": u.reshape(N, 128, 512), "v": d["v"], **weights(rng, w)}
def setup_inputs_spread(rng):
    d = setup_inputs(rng)
    d["x"] = big(wide(rng, N, 128, 4 * C, cols=6))
    return d
def check_inputs(d):
    b = []
    for k in ("x", "u", "v"):
        a = np.abs(d[k].astype(np.float32))
        if not (np.isfinite(a).all() and ((a == 0) | (a >= 2.0 ** -30) & (a <= 2.0 ** 30)).all()): b.append("a value of " + k)
    none, least, most = [emit(mx_ref.quantize(np.full((128, 16), k, np.float32).astype(BF)))[1][0, 0] for k in (0.0, 2.0 ** -30, 2.0 ** 30)]
    for r in range(N):
        if ((d["wc"][r] == 0x7F) | (d["wc"][r] == 0xFF)).any(): b.append("wc: a code that is no number")
        s = mx_ref.live(d["ws"][r])
        if ((s != none) & ((s < least) | (s > most))).any(): b.append("ws: a scale out of range")
    return b
def reference(x, u, v, wc, ws):
    qu = [mx_ref.quantize(u[r]) for r in range(N)]
    lay = [pk(wc[r], ws[r]) for r in range(N)]
    kept = [np.concatenate([x[r], np.zeros((128, 4 * C * R), BF)], axis=1) for r in range(N)]
    level = np.zeros((N, 8, C), np.int64)
    border = [decode(mx_ref.quantize(np.ascontiguousarray(x[r - 1][:, 4 * (C - E):]))).astype(BF) for r in range(N)]
    for t in range(R):
        sent = []
        for r in range(N):
            had = level[r].copy()
            o = order(mx_ref.matmul(qu[r], mx_ref.quantize(gcols(kept[r], had * C + np.arange(C)))))
            going, others = o[:, :A], np.sort(o[:, A:], axis=1)
            low = np.argsort(np.take_along_axis(had, others, axis=1), axis=1, kind="stable")[:, :B]
            e = np.concatenate([going, np.take_along_axis(others, low, axis=1)], axis=1)
            l = np.take_along_axis(had, e, axis=1)
            q = (R + 1) * C + e // F
            for k in range(F - 1, 0, -1):
                found = (e % F >= k) & (np.take_along_axis(had, np.maximum(e - k, 0), axis=1) >= l)
                q = np.where(found, l * C + e - k, q)
            a = gcols(kept[r], l * C + e).astype(np.float32)
            b = gcols(np.concatenate([kept[r], border[r]], axis=1), q).astype(np.float32)
            z = mx_ref.quantize(((a + b) * np.float32(0.5)).astype(BF))
            h = tile([mx_ref.matmul(pick(lay[r], np.arange(128 * i, 128 * i + 128)), z) * np.float32(0.03125) for i in range(4)])
            kept[r] = gput(kept[r], (l + 1) * C + e, h)
            np.put_along_axis(level[r], e, l + 1, axis=1)
            sent.append(mx_ref.quantize(gcols(h, np.argsort(going, axis=1)[:, A - E:])))
        if t < R - 1: border = [decode(sent[r - STEP[t]]).astype(BF) for r in range(N)]
    y, ol = np.zeros((N, 128, C), np.float32), np.zeros((N, 8, C), np.float32)
    oc, osc = np.zeros((N, 128, 4 * C), np.uint8), np.zeros((N, 16, C), np.uint8)
    for r in range(N):
        q = mx_ref.quantize(gcols(kept[r], level[r] * C + np.arange(C)))
        y[r] = mx_ref.matmul(mx_ref.quantize(v[r]), q)
        ol[r] = level[r]
        oc[r], osc[r] = emit(q)
    return {"y": y, "ol": ol, "oc": oc, "osc": osc}

@@ -1,0 +1,533 @@
+import numpy as np
+from concourse.mybir import dt, AluOpType as Op, ActivationFunctionType as Fn, AxisListType
+
+C, A, B, E, F, R = 352, 160, 64, 32, 11, 3
+NJ = A + B
+STEP = [1, 3, 2]
+NB = C // 16
+BCOL = [68, 36, 4]
+XCOL = 100
+HCOL = [452, 676, 900]
+ENDC = 1124
+LAND = [64, 32, 0]
+TILES = [(352, [21, 20, 19, "band"]), (288, [18, 17, 16, 15]), (224, [14, 13, 12, 11]),
+         (160, [10, 9, 8, 7]), (128, [6, 5, 4, 3]), (128, [2, 1])]
+ONACT = [21, 20]
+ONVEC = TILES[-1][1]
+HEAD = 288
+ZCH = [0, 8, 20, 32, 46, 56]
+FIN = [0, 14, 22]
+NGW = 134
+
+BF, F32, I32, U16, Q4, U8 = "bfloat16", "float32", "int32", "uint16", "float8_e4m3fn_x4", "uint8"
+
+
+def _sb(n, d):
+    return ("sbuf", [128, n], d)
+
+
+SCRATCH = {
+    "xin": _sb(4 * C, BF), "uin": _sb(512, BF), "vin": _sb(512, BF), "xt": _sb(4 * C, BF),
+    "big": _sb(4 * ENDC, BF), "own": _sb(4 * NJ, BF), "zt": _sb(4 * NJ, BF), "tt": _sb(512, BF), "ng": _sb(4 * NGW, BF),
+    "sm": _sb(C, F32), "hold": _sb(C, F32), "seg": _sb(C, BF), "junk": _sb(16 * 231, BF), "junk2": _sb(2 * C, BF),
+    "cw": _sb(C, F32), "ej": _sb(C, F32), "ew": _sb(NJ, F32), "pk": _sb(C, F32), "tab": _sb(3 * C, F32),
+    "cp": _sb(2 * C, F32), "np_": _sb(2 * C, F32), "go": _sb(C, BF), "cg": _sb(C, BF), "olv": _sb(C, F32), "yb": _sb(C, F32),
+    "rows": _sb(24, F32), "w": _sb(2048, F32), "wi": _sb(512, I32), "wu": _sb(1024, U16),
+    "tabi": _sb(ENDC, F32), "im16": _sb(C, BF), "im4": _sb(NJ, BF), "g128": _sb(128, BF), "d128": _sb(128, BF),
+    "eq16": _sb(C, BF), "eq4": _sb(NJ, F32),
+    "maska": _sb(C, BF), "maskc": _sb(C, BF), "maskd": _sb(NJ, F32), "reset": _sb(C, BF), "segr": _sb(C, BF), "ones": _sb(C, BF),
+    "hi": _sb(C, F32), "bd": _sb(512, BF), "tri": _sb(512, BF), "tru": _sb(512, BF), "ff": _sb(516, BF),
+    "ci": _sb(64, I32), "cf": _sb(512, F32), "cu": _sb(8, U16),
+    "qu": _sb(128, Q4), "su": _sb(128, U8), "qu2": _sb(128, Q4), "su2": _sb(128, U8), "qv": _sb(128, Q4), "sv": _sb(128, U8),
+    "qw": _sb(512, Q4), "sw": _sb(512, U8), "qx0": _sb(C, Q4), "sx0": _sb(C, U8), "qx": _sb(C, Q4), "sx": _sb(C, U8),
+    "qz": _sb(256, Q4), "sz": _sb(256, U8), "qn": _sb(NGW, Q4), "sn": _sb(NGW, U8),
+    "qt0": _sb(128, Q4), "st0": _sb(128, U8), "qt1": _sb(128, Q4), "st1": _sb(128, U8),
+    "ql": _sb(224, Q4), "sl": _sb(224, U8), "qbd": _sb(128, Q4), "sbd": _sb(128, U8),
+    "qtri": _sb(128, Q4), "stri": _sb(128, U8), "qtru": _sb(128, Q4), "stru": _sb(128, U8),
+    "qe": _sb(512, Q4), "se": _sb(512, U8),
+}
+for _k, (_w, _s) in enumerate(TILES):
+    SCRATCH["m%d" % _k] = _sb(4 * _w, BF)
+    SCRATCH["qm%d" % _k] = _sb(_w, Q4)
+    SCRATCH["sm%d" % _k] = _sb(_w, U8)
+for _k in range(8):
+    SCRATCH["ps%d" % _k] = ("psum", [128, 512], F32)
+
+NDMA = 20
+SEMAPHORES = ["g", "v", "a", "t"] + ["d%d" % k for k in range(NDMA)] + ["arr0", "arr1", "arr2", "out0", "out1", "out2"]
+
+
+def rank_program(g, core, T, topo):
+    rank = T.rank_of(core)
+    if rank is None:
+        return
+    n_ranks = len(T.cores)
+    queue = {"g": g, "v": g.vector, "a": g.scalar, "t": g.tensor, "s": g.sync}
+    count = {"g": 0, "v": 0, "a": 0, "t": 0}
+    known = {k: {} for k in queue}
+    seen = {}
+    uses = {}
+    final = {}
+    ndma = [0]
+
+    def V(name, a=0, b=None, s=1):
+        width = SCRATCH[name][1][1]
+        b = width if b is None else b
+        cols = np.zeros(width, bool)
+        cols[a:b:s] = True
+        if name.startswith("ps"):
+            cols[:] = True
+        ap = T[name][:, a:b] if s == 1 else T[name][:, a:b:s]
+        return (ap, [(name, cols)], name, a)
+
+    def sub(v, a, b):
+        return V(v[2], v[3] + a, v[3] + b)
+
+    def ind(win, off):
+        return (win[0].indirect(off[0]), win[1] + off[1])
+
+    def wait(q, sem, n):
+        if known[q].get(sem, 0) >= n:
+            return
+        queue[q].wait_ge(T.sem[sem], n)
+        known[q][sem] = n
+        for k, m in seen.get((sem, n), {}).items():
+            if known[q].get(k, 0) < m:
+                known[q][k] = m
+
+    def order(q, sem, n, reads, writes, chain=False):
+        need = {}
+        regs = [(r, False) for x in reads for r in x[1]] + [(r, True) for x in writes for r in x[1]]
+        for (name, cols), wr in regs:
+            bank = name.startswith("ps")
+            for c2, s2, n2, w2 in uses.get(name, []):
+                if chain and s2 == sem and bank:
+                    continue
+                if (wr or w2 or (bank and s2 != sem)) and (cols & c2).any():
+                    need[s2] = max(need.get(s2, 0), n2)
+        for s2 in sorted(need, key=lambda k: k == q):
+            wait(q, s2, need[s2])
+        for (name, cols), wr in regs:
+            uses.setdefault(name, []).append((cols, sem, n, wr))
+        seen[(sem, n)] = dict(known[q])
+        final[sem] = n
+
+    def op(q, fn, reads, writes, chain=False):
+        n = count[q] + 1
+        order(q, q, n, reads, writes, chain)
+        count[q] = n
+        fn().then_inc(T.sem[q], 1)
+
+    def dma(q, out, in_, reads, writes):
+        sem = "d%d" % ndma[0]
+        ndma[0] += 1
+        order(q, sem, 16, reads, writes)
+        queue[q].dma_start(out, in_).then_inc(T.sem[sem], 16)
+        return sem
+
+    def sc(x):
+        return x[0] if isinstance(x, tuple) else x
+
+    def cols_of(*xs):
+        return [x for x in xs if isinstance(x, tuple)]
+
+    def ts(out, in0, s1, op0, s2=None, op1=None):
+        if op1 is None:
+            op("v", lambda: g.vector.tensor_scalar(out[0], in0[0], sc(s1), None, op0), [in0] + cols_of(s1), [out])
+        else:
+            op("v", lambda: g.vector.tensor_scalar(out[0], in0[0], sc(s1), sc(s2), op0, op1), [in0] + cols_of(s1, s2), [out])
+
+    def tt(out, in0, in1, o):
+        op("v", lambda: g.vector.tensor_tensor(out[0], in0[0], in1[0], o), [in0, in1], [out])
+
+    def cp(out, in_):
+        op("v", lambda: g.vector.tensor_copy(out[0], in_[0]), [in_], [out])
+
+    def ms(out, c):
+        op("v", lambda: g.vector.memset(out[0], c), [], [out])
+
+    def scan(out, d0, d1, init, o0, o1):
+        op("v", lambda: g.vector.tensor_tensor_scan(out[0], d0[0], d1[0], init, o0, o1), [d0, d1], [out])
+
+    def act(out, in_, fn, bias=None, scale=None, acc=None):
+        kw = {}
+        if bias is not None:
+            kw["bias"] = sc(bias)
+        if scale is not None:
+            kw["scale"] = scale
+        if acc is not None:
+            kw["accum_out"] = acc[0]
+        op("a", lambda: g.scalar.activation(out[0], in_[0], fn, **kw), [in_] + cols_of(bias), [out] + cols_of(acc))
+
+    def lin(out, in_, scale, bias):
+        act(out, in_, Fn.Identity, bias=float(bias), scale=float(scale))
+
+    def quant(qn, sn, a, n, in_):
+        q, s = V(qn, a, a + n), V(sn, a, a + n)
+        op("v", lambda: g.vector.quantize_mx(q[0], s[0], in_[0]), [in_], [q, s])
+
+    def mm(bank, wq, ws, wa, xq, xs, xa, n, start=True, stop=True):
+        o = V("ps%d" % bank, 0, n)
+        a, b, c, d = V(wq, wa, wa + 128), V(ws, wa, wa + 128), V(xq, xa, xa + n), V(xs, xa, xa + n)
+        op("t", lambda: g.tensor.matmul_mx(o[0], a[0], b[0], c[0], d[0], start, stop), [a, b, c, d], [o], chain=not start)
+
+    def iota(out, pattern, base, cm, small=True):
+        if small:
+            op("g", lambda: g.iota(out[0], pattern, base, cm, allow_small_or_imprecise_dtypes=True), [], [out])
+        else:
+            op("g", lambda: g.iota(out[0], pattern, base, cm), [], [out])
+
+    def send(t, qn, sn, a):
+        dst = T.cores[(rank + STEP[t]) % n_ranks]
+        rid, pid = topo.addr(dst, core)
+        eng = topo.engines(core, dst)
+        half = len(eng) // 2
+        masks = [sum(1 << e for e in eng[:half]), sum(1 << e for e in eng[half:2 * half])]
+        q, s = V(qn, a, a + E), V(sn, a, a + E)
+        sem = "out%d" % t
+        order("g", sem, 2 * half, [q, s], [])
+        g.remote_dma(T.ql[:, LAND[t]:LAND[t] + E].bitcast(dt.uint8), q[0].bitcast(dt.uint8), T.sem["arr%d" % t], T.sem[sem], pid, rid, masks[0])
+        g.remote_dma(T.sl[:, LAND[t]:LAND[t] + E], s[0], T.sem["arr%d" % t], T.sem[sem], pid, rid, masks[1])
+
+    for t in range(R):
+        src = T.cores[(rank - STEP[t]) % n_ranks]
+        n = 2 * (len(topo.engines(src, core)) // 2)
+        for name in ("ql", "sl"):
+            uses.setdefault(name, []).append((V(name, LAND[t], LAND[t] + E)[1][0][1], "arr%d" % t, n, True))
+        final["arr%d" % t] = n
+
+    top = {"w": 0, "wi": 0, "wu": 0, "cf": 16, "ci": 8}
+
+    def nw(n=NB, name="w"):
+        a = top[name]
+        top[name] = a + n + n % 2
+        return V(name, a, a + n)
+
+    def col(k):
+        return V("cf", k, k + 1)
+
+    def zero_a(name, a, b):
+        while a < b:
+            n = min(C, b - a)
+            act(V(name, a, a + n), V("im16", 0, n), Fn.Copy, scale=0.0)
+            a += n
+
+    half = 2 * C
+    dma("s", T.uin[:], T.u[:], [], [V("uin")])
+    d1 = dma("a", T.xin[:, half:], T.x[:, half:], [], [V("xin", half)])
+    d2 = dma("s", T.xin[:, :half], T.x[:, :half], [], [V("xin", 0, half)])
+    wait("s", d1, 16)
+    wait("s", d2, 16)
+    dma("s", T.qw[:].bitcast(dt.uint8), T.wc[:], [], [V("qw")])
+    dma("s", T.sw[:], T.ws[:], [], [V("sw")])
+    dma("s", T.vin[:], T.v[:], [], [V("vin")])
+
+    RC, GC, AC, TC, C1, C1H, BC0, K0, K1, C2 = range(10)
+    iota(V("im16"), [[0, NB], [1, 16]], 0, 0)
+    iota(V("ci", 0, 1), [[0, 1]], 0, 1, False)
+    iota(V("g128"), [[1, 8], [0, 16]], 0, 0)
+    uo = nw(8, "ci")
+    iota(uo, [[16, 8]], 0, 0, False)
+    iota(V("d128"), [[1, 128]], 0, -1)
+    m16 = nw(NB, "cf")
+    iota(m16, [[16, NB]], 0, 0)
+    iota(V("im4"), [[0, NJ // 4], [1, 4]], 0, 0)
+
+    low = [min(16 * m for m in slots if m != "band") for wd, slots in TILES]
+    zero = nw(3 * NB, "cf")
+    ms(V("ff"), 0.0)
+    ms(V("m5"), 0.0)
+    ms(V("ng"), 0.0)
+    ms(V("rows"), 0.0)
+    ms(zero, 0.0)
+    p = V("ci", 0, 1)
+    ts(V("ci", 2, 3), p, 15, Op.bitwise_and)
+    ts(V("ci", 3, 4), p, 4, Op.arith_shift_right)
+    ts(V("ci", 4, 5), p, 2, Op.arith_shift_right, 3, Op.bitwise_and)
+    ts(V("ci", 5, 6), p, 3, Op.bitwise_and)
+    ts(V("reset"), V("im16"), 0.0, Op.is_equal, -2e29, Op.mult)
+    cp(V("cf", 0, 4), V("ci", 2, 6))
+    ts(V("segr"), V("im16"), 0.0, Op.not_equal)
+    for k in range(5):
+        zero_a("m%d" % k, 4 * low[k], 4 * TILES[k][0])
+    for t in range(4):
+        ts(V("bd", t, 512, 4), V("g128"), col(GC), Op.is_equal)
+    ts(V("eq16"), V("im16"), col(RC), Op.is_equal)
+    lin(V("maska"), V("eq16"), 2e29, -1e29)
+    zero_a("tt", 0, 512)
+    lin(V("maskc"), V("eq16"), 66560.0, -1024.0)
+    tri, tru, bd = V("tri"), V("tru"), V("bd")
+    op("g", lambda: g.affine_select(tri[0], bd[0], [[1, 128], [0, 4]], Op.is_gt, 0.0, 0, -1), [bd], [tri])
+    op("g", lambda: g.affine_select(tru[0], bd[0], [[-1, 128], [0, 4]], Op.is_ge, 0.0, 0, 1), [bd], [tru])
+    cp(V("cu"), uo)
+    quant("qbd", "sbd", 0, 128, V("bd"))
+    ts(V("ff", 3, 515, 4), V("d128"), 0.0, Op.is_equal)
+    bcw, iw = nw(NB, "cf"), nw(NB, "cf")
+    iota(V("tabi", 0, C), [[1, C]], 0, 0)
+    act(V("maskd"), V("im4"), Fn.Abs, bias=col(AC), scale=-1.0)
+    act(V("eq4"), V("maskd"), Fn.Relu, bias=2.0 ** 28 + 2.0 ** 24, scale=-2.0 ** 29)
+    lin(V("maskd"), V("eq4"), 1, -2.0 ** 24)
+    quant("qu", "su", 0, 128, V("uin"))
+    q2, q1, cu = V("qu2"), V("qu"), V("cu")
+    op("v", lambda: g.vector.tensor_copy(q2[0].bitcast(dt.uint32), q1[0].bitcast(dt.uint32).indirect(cu[0])), [q1, cu], [q2])
+    cp(V("su2"), ind(V("su"), cu))
+    for b in range(2):
+        quant("qe", "se", 128 * b, 128, V("ff", 3 - b, 515 - b))
+
+    cur0 = nw(NB, "cf")
+    st = {"lev": None, "cur": cur0}
+    xsrc = "xin"
+
+    for t in range(R):
+        last = t == R - 1
+        qn, sn = ("qx0", "sx0") if t == 0 else ("qx", "sx")
+        if t == 0:
+            quant(qn, sn, C // 2, C // 2, V(xsrc, half))
+            quant(qn, sn, 0, C // 2, V(xsrc, 0, half))
+        else:
+            acc, tf, toff = nw(2), nw(8), nw(8, "wu")
+            for k in range(2):
+                act(V("junk2", k * C, (k + 1) * C), V("cg"), Fn.Sign, bias=col(K0 + k), scale=-1.0, acc=sub(acc, k, k + 1))
+            for k in range(4):
+                lin(sub(tf, 2 * k, 2 * k + 2), acc, 2, 2 * C + k)
+            quant(qn, sn, 0, C, V(xsrc))
+        mm(0, "qu2", "su2", 0, qn, sn, 0, C)
+        mm(2, "qu2", "su2", 0, qn, sn, 0, C)
+        if t == 0:
+            send(0, qn, sn, C - E)
+            iota(V("ones"), [[0, C]], 1, 0)
+            iota(V("tabi", C), [[1, ENDC - C]], C, 0)
+            for b in range(2, 4):
+                quant("qe", "se", 128 * b, 128, V("ff", 3 - b, 515 - b))
+            quant("ql", "sl", 96, 128, V("tt"))
+            act(col(BC0), col(RC), Fn.Identity, bias=15 * 1025.0 - A, scale=-1025.0)
+            act(bcw, m16, Fn.Identity, bias=col(BC0))
+            act(iw, m16, Fn.Identity, bias=col(RC))
+            lin(cur0, iw, 1, XCOL)
+            lin(col(C1), col(AC), -2.0 ** 24, 3 * 2.0 ** 24)
+            act(col(C1H), col(TC), Fn.Identity, bias=col(C1), scale=8192.0)
+            for k in range(R):
+                lin(col(C2 + k), col(TC), 1, -4 * BCOL[k])
+            lin(col(K0), col(RC), 2, 2 * (A - E) + 1)
+            lin(col(K1), col(RC), 2, 2 * (A - E + 16) + 1)
+        else:
+            lev, lf, lu = nw(), nw(), nw(NB, "wu")
+            if t == 1:
+                ts(lev, st["pos"], float(B), Op.is_lt, float(C), Op.mult)
+                quant("qv", "sv", 0, 128, V("vin"))
+            else:
+                sel = nw()
+                ts(sel, st["pos"], float(B), Op.is_lt, float(C), Op.mult)
+                tt(lev, st["lev"], sel, Op.add)
+            thr = [nw() for k in range(t + 1)]
+            for k in range(t + 1):
+                act(thr[k], lev, Fn.Abs, bias=-float(C * k))
+        for a, b in ((HEAD, C), (0, HEAD)):
+            tt(V("sm", a, b), V("ps0", a, b), V("maska", a, b), Op.min)
+            if t > 0 and a > 0:
+                tt(lf, lev, iw, Op.add)
+            elif t > 0:
+                cp(lu, lf)
+            scan(V("hold", a, b), V("reset", a, b), V("sm", a, b), -1e29, Op.add, Op.max)
+        jk = [0]
+
+        def slot(k, e, m):
+            o, s = V("m%d" % k, e, 64 * m, 4), V("hold", 16 * m + 15, 16 * m + 16)
+            j = V("junk", jk[0], jk[0] + 16 * m)
+            jk[0] += 16 * m
+            if m in ONACT:
+                act(j, V("ps2", 0, 16 * m), Fn.Sign, bias=s, scale=-1.0)
+                act(o, j, Fn.Relu, acc=V("rows", m, m + 1))
+            else:
+                ts(o, V("ps0", 0, 16 * m), s, Op.is_lt)
+                if m not in ONVEC:
+                    act(j, o, Fn.Copy, acc=V("rows", m, m + 1))
+
+        def count_tile(k):
+            wd = TILES[k][0]
+            quant("qm%d" % k, "sm%d" % k, 0, wd, V("m%d" % k))
+            if wd > 128:
+                mm(1, "qbd", "sbd", 0, "qm%d" % k, "sm%d" % k, 0, wd, start=k == 0, stop=TILES[k + 1][0] == 128)
+            mm(3, "qbd", "sbd", 0, "qm%d" % k, "sm%d" % k, 0, 128, start=k == 0, stop=k == len(TILES) - 1)
+
+        b1, b2, rk = nw(), nw(), nw()
+        for k, (wd, slots) in enumerate(TILES):
+            for e, m in enumerate(slots):
+                if m == "band":
+                    tt(V("m0", e, 4 * C, 4), V("ps0", 0, C), V("hold"), Op.is_le)
+                else:
+                    slot(k, e, m)
+                if k == 0 and e == 1 and t > 0:
+                    cp(toff, tf)
+                    for j in range(4):
+                        act(V("tt", j, 4 * E, 4), ind(V("xt"), sub(toff, 2 * j, 2 * j + 2)), Fn.Copy)
+                if k == 4 and e == 3 and t == 2:
+                    o1, o2 = nw(), nw(2 * NB)
+                    tt(o1, st["nl"], st["s1"], Op.min)
+                if k > 1 and e == 0:
+                    count_tile(k - 1)
+                if k == 5 and e == 0 and t == 2:
+                    tt(sub(o2, NB, 2 * NB), st["nl"], st["s2"], Op.min)
+                    tt(sub(o2, 0, NB), o1, st["nl0"], Op.max)
+                if k == 1 and e == 0:
+                    scan(V("seg"), V("segr"), V("m0", 3, 4 * C, 4), 0.0, Op.mult, Op.add)
+                if k == 1 and e == 1:
+                    count_tile(0)
+                    tt(b1, bcw, V("seg", 15, C, 16), Op.subtract)
+                    if t > 0:
+                        quant("qt%d" % (t - 1), "st%d" % (t - 1), 0, 128, V("tt"))
+                        send(t, "qt%d" % (t - 1), "st%d" % (t - 1), 0)
+        if t > 0:
+            off = nw(t * NB, "wu")
+            cp(off, st["nl"] if t == 1 else o2)
+        else:
+            quant("qtri", "stri", 0, 128, tri)
+        count_tile(len(TILES) - 1)
+        if t == 0:
+            quant("qtru", "stru", 0, 128, tru)
+            lin(V("pk"), V("tabi", 0, C), 32772, 4 * (XCOL - 1))
+            lin(V("pk", 0, C, F), V("tabi", 0, E), 4 + 32768 * F, 4 * BCOL[0])
+        else:
+            def spread(k):
+                act(V("cp", k * C, (k + 1) * C), ind(V("tabi"), sub(off, k * NB, (k + 1) * NB)), Fn.Copy, scale=4.0)
+                lin(V("cp", k * C + F - 1, (k + 1) * C, F), V("tabi", 0, E), 4, 4 * (BCOL[t] + 1))
+                act(V("np_", k * C, (k + 1) * C), V("cp", k * C, (k + 1) * C), Fn.Relu, bias=1.0, scale=-1.0)
+
+            def nearest(k):
+                scan(V("tab", (k + 1) * C + 1, (k + 2) * C), V("np_", k * C, (k + 1) * C - 1), V("cp", k * C, (k + 1) * C - 1),
+                     4.0 * BCOL[t], Op.mult, Op.add)
+            spread(0)
+        for e, m in enumerate(ONVEC):
+            o, i = V("rows", m, m + 1), V("m5", e, 64 * m, 4)
+            op("v", lambda: g.vector.tensor_reduce(o[0], i[0], AxisListType.X, Op.add), [i], [o])
+        scan(V("cw", 128), V("maskc", 128), V("ps1", 128, C), 0.0, Op.add, Op.min)
+        tt(b2, b1, V("rows", 0, NB), Op.subtract)
+        scan(V("cw", 0, 128), V("maskc", 0, 128), V("ps3", 0, 128), 0.0, Op.add, Op.min)
+        tt(rk, V("cw", 15, C, 16), b2, Op.add)
+        n = (t + 1) * NB
+        for k in range(t + 1):
+            o = V("ng", 8 * (1 + k * NB), 8 * (1 + (k + 1) * NB), 8)
+            if t == 0:
+                ts(o, rk, 0.0, Op.is_ge)
+            else:
+                tt(o, rk, thr[k], Op.is_ge)
+        nn = max(128, 2 * n)
+        quant("qn", "sn", 0, nn + 2, V("ng", 0, 4 * (nn + 2)))
+        mm(3, "qtri", "stri", 0, "qn", "sn", 2, nn, stop=False)
+        mm(3, "qtru", "stru", 0, "qn", "sn", 0, nn, start=False)
+        pr = nw(4 * NB)
+        ts(sub(pr, n, n + NB), rk, 0.0, Op.min)
+        if t == 0:
+            act(V("big", 4 * XCOL, 4 * (XCOL + C)), V("xin"), Fn.Copy, scale=0.5)
+        else:
+            nearest(0)
+            if t == 2:
+                spread(1)
+        for b in range(4):
+            mm(4 + b, "qe", "se", 128 * b, "ql", "sl", LAND[t], 128)
+        od, pos, posu = nw(n), nw(), nw(NB, "wu")
+        scan(od, V("ps3", 0, 2 * n, 2), sub(zero, 0, n), 0.0, Op.add, Op.add)
+        tt(sub(pr, 0, n), od, V("ng", 8, 8 * (n + 1), 8), Op.mult)
+        if t == 0:
+            tt(pos, sub(pr, 0, NB), sub(pr, NB, 2 * NB), Op.add)
+        elif t == 1:
+            h = nw()
+            tt(h, sub(pr, 0, NB), sub(pr, NB, 2 * NB), Op.add)
+            tt(pos, h, sub(pr, 2 * NB, 3 * NB), Op.add)
+            tt(V("pk"), ind(V("tab", 0, 2 * C), lu), V("hi"), Op.add)
+        else:
+            h = nw(2 * NB)
+            tt(h, sub(pr, 0, 2 * NB), sub(pr, 2 * NB, 4 * NB), Op.add)
+            tt(pos, sub(h, 0, NB), sub(h, NB, 2 * NB), Op.add)
+            nearest(1)
+        ts(posu, pos, float(A), Op.add)
+        if t == 2:
+            tt(V("pk"), ind(V("tab"), lu), V("hi"), Op.add)
+        ej = V("ej")
+        op("v", lambda: g.vector.tensor_copy(ej[0].indirect(posu[0]), T.pk[:]), [V("pk"), posu], [ej])
+        for b in range(4):
+            act(V("big", 4 * BCOL[t] + b, 4 * (BCOL[t] + E), 4), V("ps%d" % (4 + b), 0, E), Fn.Copy, scale=0.5)
+        pb, s0, nl, cur = nw(), nw(), nw(), nw()
+        lin(pb, pos, 1, A + HCOL[t])
+        lin(s0, pos, -1e4, (B - 0.5) * 1e4)
+        if not last:
+            act(V("go"), ind(V("tabi", 0, C), posu), Fn.Sign, bias=A - 0.5, scale=-1.0)
+        if t == 0:
+            act(V("hi"), V("tabi", 0, C), Fn.Copy, scale=32768.0)
+            lin(V("tab", 0, C), V("tabi", 0, C), 4, 4 * (XCOL - 1))
+            st["nl0"] = nl
+        if not last:
+            lin(V("tab", 0, C, F), V("tabi", 0, E), 4, 4 * BCOL[t + 1])
+            lin(V("tab", C, 3 * C, C), V("tabi", 0, 2), 0, 4 * BCOL[t + 1])
+        if t == 1:
+            st["s1"], st["s2"] = nw(), nw()
+            lin(st["s1"], lev, -8, 4 * C)
+            lin(st["s2"], lev, 8, -4 * C)
+        if last:
+            sel, lev3, lu3 = nw(), nw(), nw(NB, "wu")
+            act(sel, s0, Fn.Sign)
+            lin(lev3, lev, 2.0 / C, 1.25)
+        scan(V("ew"), V("maskd"), V("ej", 0, NJ), 0.0, Op.add, Op.min)
+        nq = NJ // 4
+        vi, lo_, hu, lou = nw(nq, "wi"), nw(nq, "wi"), nw(nq, "wu"), nw(nq, "wu")
+        ts(hu, V("ew", 3, NJ, 4), col(C1H), Op.add, 2.0 ** -13, Op.mult)
+        ts(vi, V("ew", 3, NJ, 4), col(C1), Op.add, col(C2 + t), Op.add)
+        tt(nl, pb, s0, Op.min)
+        ts(lo_, vi, 8191, Op.bitwise_and)
+        tt(cur, nl, st["cur"], Op.max)
+        cp(lou, lo_)
+        for a, b in zip(ZCH, ZCH[1:]):
+            act(V("own", 16 * a, 16 * b), ind(V(xsrc), sub(hu, a, b)), Fn.Copy, scale=0.5)
+        for a, b in zip(ZCH, ZCH[1:]):
+            tt(V("zt", 16 * a, 16 * b), ind(V("big", 4 * BCOL[t], 4 * HCOL[t]), sub(lou, a, b)), V("own", 16 * a, 16 * b), Op.add)
+            if b == 32 or b == nq:
+                z0, q0, bank = (0, 0, 4) if b == 32 else (NJ - 128, 128, 0)
+                quant("qz", "sz", q0, 128, V("zt", 4 * z0, 4 * z0 + 512))
+                for k in range(4):
+                    mm(bank + k, "qw", "sw", 128 * k, "qz", "sz", q0, 128)
+        xo = nw(4 * NB, "wu")
+        for k in range(4):
+            ts(sub(xo, k * NB, (k + 1) * NB), cur, 4.0, Op.mult, float(k - 4 * XCOL), Op.add)
+        for b in range(4):
+            act(V("big", 4 * HCOL[t] + b, 4 * (HCOL[t] + 128), 4), V("ps%d" % (4 + b), 0, 128), Fn.Copy, scale=2.0 ** -6)
+        for b in range(4):
+            o, i = V("big", 4 * (HCOL[t] + 128) + b, 4 * (HCOL[t] + NJ), 4), V("ps%d" % b, 256 - NJ, 128)
+            if b != 2:
+                ts(o, i, 2.0 ** -6, Op.mult)
+            else:
+                act(o, i, Fn.Copy, scale=2.0 ** -6)
+        if not last:
+            scan(V("cg"), V("go"), V("ones"), 0.0, Op.add, Op.add)
+        else:
+            tt(lev3, lev3, sel, Op.add)
+        win = V("big", 4 * XCOL, 4 * (HCOL[t] + NJ))
+        pieces = FIN if last else [0, NB]
+        for j, (a, b) in enumerate(zip(pieces, pieces[1:])):
+            for k in range(4):
+                o, i = V("xt", 64 * a + k, 64 * b, 4), ind(win, sub(xo, k * NB + a, k * NB + b))
+                if k < 2:
+                    ts(o, i, 2.0, Op.mult)
+                else:
+                    act(o, i, Fn.Copy, scale=2.0)
+            if last:
+                if j == 0:
+                    cp(lu3, lev3)
+                a, b = 16 * a, 16 * b
+                quant("qx", "sx", a, b - a, V("xt", 4 * a, 4 * b))
+                mm(j, "qv", "sv", 0, "qx", "sx", a, b - a)
+                dma("s", T.oc[:, 4 * a:4 * b], T.qx[:, a:b].bitcast(dt.uint8), [V("qx", a, b)], [])
+        xsrc = "xt"
+        st.update(nl=nl, cur=cur, pos=pos)
+        if t > 0:
+            st["lev"] = lev
+
+    act(V("olv"), ind(V("tabi", 0, 16), lu3), Fn.Copy, scale=0.5)
+    dma("a", T.ol[:], T.olv[0:128:16, :], [V("olv")], [])
+    for k in range(4):
+        dma("a", T.osc[4 * k:4 * k + 4, :], T.sx[32 * k:32 * k + 4, :], [V("sx")], [])
+    for j, (a, b) in enumerate(zip(FIN, FIN[1:])):
+        a, b = 16 * a, 16 * b
+        cp(V("yb", a, b), V("ps%d" % j, 0, b - a))
+        dma("s", T.y[:, a:b], T.yb[:, a:b], [V("yb", a, b)], [])
+    for sem, n in final.items():
+        wait("g", sem, n)

@@ -14,7 +14,7 @@ TILES = [(352, [21, 20, 19, "band"]), (288, [18, 17, 16, 15]), (224, [14, 13, 12
          (160, [10, 9, 8, 7]), (128, [6, 5, 4, 3]), (128, [2, 1])]
 ONACT = [21, 20]
 ONVEC = TILES[-1][1]
-HEAD = 288
+HEAD = C - 128
 ZCH = [0, 8, 20, 32, 46, 56]
 FIN = [0, 14, 22]
 NGW = 134
@@ -212,15 +212,14 @@ def rank_program(g, core, T, topo):
             act(V(name, a, a + n), V("im16", 0, n), Fn.Copy, scale=0.0)
             a += n
 
-    half = 2 * C
+    cut = 4 * HEAD
     dma("s", T.uin[:], T.u[:], [], [V("uin")])
-    d1 = dma("a", T.xin[:, half:], T.x[:, half:], [], [V("xin", half)])
-    d2 = dma("s", T.xin[:, :half], T.x[:, :half], [], [V("xin", 0, half)])
+    d1 = dma("a", T.xin[:, cut:], T.x[:, cut:], [], [V("xin", cut)])
+    d2 = dma("s", T.xin[:, :cut], T.x[:, :cut], [], [V("xin", 0, cut)])
     wait("s", d1, 16)
     wait("s", d2, 16)
     dma("s", T.qw[:].bitcast(dt.uint8), T.wc[:], [], [V("qw")])
     dma("s", T.sw[:], T.ws[:], [], [V("sw")])
-    dma("s", T.vin[:], T.v[:], [], [V("vin")])
 
     RC, GC, AC, TC, C1, C1H, BC0, K0, K1, C2 = range(10)
     iota(V("im16"), [[0, NB], [1, 16]], 0, 0)
@@ -240,6 +239,8 @@ def rank_program(g, core, T, topo):
     ms(V("ng"), 0.0)
     ms(V("rows"), 0.0)
     ms(zero, 0.0)
+    runs = [nw((k + 2) * NB, "cf") for k in range(R)]
+    ms(V("cf", runs[0][3], runs[2][3] + 4 * NB), 1.0)
     p = V("ci", 0, 1)
     ts(V("ci", 2, 3), p, 15, Op.bitwise_and)
     ts(V("ci", 3, 4), p, 4, Op.arith_shift_right)
@@ -247,6 +248,8 @@ def rank_program(g, core, T, topo):
     ts(V("ci", 5, 6), p, 3, Op.bitwise_and)
     ts(V("reset"), V("im16"), 0.0, Op.is_equal, -2e29, Op.mult)
     cp(V("cf", 0, 4), V("ci", 2, 6))
+    for k in range(R):
+        ms(V("cf", runs[k][3], runs[k][3] + (k + 2) * NB, k + 2), 0.0)
     ts(V("segr"), V("im16"), 0.0, Op.not_equal)
     for k in range(5):
         zero_a("m%d" % k, 4 * low[k], 4 * TILES[k][0])
@@ -262,10 +265,19 @@ def rank_program(g, core, T, topo):
     cp(V("cu"), uo)
     quant("qbd", "sbd", 0, 128, V("bd"))
     ts(V("ff", 3, 515, 4), V("d128"), 0.0, Op.is_equal)
-    bcw, iw = nw(NB, "cf"), nw(NB, "cf")
+    bcw, iw, cur0 = nw(NB, "cf"), nw(NB, "cf"), nw(NB, "cf")
     iota(V("tabi", 0, C), [[1, C]], 0, 0)
-    act(V("maskd"), V("im4"), Fn.Abs, bias=col(AC), scale=-1.0)
-    act(V("eq4"), V("maskd"), Fn.Relu, bias=2.0 ** 28 + 2.0 ** 24, scale=-2.0 ** 29)
+    ts(V("eq4"), V("im4"), col(AC), Op.is_equal, 2.0 ** 28 + 2.0 ** 24, Op.mult)
+    lin(col(BC0), col(RC), -1025, 15 * 1025 - A)
+    lin(col(C1), col(AC), -2.0 ** 24, 3 * 2.0 ** 24)
+    act(iw, m16, Fn.Identity, bias=col(RC))
+    for k in range(R):
+        lin(col(C2 + k), col(TC), 1, -4 * BCOL[k])
+    lin(col(K0), col(RC), 2, 2 * (A - E) + 1)
+    lin(col(K1), col(RC), 2, 2 * (A - E + 16) + 1)
+    act(bcw, m16, Fn.Identity, bias=col(BC0))
+    act(col(C1H), col(TC), Fn.Identity, bias=col(C1), scale=8192.0)
+    lin(cur0, iw, 1, XCOL)
     lin(V("maskd"), V("eq4"), 1, -2.0 ** 24)
     quant("qu", "su", 0, 128, V("uin"))
     q2, q1, cu = V("qu2"), V("qu"), V("cu")
@@ -274,62 +286,41 @@ def rank_program(g, core, T, topo):
     for b in range(2):
         quant("qe", "se", 128 * b, 128, V("ff", 3 - b, 515 - b))
 
-    cur0 = nw(NB, "cf")
-    st = {"lev": None, "cur": cur0}
+    st = {"cur": cur0}
     xsrc = "xin"
 
     for t in range(R):
         last = t == R - 1
         qn, sn = ("qx0", "sx0") if t == 0 else ("qx", "sx")
-        if t == 0:
-            quant(qn, sn, C // 2, C // 2, V(xsrc, half))
-            quant(qn, sn, 0, C // 2, V(xsrc, 0, half))
-        else:
+        if t > 0:
+            lev, lf, lu = st["sel"] if t == 1 else st["lev2"], nw(), nw(NB, "wu")
             acc, tf, toff = nw(2), nw(8), nw(8, "wu")
             for k in range(2):
                 act(V("junk2", k * C, (k + 1) * C), V("cg"), Fn.Sign, bias=col(K0 + k), scale=-1.0, acc=sub(acc, k, k + 1))
+            thr = [nw() for k in range(t + 1)]
+            for k in range(t + 1):
+                act(thr[k], lev, Fn.Abs, bias=-float(C * k))
             for k in range(4):
                 lin(sub(tf, 2 * k, 2 * k + 2), acc, 2, 2 * C + k)
-            quant(qn, sn, 0, C, V(xsrc))
+        quant(qn, sn, HEAD, 128, V(xsrc, 4 * HEAD))
+        mm(1, "qu2", "su2", 0, qn, sn, HEAD, 128)
+        quant(qn, sn, 0, HEAD, V(xsrc, 0, 4 * HEAD))
         mm(0, "qu2", "su2", 0, qn, sn, 0, C)
         mm(2, "qu2", "su2", 0, qn, sn, 0, C)
         if t == 0:
             send(0, qn, sn, C - E)
+            dma("g", T.vin[:], T.v[:], [], [V("vin")])
             iota(V("ones"), [[0, C]], 1, 0)
             iota(V("tabi", C), [[1, ENDC - C]], C, 0)
-            for b in range(2, 4):
-                quant("qe", "se", 128 * b, 128, V("ff", 3 - b, 515 - b))
-            quant("ql", "sl", 96, 128, V("tt"))
-            act(col(BC0), col(RC), Fn.Identity, bias=15 * 1025.0 - A, scale=-1025.0)
-            act(bcw, m16, Fn.Identity, bias=col(BC0))
-            act(iw, m16, Fn.Identity, bias=col(RC))
-            lin(cur0, iw, 1, XCOL)
-            lin(col(C1), col(AC), -2.0 ** 24, 3 * 2.0 ** 24)
-            act(col(C1H), col(TC), Fn.Identity, bias=col(C1), scale=8192.0)
-            for k in range(R):
-                lin(col(C2 + k), col(TC), 1, -4 * BCOL[k])
-            lin(col(K0), col(RC), 2, 2 * (A - E) + 1)
-            lin(col(K1), col(RC), 2, 2 * (A - E + 16) + 1)
+            quant("qe", "se", 256, 128, V("ff", 1, 513))
+        tt(V("sm", HEAD), V("ps1", 0, 128), V("maska", HEAD), Op.min)
+        if t > 0:
+            tt(lf, lev, iw, Op.add)
         else:
-            lev, lf, lu = nw(), nw(), nw(NB, "wu")
-            if t == 1:
-                ts(lev, st["pos"], float(B), Op.is_lt, float(C), Op.mult)
-                quant("qv", "sv", 0, 128, V("vin"))
-            else:
-                sel = nw()
-                ts(sel, st["pos"], float(B), Op.is_lt, float(C), Op.mult)
-                tt(lev, st["lev"], sel, Op.add)
-            thr = [nw() for k in range(t + 1)]
-            for k in range(t + 1):
-                act(thr[k], lev, Fn.Abs, bias=-float(C * k))
-        for a, b in ((HEAD, C), (0, HEAD)):
-            tt(V("sm", a, b), V("ps0", a, b), V("maska", a, b), Op.min)
-            if t > 0 and a > 0:
-                tt(lf, lev, iw, Op.add)
-            elif t > 0:
-                cp(lu, lf)
-            scan(V("hold", a, b), V("reset", a, b), V("sm", a, b), -1e29, Op.add, Op.max)
-        jk = [0]
+            quant("qe", "se", 384, 128, V("ff", 0, 512))
+        scan(V("hold", HEAD), V("reset", HEAD), V("sm", HEAD), -1e29, Op.add, Op.max)
+        tt(V("sm", 0, HEAD), V("ps0", 0, HEAD), V("maska", 0, HEAD), Op.min)
+        jk, signs = [0], []
 
         def slot(k, e, m):
             o, s = V("m%d" % k, e, 64 * m, 4), V("hold", 16 * m + 15, 16 * m + 16)
@@ -337,7 +328,10 @@ def rank_program(g, core, T, topo):
             jk[0] += 16 * m
             if m in ONACT:
                 act(j, V("ps2", 0, 16 * m), Fn.Sign, bias=s, scale=-1.0)
-                act(o, j, Fn.Relu, acc=V("rows", m, m + 1))
+                signs.append((o, j, m))
+                if m == ONACT[-1]:
+                    for o, j, m in signs:
+                        act(o, j, Fn.Relu, acc=V("rows", m, m + 1))
             else:
                 ts(o, V("ps0", 0, 16 * m), s, Op.is_lt)
                 if m not in ONVEC:
@@ -354,32 +348,27 @@ def rank_program(g, core, T, topo):
         for k, (wd, slots) in enumerate(TILES):
             for e, m in enumerate(slots):
                 if m == "band":
-                    tt(V("m0", e, 4 * C, 4), V("ps0", 0, C), V("hold"), Op.is_le)
-                else:
-                    slot(k, e, m)
-                if k == 0 and e == 1 and t > 0:
+                    scan(V("hold", 0, HEAD), V("reset", 0, HEAD), V("sm", 0, HEAD), -1e29, Op.add, Op.max)
+                    continue
+                if k == 1 and e == 1:
+                    tt(V("m0", 3, 4 * C, 4), V("ps0", 0, C), V("hold"), Op.is_le)
+                slot(k, e, m)
+                if k == 0 and e == 2 and t > 0:
                     cp(toff, tf)
                     for j in range(4):
                         act(V("tt", j, 4 * E, 4), ind(V("xt"), sub(toff, 2 * j, 2 * j + 2)), Fn.Copy)
-                if k == 4 and e == 3 and t == 2:
-                    o1, o2 = nw(), nw(2 * NB)
-                    tt(o1, st["nl"], st["s1"], Op.min)
                 if k > 1 and e == 0:
                     count_tile(k - 1)
-                if k == 5 and e == 0 and t == 2:
-                    tt(sub(o2, NB, 2 * NB), st["nl"], st["s2"], Op.min)
-                    tt(sub(o2, 0, NB), o1, st["nl0"], Op.max)
-                if k == 1 and e == 0:
-                    scan(V("seg"), V("segr"), V("m0", 3, 4 * C, 4), 0.0, Op.mult, Op.add)
                 if k == 1 and e == 1:
+                    scan(V("seg"), V("segr"), V("m0", 3, 4 * C, 4), 0.0, Op.mult, Op.add)
+                if k == 1 and e == 3:
                     count_tile(0)
                     tt(b1, bcw, V("seg", 15, C, 16), Op.subtract)
-                    if t > 0:
-                        quant("qt%d" % (t - 1), "st%d" % (t - 1), 0, 128, V("tt"))
-                        send(t, "qt%d" % (t - 1), "st%d" % (t - 1), 0)
+                if k == 2 and e == 1 and t > 0:
+                    quant("qt%d" % (t - 1), "st%d" % (t - 1), 0, 128, V("tt"))
+                    send(t, "qt%d" % (t - 1), "st%d" % (t - 1), 0)
         if t > 0:
-            off = nw(t * NB, "wu")
-            cp(off, st["nl"] if t == 1 else o2)
+            cp(lu, lf)
         else:
             quant("qtri", "stri", 0, 128, tri)
         count_tile(len(TILES) - 1)
@@ -401,14 +390,18 @@ def rank_program(g, core, T, topo):
             o, i = V("rows", m, m + 1), V("m5", e, 64 * m, 4)
             op("v", lambda: g.vector.tensor_reduce(o[0], i[0], AxisListType.X, Op.add), [i], [o])
         scan(V("cw", 128), V("maskc", 128), V("ps1", 128, C), 0.0, Op.add, Op.min)
-        tt(b2, b1, V("rows", 0, NB), Op.subtract)
+        tt(b2, V("rows", 0, NB), b1, Op.subtract)
         scan(V("cw", 0, 128), V("maskc", 0, 128), V("ps3", 0, 128), 0.0, Op.add, Op.min)
-        tt(rk, V("cw", 15, C, 16), b2, Op.add)
+        if t > 0:
+            tt(rk, V("cw", 15, C, 16), b2, Op.subtract)
+        else:
+            quant("ql", "sl", 96, 128, V("tt"))
         n = (t + 1) * NB
         for k in range(t + 1):
             o = V("ng", 8 * (1 + k * NB), 8 * (1 + (k + 1) * NB), 8)
             if t == 0:
-                ts(o, rk, 0.0, Op.is_ge)
+                tt(o, V("cw", 15, C, 16), b2, Op.is_ge)
+                tt(rk, V("cw", 15, C, 16), b2, Op.subtract)
             else:
                 tt(o, rk, thr[k], Op.is_ge)
         nn = max(128, 2 * n)
@@ -416,8 +409,10 @@ def rank_program(g, core, T, topo):
         mm(3, "qtri", "stri", 0, "qn", "sn", 2, nn, stop=False)
         mm(3, "qtru", "stru", 0, "qn", "sn", 0, nn, start=False)
         pr = nw(4 * NB)
-        ts(sub(pr, n, n + NB), rk, 0.0, Op.min)
+        w0 = pr[3]
+        ts(V("w", w0, w0 + (t + 2) * NB, t + 2), rk, 0.0, Op.min)
         if t == 0:
+            quant("qv", "sv", 0, 128, V("vin"))
             act(V("big", 4 * XCOL, 4 * (XCOL + C)), V("xin"), Fn.Copy, scale=0.5)
         else:
             nearest(0)
@@ -425,31 +420,25 @@ def rank_program(g, core, T, topo):
                 spread(1)
         for b in range(4):
             mm(4 + b, "qe", "se", 128 * b, "ql", "sl", LAND[t], 128)
-        od, pos, posu = nw(n), nw(), nw(NB, "wu")
+        od, posu, sums = nw(n), nw(NB, "wu"), nw(4 * NB)
         scan(od, V("ps3", 0, 2 * n, 2), sub(zero, 0, n), 0.0, Op.add, Op.add)
-        tt(sub(pr, 0, n), od, V("ng", 8, 8 * (n + 1), 8), Op.mult)
-        if t == 0:
-            tt(pos, sub(pr, 0, NB), sub(pr, NB, 2 * NB), Op.add)
-        elif t == 1:
-            h = nw()
-            tt(h, sub(pr, 0, NB), sub(pr, NB, 2 * NB), Op.add)
-            tt(pos, h, sub(pr, 2 * NB, 3 * NB), Op.add)
+        if t == 1:
             tt(V("pk"), ind(V("tab", 0, 2 * C), lu), V("hi"), Op.add)
-        else:
-            h = nw(2 * NB)
-            tt(h, sub(pr, 0, 2 * NB), sub(pr, 2 * NB, 4 * NB), Op.add)
-            tt(pos, sub(h, 0, NB), sub(h, NB, 2 * NB), Op.add)
+        for k in range(t + 1):
+            tt(V("w", w0 + k + 1, w0 + (t + 2) * NB, t + 2), sub(od, k * NB, (k + 1) * NB),
+               V("ng", 8 * (1 + k * NB), 8 * (1 + (k + 1) * NB), 8), Op.mult)
+        scan(sub(sums, 0, n + NB), sub(runs[t], 0, n + NB), sub(pr, 0, n + NB), 0.0, Op.mult, Op.add)
+        pos = V("w", sums[3] + t + 1, sums[3] + n + NB, t + 2)
+        if t == 2:
             nearest(1)
         ts(posu, pos, float(A), Op.add)
         if t == 2:
             tt(V("pk"), ind(V("tab"), lu), V("hi"), Op.add)
-        ej = V("ej")
-        op("v", lambda: g.vector.tensor_copy(ej[0].indirect(posu[0]), T.pk[:]), [V("pk"), posu], [ej])
-        for b in range(4):
-            act(V("big", 4 * BCOL[t] + b, 4 * (BCOL[t] + E), 4), V("ps%d" % (4 + b), 0, E), Fn.Copy, scale=0.5)
         pb, s0, nl, cur = nw(), nw(), nw(), nw()
         lin(pb, pos, 1, A + HCOL[t])
         lin(s0, pos, -1e4, (B - 0.5) * 1e4)
+        ej = V("ej")
+        op("v", lambda: g.vector.tensor_copy(ej[0].indirect(posu[0]), T.pk[:]), [V("pk"), posu], [ej])
         if not last:
             act(V("go"), ind(V("tabi", 0, C), posu), Fn.Sign, bias=A - 0.5, scale=-1.0)
         if t == 0:
@@ -460,34 +449,63 @@ def rank_program(g, core, T, topo):
             lin(V("tab", 0, C, F), V("tabi", 0, E), 4, 4 * BCOL[t + 1])
             lin(V("tab", C, 3 * C, C), V("tabi", 0, 2), 0, 4 * BCOL[t + 1])
         if t == 1:
-            st["s1"], st["s2"] = nw(), nw()
-            lin(st["s1"], lev, -8, 4 * C)
-            lin(st["s2"], lev, 8, -4 * C)
+            s1, s2 = nw(), nw()
+            lin(s1, lev, -8, 4 * C)
+            lin(s2, lev, 8, -4 * C)
         if last:
             sel, lev3, lu3 = nw(), nw(), nw(NB, "wu")
             act(sel, s0, Fn.Sign)
             lin(lev3, lev, 2.0 / C, 1.25)
+        for b in range(4):
+            act(V("big", 4 * BCOL[t] + b, 4 * (BCOL[t] + E), 4), V("ps%d" % (4 + b), 0, E), Fn.Copy, scale=0.5)
+        tt(nl, pb, s0, Op.min)
+        if last:
+            tt(lev3, lev3, sel, Op.add)
         scan(V("ew"), V("maskd"), V("ej", 0, NJ), 0.0, Op.add, Op.min)
         nq = NJ // 4
         vi, lo_, hu, lou = nw(nq, "wi"), nw(nq, "wi"), nw(nq, "wu"), nw(nq, "wu")
-        ts(hu, V("ew", 3, NJ, 4), col(C1H), Op.add, 2.0 ** -13, Op.mult)
-        ts(vi, V("ew", 3, NJ, 4), col(C1), Op.add, col(C2 + t), Op.add)
-        tt(nl, pb, s0, Op.min)
-        ts(lo_, vi, 8191, Op.bitwise_and)
+        xo = nw(4 * NB, "wu")
+
+        def xlist(k):
+            ts(sub(xo, k * NB, (k + 1) * NB), cur, 4.0, Op.mult, float(k - 4 * XCOL), Op.add)
         tt(cur, nl, st["cur"], Op.max)
+        if last:
+            cp(lu3, lev3)
+        ts(vi, V("ew", 3, NJ, 4), col(C1), Op.add, col(C2 + t), Op.add)
+        ts(hu, V("ew", 3, NJ, 4), col(C1H), Op.add, 2.0 ** -13, Op.mult)
+        xlist(0)
+        ts(lo_, vi, 8191, Op.bitwise_and)
+        xlist(1)
+        xlist(2)
         cp(lou, lo_)
         for a, b in zip(ZCH, ZCH[1:]):
             act(V("own", 16 * a, 16 * b), ind(V(xsrc), sub(hu, a, b)), Fn.Copy, scale=0.5)
         for a, b in zip(ZCH, ZCH[1:]):
             tt(V("zt", 16 * a, 16 * b), ind(V("big", 4 * BCOL[t], 4 * HCOL[t]), sub(lou, a, b)), V("own", 16 * a, 16 * b), Op.add)
+            if b == 32 and not last:
+                scan(V("cg"), V("go"), V("ones"), 0.0, Op.add, Op.add)
+            if b == nq:
+                xlist(3)
+                if not last:
+                    st["sel"] = nw()
+                    ts(st["sel"], pos, float(B), Op.is_lt, float(C), Op.mult)
             if b == 32 or b == nq:
                 z0, q0, bank = (0, 0, 4) if b == 32 else (NJ - 128, 128, 0)
                 quant("qz", "sz", q0, 128, V("zt", 4 * z0, 4 * z0 + 512))
                 for k in range(4):
                     mm(bank + k, "qw", "sw", 128 * k, "qz", "sz", q0, 128)
-        xo = nw(4 * NB, "wu")
-        for k in range(4):
-            ts(sub(xo, k * NB, (k + 1) * NB), cur, 4.0, Op.mult, float(k - 4 * XCOL), Op.add)
+        if last:
+            act(V("olv"), ind(V("tabi", 0, 16), lu3), Fn.Copy, scale=0.5)
+            dma("s", T.ol[:], T.olv[0:128:16, :], [V("olv")], [])
+        off = nw((t + 1) * NB, "wu")
+        if t == 0:
+            cp(off, nl)
+        elif t == 1:
+            o1, o2, st["lev2"] = nw(), nw(2 * NB), nw()
+            tt(o1, nl, s1, Op.min)
+            tt(sub(o2, NB, 2 * NB), nl, s2, Op.min)
+            tt(st["lev2"], lev, st["sel"], Op.add)
+            tt(sub(o2, 0, NB), o1, st["nl0"], Op.max)
         for b in range(4):
             act(V("big", 4 * HCOL[t] + b, 4 * (HCOL[t] + 128), 4), V("ps%d" % (4 + b), 0, 128), Fn.Copy, scale=2.0 ** -6)
         for b in range(4):
@@ -496,10 +514,8 @@ def rank_program(g, core, T, topo):
                 ts(o, i, 2.0 ** -6, Op.mult)
             else:
                 act(o, i, Fn.Copy, scale=2.0 ** -6)
-        if not last:
-            scan(V("cg"), V("go"), V("ones"), 0.0, Op.add, Op.add)
-        else:
-            tt(lev3, lev3, sel, Op.add)
+        if t == 1:
+            cp(off, o2)
         win = V("big", 4 * XCOL, 4 * (HCOL[t] + NJ))
         pieces = FIN if last else [0, NB]
         for j, (a, b) in enumerate(zip(pieces, pieces[1:])):
@@ -510,21 +526,15 @@ def rank_program(g, core, T, topo):
                 else:
                     act(o, i, Fn.Copy, scale=2.0)
             if last:
-                if j == 0:
-                    cp(lu3, lev3)
                 a, b = 16 * a, 16 * b
                 quant("qx", "sx", a, b - a, V("xt", 4 * a, 4 * b))
                 mm(j, "qv", "sv", 0, "qx", "sx", a, b - a)
-                dma("s", T.oc[:, 4 * a:4 * b], T.qx[:, a:b].bitcast(dt.uint8), [V("qx", a, b)], [])
+                dma("sa"[j], T.oc[:, 4 * a:4 * b], T.qx[:, a:b].bitcast(dt.uint8), [V("qx", a, b)], [])
         xsrc = "xt"
-        st.update(nl=nl, cur=cur, pos=pos)
-        if t > 0:
-            st["lev"] = lev
+        st["cur"] = cur
 
-    act(V("olv"), ind(V("tabi", 0, 16), lu3), Fn.Copy, scale=0.5)
-    dma("a", T.ol[:], T.olv[0:128:16, :], [V("olv")], [])
     for k in range(4):
-        dma("a", T.osc[4 * k:4 * k + 4, :], T.sx[32 * k:32 * k + 4, :], [V("sx")], [])
+        dma("ag"[k % 2], T.osc[4 * k:4 * k + 4, :], T.sx[32 * k:32 * k + 4, :], [V("sx")], [])
     for j, (a, b) in enumerate(zip(FIN, FIN[1:])):
         a, b = 16 * a, 16 * b
         cp(V("yb", a, b), V("ps%d" % j, 0, b - a))

@@ -1,25 +1,33 @@
-import numpy as np
-from concourse.mybir import dt, AluOpType as Op, ActivationFunctionType as Fn, AxisListType
+from concourse.mybir import dt, AluOpType as Op, ActivationFunctionType as Fn
 
 C, A, B, E, F, R = 352, 160, 64, 32, 11, 3
 NJ = A + B
 STEP = [1, 3, 2]
 NB = C // 16
-BCOL = [68, 36, 4]
+UP = C - (A - E)
+BCOL = [0, 68, 36]
 XCOL = 100
 HCOL = [452, 676, 900]
 ENDC = 1124
 LAND = [64, 32, 0]
+KEY = 16384
 TILES = [(352, [21, 20, 19, "band"]), (288, [18, 17, 16, 15]), (224, [14, 13, 12, 11]),
          (160, [10, 9, 8, 7]), (128, [6, 5, 4, 3]), (128, [2, 1])]
-ONACT = [21, 20]
-ONVEC = TILES[-1][1]
+ONACT = [21, 20, 19, 18, 17, 16]
+ONVEC = list(range(9, 16))
+RS = 128
 HEAD = C - 128
 ZCH = [0, 8, 20, 32, 46, 56]
-FIN = [0, 14, 22]
-NGW = 134
+Z0 = [(0, 16, "v"), (16, 32, "a"), (32, 44, "v"), (44, 56, "a")]
+ZMM = [(0, 128, "aava"), (128, NJ, "vvav")]
+MID = [(0, NB)]
+FIN = [(0, 14), (14, NB)]
+XWHO, YWHO = "vvaa", "vv"
+FAROFF, HOLD = 2.0 ** 96, 2.0 ** 24
+CYC, PECYC, VFIX, AFIX, WAKE, DMA, FAR, TURNS = 0.83e-3, 0.63e-3, 0.03, 0.09, 0.15, 1.5, 1.5, 8
 
 BF, F32, I32, U16, Q4, U8 = "bfloat16", "float32", "int32", "uint16", "float8_e4m3fn_x4", "uint8"
+NGW = 134
 
 
 def _sb(n, d):
@@ -27,15 +35,14 @@ def _sb(n, d):
 
 
 SCRATCH = {
-    "xin": _sb(4 * C, BF), "uin": _sb(512, BF), "vin": _sb(512, BF), "xt": _sb(4 * C, BF),
+    "xin": _sb(4 * C, BF), "uin": _sb(512, BF), "vin": _sb(512, BF), "xt": _sb(4 * C, BF), "zall": _sb(4 * C, BF),
     "big": _sb(4 * ENDC, BF), "own": _sb(4 * NJ, BF), "zt": _sb(4 * NJ, BF), "tt": _sb(512, BF), "ng": _sb(4 * NGW, BF),
-    "sm": _sb(C, F32), "hold": _sb(C, F32), "seg": _sb(C, BF), "junk": _sb(16 * 231, BF), "junk2": _sb(2 * C, BF),
-    "cw": _sb(C, F32), "ej": _sb(C, F32), "ew": _sb(NJ, F32), "pk": _sb(C, F32), "tab": _sb(3 * C, F32),
-    "cp": _sb(2 * C, F32), "np_": _sb(2 * C, F32), "go": _sb(C, BF), "cg": _sb(C, BF), "olv": _sb(C, F32), "yb": _sb(C, F32),
-    "rows": _sb(24, F32), "w": _sb(2048, F32), "wi": _sb(512, I32), "wu": _sb(1024, U16),
-    "tabi": _sb(ENDC, F32), "im16": _sb(C, BF), "im4": _sb(NJ, BF), "g128": _sb(128, BF), "d128": _sb(128, BF),
-    "eq16": _sb(C, BF), "eq4": _sb(NJ, F32),
-    "maska": _sb(C, BF), "maskc": _sb(C, BF), "maskd": _sb(NJ, F32), "reset": _sb(C, BF), "segr": _sb(C, BF), "ones": _sb(C, BF),
+    "sm": _sb(C, F32), "hold": _sb(C, F32), "seg": _sb(C, BF), "junk": _sb(16 * 231, BF), "junk2": _sb(2 * UP, BF),
+    "cw": _sb(C, F32), "ej": _sb(C, F32), "ew": _sb(NJ, F32), "pk0": _sb(C, F32), "pk": _sb(C, F32), "tab": _sb(3 * C, F32),
+    "cp": _sb(2 * C, F32), "go": _sb(UP, BF), "cg": _sb(UP, BF), "olv": _sb(C, F32), "yb": _sb(C, F32),
+    "rows": _sb(24, F32), "rv": _sb(RS * 17, BF), "w": _sb(2560, F32), "wi": _sb(512, I32), "wu": _sb(1024, U16),
+    "tabi": _sb(C, F32), "tabl": _sb(2 * NJ + 1, F32), "im16": _sb(C, BF), "im4": _sb(NJ, BF), "g128": _sb(128, BF), "d128": _sb(128, BF),
+    "maska": _sb(C, BF), "maskc": _sb(C, BF), "maskd": _sb(NJ, BF), "reset": _sb(C, BF), "segr": _sb(C, BF), "ones": _sb(UP, BF),
     "hi": _sb(C, F32), "bd": _sb(512, BF), "tri": _sb(512, BF), "tru": _sb(512, BF), "ff": _sb(516, BF),
     "ci": _sb(64, I32), "cf": _sb(512, F32), "cu": _sb(8, U16),
     "qu": _sb(128, Q4), "su": _sb(128, U8), "qu2": _sb(128, Q4), "su2": _sb(128, U8), "qv": _sb(128, Q4), "sv": _sb(128, U8),
@@ -46,14 +53,14 @@ SCRATCH = {
     "qtri": _sb(128, Q4), "stri": _sb(128, U8), "qtru": _sb(128, Q4), "stru": _sb(128, U8),
     "qe": _sb(512, Q4), "se": _sb(512, U8),
 }
-for _k, (_w, _s) in enumerate(TILES):
-    SCRATCH["m%d" % _k] = _sb(4 * _w, BF)
-    SCRATCH["qm%d" % _k] = _sb(_w, Q4)
-    SCRATCH["sm%d" % _k] = _sb(_w, U8)
+for _k in range(len(TILES)):
+    SCRATCH["m%d" % _k] = _sb(4 * C, BF)
+    SCRATCH["qm%d" % _k] = _sb(C, Q4)
+    SCRATCH["sm%d" % _k] = _sb(C, U8)
 for _k in range(8):
     SCRATCH["ps%d" % _k] = ("psum", [128, 512], F32)
 
-NDMA = 20
+NDMA = 24
 SEMAPHORES = ["g", "v", "a", "t"] + ["d%d" % k for k in range(NDMA)] + ["arr0", "arr1", "arr2", "out0", "out1", "out2"]
 
 
@@ -63,67 +70,110 @@ def rank_program(g, core, T, topo):
         return
     n_ranks = len(T.cores)
     queue = {"g": g, "v": g.vector, "a": g.scalar, "t": g.tensor, "s": g.sync}
-    count = {"g": 0, "v": 0, "a": 0, "t": 0}
-    known = {k: {} for k in queue}
-    seen = {}
+    calls = []
     uses = {}
-    final = {}
-    ndma = [0]
 
     def V(name, a=0, b=None, s=1):
         width = SCRATCH[name][1][1]
         b = width if b is None else b
-        cols = np.zeros(width, bool)
-        cols[a:b:s] = True
         if name.startswith("ps"):
-            cols[:] = True
+            cols = 1
+        elif s == 1:
+            cols = ((1 << (b - a)) - 1) << a
+        else:
+            cols = sum(1 << c for c in range(a, b, s))
         ap = T[name][:, a:b] if s == 1 else T[name][:, a:b:s]
-        return (ap, [(name, cols)], name, a)
+        return (ap, [(name, cols)], name, a, len(range(a, b, s)), SCRATCH[name][2] in (BF, U16))
 
     def sub(v, a, b):
         return V(v[2], v[3] + a, v[3] + b)
 
     def ind(win, off):
-        return (win[0].indirect(off[0]), win[1] + off[1])
+        return (win[0].indirect(off[0]), win[1] + off[1], None, 0, 16 * off[4], None)
 
-    def wait(q, sem, n):
-        if known[q].get(sem, 0) >= n:
-            return
-        queue[q].wait_ge(T.sem[sem], n)
-        known[q][sem] = n
-        for k, m in seen.get((sem, n), {}).items():
-            if known[q].get(k, 0) < m:
-                known[q][k] = m
-
-    def order(q, sem, n, reads, writes, chain=False):
-        need = {}
+    def op(q, fn, reads, writes, busy, chain=False, sem=None, inc=1, late=0.0, after=()):
+        me = len(calls)
+        need = {k: True for k in after}
         regs = [(r, False) for x in reads for r in x[1]] + [(r, True) for x in writes for r in x[1]]
         for (name, cols), wr in regs:
             bank = name.startswith("ps")
-            for c2, s2, n2, w2 in uses.get(name, []):
-                if chain and s2 == sem and bank:
-                    continue
-                if (wr or w2 or (bank and s2 != sem)) and (cols & c2).any():
-                    need[s2] = max(need.get(s2, 0), n2)
-        for s2 in sorted(need, key=lambda k: k == q):
-            wait(q, s2, need[s2])
+            for c2, k, w2 in uses.get(name, []):
+                if (wr or w2 or (bank and calls[k]["q"] != q)) and cols & c2:
+                    need[k] = need.get(k, False) or not (chain and bank and calls[k]["q"] == q)
         for (name, cols), wr in regs:
-            uses.setdefault(name, []).append((cols, sem, n, wr))
-        seen[(sem, n)] = dict(known[q])
-        final[sem] = n
+            old = uses.get(name, [])
+            if wr and not chain:
+                old = [u for u in old if u[0] & ~cols or u[1] == me]
+            uses[name] = old + [(cols, me, wr)]
+        calls.append({"q": q, "fn": fn, "need": need, "sem": sem or q, "inc": inc, "busy": busy, "late": late})
+        return me
 
-    def op(q, fn, reads, writes, chain=False):
-        n = count[q] + 1
-        order(q, q, n, reads, writes, chain)
-        count[q] = n
-        fn().then_inc(T.sem[q], 1)
+    def issue():
+        n = len(calls)
+        busy = [c["busy"] for c in calls]
+        before, behind = [[] for c in calls], [[] for c in calls]
+        for i, c in enumerate(calls):
+            for k, w in c["need"].items():
+                gap = calls[k]["late"] + WAKE if w else 0.0
+                before[i].append((k, gap))
+                behind[k].append((i, gap))
 
-    def dma(q, out, in_, reads, writes):
-        sem = "d%d" % ndma[0]
+        def deal(order, links, tail):
+            end, slots = [0.0] * n, {q: [] for q in "gvatsx"}
+            for i in order:
+                at = max([end[k] + gap for k, gap in links[i]] + [tail * calls[i]["late"]])
+                row, j = slots[calls[i]["q"]], 0
+                while j < len(row) and row[j][0] < at + busy[i]:
+                    at = max(at, row[j][1])
+                    j += 1
+                row.insert(j, (at, at + busy[i]))
+                end[i] = at + busy[i]
+            return end
+
+        way = [0.0] * n
+        for i in range(n - 1, -1, -1):
+            way[i] = busy[i] + max([way[k] + gap for k, gap in behind[i]] + [calls[i]["late"]])
+        best = None
+        for turn in range(TURNS):
+            end = deal(sorted(range(n), key=lambda i: (-way[i], i)), before, 0)
+            span = max(end[i] + calls[i]["late"] for i in range(n))
+            if best is None or span < best[0]:
+                best = (span, end)
+            way = deal(sorted(range(n), key=lambda i: (-end[i], -i)), behind, 1)
+        count, known, seen, mark, final = {}, {q: {} for q in queue}, {}, {}, {}
+        for i in sorted(range(n), key=lambda i: (best[1][i] - busy[i], best[1][i], i)):
+            c = calls[i]
+            q = c["q"]
+            count[c["sem"]] = count.get(c["sem"], 0) + c["inc"]
+            mark[i] = (c["sem"], count[c["sem"]])
+            final[c["sem"]] = count[c["sem"]]
+            if q == "x":
+                continue
+            want = {}
+            for k, w in c["need"].items():
+                if w:
+                    want[mark[k][0]] = max(want.get(mark[k][0], 0), mark[k][1])
+            for sem in sorted(want, key=lambda k: k == q):
+                if known[q].get(sem, 0) < want[sem]:
+                    queue[q].wait_ge(T.sem[sem], want[sem])
+                    known[q][sem] = want[sem]
+                    for k, m in seen.get((sem, want[sem]), {}).items():
+                        known[q][k] = max(known[q].get(k, 0), m)
+            seen[mark[i]] = dict(known[q])
+            c["fn"](T.sem[c["sem"]])
+        for sem, m in final.items():
+            if known["g"].get(sem, 0) < m:
+                g.wait_ge(T.sem[sem], m)
+
+    def run(q, fn, reads, writes, busy, chain=False):
+        return op(q, lambda s: fn().then_inc(s, 1), reads, writes, busy, chain, late=0.06 if q == "t" else 0.0)
+
+    ndma = [0]
+
+    def dma(q, out, in_, reads, writes, after=(), **kw):
         ndma[0] += 1
-        order(q, sem, 16, reads, writes)
-        queue[q].dma_start(out, in_).then_inc(T.sem[sem], 16)
-        return sem
+        return op(q, lambda s: queue[q].dma_start(out, in_, **kw).then_inc(s, 16), reads, writes, 0.6 if q == "g" else 0.05,
+                  sem="d%d" % (ndma[0] - 1), inc=16, late=DMA, after=after)
 
     def sc(x):
         return x[0] if isinstance(x, tuple) else x
@@ -131,70 +181,83 @@ def rank_program(g, core, T, topo):
     def cols_of(*xs):
         return [x for x in xs if isinstance(x, tuple)]
 
+    def vec(out, *ins, k=1.0):
+        if ins and ins[0][5] is None:
+            return 0.05 + 1.56 * CYC * out[4]
+        if k == 1.0 and all(x[5] for x in (out,) + ins):
+            k = 0.5
+        return VFIX + CYC * max(64, k * (ins[0][4] if ins else out[4]))
+
     def ts(out, in0, s1, op0, s2=None, op1=None):
         if op1 is None:
-            op("v", lambda: g.vector.tensor_scalar(out[0], in0[0], sc(s1), None, op0), [in0] + cols_of(s1), [out])
+            run("v", lambda: g.vector.tensor_scalar(out[0], in0[0], sc(s1), None, op0), [in0] + cols_of(s1), [out], vec(out, in0))
         else:
-            op("v", lambda: g.vector.tensor_scalar(out[0], in0[0], sc(s1), sc(s2), op0, op1), [in0] + cols_of(s1, s2), [out])
+            run("v", lambda: g.vector.tensor_scalar(out[0], in0[0], sc(s1), sc(s2), op0, op1), [in0] + cols_of(s1, s2), [out], vec(out, in0))
 
     def tt(out, in0, in1, o):
-        op("v", lambda: g.vector.tensor_tensor(out[0], in0[0], in1[0], o), [in0, in1], [out])
+        k = 1.001 if (in0[2] or "").startswith("ps") else 2.0
+        run("v", lambda: g.vector.tensor_tensor(out[0], in0[0], in1[0], o), [in0, in1], [out], vec(out, in0, in1, k=k))
 
     def cp(out, in_):
-        op("v", lambda: g.vector.tensor_copy(out[0], in_[0]), [in_], [out])
+        run("v", lambda: g.vector.tensor_copy(out[0], in_[0]), [in_], [out], vec(out, in_))
 
     def ms(out, c):
-        op("v", lambda: g.vector.memset(out[0], c), [], [out])
+        run("v", lambda: g.vector.memset(out[0], c), [], [out], vec(out))
 
     def scan(out, d0, d1, init, o0, o1):
-        op("v", lambda: g.vector.tensor_tensor_scan(out[0], d0[0], d1[0], init, o0, o1), [d0, d1], [out])
+        run("v", lambda: g.vector.tensor_tensor_scan(out[0], d0[0], d1[0], init, o0, o1), [d0, d1], [out], vec(out, d0, d1))
 
     def act(out, in_, fn, bias=None, scale=None, acc=None):
         kw = {}
         if bias is not None:
             kw["bias"] = sc(bias)
         if scale is not None:
-            kw["scale"] = scale
+            kw["scale"] = sc(scale)
         if acc is not None:
             kw["accum_out"] = acc[0]
-        op("a", lambda: g.scalar.activation(out[0], in_[0], fn, **kw), [in_] + cols_of(bias), [out] + cols_of(acc))
+        busy = 0.065 + 1.56 * CYC * out[4] if in_[5] is None else AFIX + CYC * out[4]
+        run("a", lambda: g.scalar.activation(out[0], in_[0], fn, **kw), [in_] + cols_of(bias, scale), [out] + cols_of(acc), busy)
 
     def lin(out, in_, scale, bias):
         act(out, in_, Fn.Identity, bias=float(bias), scale=float(scale))
 
+    def scaled(q, out, in_, c):
+        if q == "v":
+            ts(out, in_, c, Op.mult)
+        else:
+            act(out, in_, Fn.Copy, scale=c)
+
     def quant(qn, sn, a, n, in_):
         q, s = V(qn, a, a + n), V(sn, a, a + n)
-        op("v", lambda: g.vector.quantize_mx(q[0], s[0], in_[0]), [in_], [q, s])
+        run("v", lambda: g.vector.quantize_mx(q[0], s[0], in_[0]), [in_], [q, s], 0.012 + 0.88e-3 * n)
 
     def mm(bank, wq, ws, wa, xq, xs, xa, n, start=True, stop=True):
         o = V("ps%d" % bank, 0, n)
         a, b, c, d = V(wq, wa, wa + 128), V(ws, wa, wa + 128), V(xq, xa, xa + n), V(xs, xa, xa + n)
-        op("t", lambda: g.tensor.matmul_mx(o[0], a[0], b[0], c[0], d[0], start, stop), [a, b, c, d], [o], chain=not start)
+        run("t", lambda: g.tensor.matmul_mx(o[0], a[0], b[0], c[0], d[0], start, stop), [a, b, c, d], [o], PECYC * (n + 16), chain=not start)
 
     def iota(out, pattern, base, cm, small=True):
+        busy = 0.13 + 2 * CYC * out[4]
         if small:
-            op("g", lambda: g.iota(out[0], pattern, base, cm, allow_small_or_imprecise_dtypes=True), [], [out])
+            run("g", lambda: g.iota(out[0], pattern, base, cm, allow_small_or_imprecise_dtypes=True), [], [out], busy)
         else:
-            op("g", lambda: g.iota(out[0], pattern, base, cm), [], [out])
+            run("g", lambda: g.iota(out[0], pattern, base, cm), [], [out], busy)
 
     def send(t, qn, sn, a):
         dst = T.cores[(rank + STEP[t]) % n_ranks]
+        src = T.cores[(rank - STEP[t]) % n_ranks]
         rid, pid = topo.addr(dst, core)
         eng = topo.engines(core, dst)
         half = len(eng) // 2
         masks = [sum(1 << e for e in eng[:half]), sum(1 << e for e in eng[half:2 * half])]
         q, s = V(qn, a, a + E), V(sn, a, a + E)
-        sem = "out%d" % t
-        order("g", sem, 2 * half, [q, s], [])
-        g.remote_dma(T.ql[:, LAND[t]:LAND[t] + E].bitcast(dt.uint8), q[0].bitcast(dt.uint8), T.sem["arr%d" % t], T.sem[sem], pid, rid, masks[0])
-        g.remote_dma(T.sl[:, LAND[t]:LAND[t] + E], s[0], T.sem["arr%d" % t], T.sem[sem], pid, rid, masks[1])
+        lq, ls, arr = V("ql", LAND[t], LAND[t] + E), V("sl", LAND[t], LAND[t] + E), T.sem["arr%d" % t]
 
-    for t in range(R):
-        src = T.cores[(rank - STEP[t]) % n_ranks]
-        n = 2 * (len(topo.engines(src, core)) // 2)
-        for name in ("ql", "sl"):
-            uses.setdefault(name, []).append((V(name, LAND[t], LAND[t] + E)[1][0][1], "arr%d" % t, n, True))
-        final["arr%d" % t] = n
+        def both(sem):
+            g.remote_dma(lq[0].bitcast(dt.uint8), q[0].bitcast(dt.uint8), arr, sem, pid, rid, masks[0])
+            g.remote_dma(ls[0], s[0], arr, sem, pid, rid, masks[1])
+        k = op("g", both, [q, s], [], 0.6, sem="out%d" % t, inc=2 * half, late=DMA)
+        op("x", None, [], [lq, ls], 0.0, sem="arr%d" % t, inc=2 * (len(topo.engines(src, core)) // 2), late=FAR, after=[k])
 
     top = {"w": 0, "wi": 0, "wu": 0, "cf": 16, "ci": 8}
 
@@ -206,85 +269,97 @@ def rank_program(g, core, T, topo):
     def col(k):
         return V("cf", k, k + 1)
 
-    def zero_a(name, a, b):
-        while a < b:
-            n = min(C, b - a)
-            act(V(name, a, a + n), V("im16", 0, n), Fn.Copy, scale=0.0)
-            a += n
-
     cut = 4 * HEAD
     dma("s", T.uin[:], T.u[:], [], [V("uin")])
     d1 = dma("a", T.xin[:, cut:], T.x[:, cut:], [], [V("xin", cut)])
     d2 = dma("s", T.xin[:, :cut], T.x[:, :cut], [], [V("xin", 0, cut)])
-    wait("s", d1, 16)
-    wait("s", d2, 16)
-    dma("s", T.qw[:].bitcast(dt.uint8), T.wc[:], [], [V("qw")])
-    dma("s", T.sw[:], T.ws[:], [], [V("sw")])
+    dma("s", T.zall[:, 4:], T.x[:, :4 * C - 4], [], [V("zall")], after=[d1, d2])
+    dma("g", T.zall[:, 4:], T.xin[:, 4:], [V("xin")], [V("zall")], accum_op=Op.add)
+    dma("s", T.qw[:].bitcast(dt.uint8), T.wc[:], [], [V("qw")], after=[d1, d2])
+    dma("s", T.sw[:], T.ws[:], [], [V("sw")], after=[d1, d2])
+    dma("s", T.vin[:], T.v[:], [], [V("vin")], after=[d1, d2])
 
-    RC, GC, AC, TC, C1, C1H, BC0, K0, K1, C2 = range(10)
+    RC, GC, AC, TC, DH, BC0, TH, C2, K0 = 0, 1, 2, 3, 5, 6, 4, 7, 10
     iota(V("im16"), [[0, NB], [1, 16]], 0, 0)
     iota(V("ci", 0, 1), [[0, 1]], 0, 1, False)
-    iota(V("g128"), [[1, 8], [0, 16]], 0, 0)
     uo = nw(8, "ci")
     iota(uo, [[16, 8]], 0, 0, False)
+    iota(V("g128"), [[1, 8], [0, 16]], 0, 0)
     iota(V("d128"), [[1, 128]], 0, -1)
     m16 = nw(NB, "cf")
     iota(m16, [[16, NB]], 0, 0)
     iota(V("im4"), [[0, NJ // 4], [1, 4]], 0, 0)
+    iota(V("pk0"), [[-4, C]], -4, 0)
+    iota(V("tabi"), [[1, C]], 0, 0)
+    iota(V("tabl"), [[-4, 2 * NJ + 1]], -4 * (HCOL[0] - 1), 0)
+    iota(V("tabl", 0, 1), [[0, 1]], 1, 0)
+    iota(V("hi"), [[KEY, C]], 0, 0)
+    iota(V("tab", 0, C), [[-4, C]], -4 * (XCOL - 1), 0)
+    iota(V("ones"), [[0, UP]], 1, 0)
 
     low = [min(16 * m for m in slots if m != "band") for wd, slots in TILES]
     zero = nw(3 * NB, "cf")
     ms(V("ff"), 0.0)
-    ms(V("m5"), 0.0)
     ms(V("ng"), 0.0)
     ms(V("rows"), 0.0)
+    ms(V("rv", RS - 1, RS), 0.0)
     ms(zero, 0.0)
-    runs = [nw((k + 2) * NB, "cf") for k in range(R)]
-    ms(V("cf", runs[0][3], runs[2][3] + 4 * NB), 1.0)
+    runs = [None] + [nw((k + 2) * NB, "cf") for k in range(1, R)]
+    for k in range(1, R):
+        iota(runs[k], [[0, (k + 2) * NB]], 1, 0)
+        iota(V("cf", runs[k][3], runs[k][3] + (k + 2) * NB, k + 2), [[0, NB]], 0, 0)
+    for k, (wd, slots) in enumerate(TILES):
+        a = 4 * low[k] if len(slots) == 4 else 0
+        while a < 4 * wd:
+            n = min(512, 4 * wd - a)
+            act(V("m%d" % k, a, a + n), V("ng", 0, n), Fn.Copy)
+            a += n
+    act(V("tt"), V("ng", 0, 512), Fn.Copy)
     p = V("ci", 0, 1)
     ts(V("ci", 2, 3), p, 15, Op.bitwise_and)
     ts(V("ci", 3, 4), p, 4, Op.arith_shift_right)
     ts(V("ci", 4, 5), p, 2, Op.arith_shift_right, 3, Op.bitwise_and)
     ts(V("ci", 5, 6), p, 3, Op.bitwise_and)
-    ts(V("reset"), V("im16"), 0.0, Op.is_equal, -2e29, Op.mult)
     cp(V("cf", 0, 4), V("ci", 2, 6))
-    for k in range(R):
-        ms(V("cf", runs[k][3], runs[k][3] + (k + 2) * NB, k + 2), 0.0)
+    ts(V("reset"), V("im16"), 0.0, Op.is_equal, -2 * FAROFF, Op.mult)
     ts(V("segr"), V("im16"), 0.0, Op.not_equal)
-    for k in range(5):
-        zero_a("m%d" % k, 4 * low[k], 4 * TILES[k][0])
+    ts(V("maska"), V("im16"), col(RC), Op.not_equal, -FAROFF, Op.mult)
+    lin(V("maskc"), V("maska"), 66560.0 / FAROFF, 65536.0)
     for t in range(4):
         ts(V("bd", t, 512, 4), V("g128"), col(GC), Op.is_equal)
-    ts(V("eq16"), V("im16"), col(RC), Op.is_equal)
-    lin(V("maska"), V("eq16"), 2e29, -1e29)
-    zero_a("tt", 0, 512)
-    lin(V("maskc"), V("eq16"), 66560.0, -1024.0)
     tri, tru, bd = V("tri"), V("tru"), V("bd")
-    op("g", lambda: g.affine_select(tri[0], bd[0], [[1, 128], [0, 4]], Op.is_gt, 0.0, 0, -1), [bd], [tri])
-    op("g", lambda: g.affine_select(tru[0], bd[0], [[-1, 128], [0, 4]], Op.is_ge, 0.0, 0, 1), [bd], [tru])
+    run("g", lambda: g.affine_select(tri[0], bd[0], [[1, 128], [0, 4]], Op.is_gt, 0.0, 0, -1), [bd], [tri], 1.02)
+    run("g", lambda: g.affine_select(tru[0], bd[0], [[-1, 128], [0, 4]], Op.is_ge, 0.0, 0, 1), [bd], [tru], 1.02)
     cp(V("cu"), uo)
-    quant("qbd", "sbd", 0, 128, V("bd"))
+    quant("qbd", "sbd", 0, 128, bd)
+    quant("qtri", "stri", 0, 128, tri)
+    quant("qtru", "stru", 0, 128, tru)
     ts(V("ff", 3, 515, 4), V("d128"), 0.0, Op.is_equal)
-    bcw, iw, cur0 = nw(NB, "cf"), nw(NB, "cf"), nw(NB, "cf")
-    iota(V("tabi", 0, C), [[1, C]], 0, 0)
-    ts(V("eq4"), V("im4"), col(AC), Op.is_equal, 2.0 ** 28 + 2.0 ** 24, Op.mult)
+    for b in range(4):
+        quant("qe", "se", 128 * b, 128, V("ff", 3 - b, 515 - b))
+    quant("ql", "sl", 96, 128, V("tt"))
+    bcw, iw, cur0, e4, m4, d4 = nw(NB, "cf"), nw(NB, "cf"), nw(NB, "cf"), nw(4, "cf"), nw(4, "cf"), nw(4, "cf")
+    ts(V("maskd"), V("im4"), col(AC), Op.not_equal, HOLD, Op.mult)
+    ts(e4, V("im4", 0, 4), col(AC), Op.is_equal, -1.0, Op.mult)
+    ts(m4, V("im4", 0, 4), col(AC), Op.not_equal, 1.0 / HOLD, Op.mult)
+    scan(d4, m4, e4, 0.0, Op.mult, Op.add)
+    dlo = sub(d4, 3, 4)
+    lin(col(DH), dlo, 4.0 / KEY, 0)
+    lin(col(TH), col(TC), 1, -0.4)
     lin(col(BC0), col(RC), -1025, 15 * 1025 - A)
-    lin(col(C1), col(AC), -2.0 ** 24, 3 * 2.0 ** 24)
     act(iw, m16, Fn.Identity, bias=col(RC))
-    for k in range(R):
-        lin(col(C2 + k), col(TC), 1, -4 * BCOL[k])
-    lin(col(K0), col(RC), 2, 2 * (A - E) + 1)
-    lin(col(K1), col(RC), 2, 2 * (A - E + 16) + 1)
     act(bcw, m16, Fn.Identity, bias=col(BC0))
-    act(col(C1H), col(TC), Fn.Identity, bias=col(C1), scale=8192.0)
-    lin(cur0, iw, 1, XCOL)
-    lin(V("maskd"), V("eq4"), 1, -2.0 ** 24)
+    lin(cur0, iw, 4, 0)
+    for k in range(R):
+        lin(col(C2 + k), col(TC), 1, -4 * BCOL[k] if k else -4)
+    for k in range(2):
+        lin(col(K0 + k), col(RC), 2, 32 * k + 1 - 2 * E)
     quant("qu", "su", 0, 128, V("uin"))
     q2, q1, cu = V("qu2"), V("qu"), V("cu")
-    op("v", lambda: g.vector.tensor_copy(q2[0].bitcast(dt.uint32), q1[0].bitcast(dt.uint32).indirect(cu[0])), [q1, cu], [q2])
-    cp(V("su2"), ind(V("su"), cu))
-    for b in range(2):
-        quant("qe", "se", 128 * b, 128, V("ff", 3 - b, 515 - b))
+    run("v", lambda: g.vector.tensor_copy(q2[0].bitcast(dt.uint32), q1[0].bitcast(dt.uint32).indirect(cu[0])), [q1, cu], [q2], 0.22)
+    act(V("su2"), ind(V("su"), cu), Fn.Copy)
+    quant("qv", "sv", 0, 128, V("vin"))
+    act(V("big", 4 * XCOL, 4 * (XCOL + C)), V("xin"), Fn.Copy, scale=0.5)
 
     st = {"cur": cur0}
     xsrc = "xin"
@@ -292,252 +367,185 @@ def rank_program(g, core, T, topo):
     for t in range(R):
         last = t == R - 1
         qn, sn = ("qx0", "sx0") if t == 0 else ("qx", "sx")
-        if t > 0:
-            lev, lf, lu = st["sel"] if t == 1 else st["lev2"], nw(), nw(NB, "wu")
-            acc, tf, toff = nw(2), nw(8), nw(8, "wu")
-            for k in range(2):
-                act(V("junk2", k * C, (k + 1) * C), V("cg"), Fn.Sign, bias=col(K0 + k), scale=-1.0, acc=sub(acc, k, k + 1))
-            thr = [nw() for k in range(t + 1)]
-            for k in range(t + 1):
-                act(thr[k], lev, Fn.Abs, bias=-float(C * k))
-            for k in range(4):
-                lin(sub(tf, 2 * k, 2 * k + 2), acc, 2, 2 * C + k)
         quant(qn, sn, HEAD, 128, V(xsrc, 4 * HEAD))
         mm(1, "qu2", "su2", 0, qn, sn, HEAD, 128)
         quant(qn, sn, 0, HEAD, V(xsrc, 0, 4 * HEAD))
         mm(0, "qu2", "su2", 0, qn, sn, 0, C)
         mm(2, "qu2", "su2", 0, qn, sn, 0, C)
+        tt(V("sm", HEAD), V("ps1", 0, 128), V("maska", HEAD), Op.add)
+        scan(V("hold", HEAD), V("reset", HEAD), V("sm", HEAD), -FAROFF, Op.add, Op.max)
+        tt(V("sm", 0, HEAD), V("ps0", 0, HEAD), V("maska", 0, HEAD), Op.add)
+        scan(V("hold", 0, HEAD), V("reset", 0, HEAD), V("sm", 0, HEAD), -FAROFF, Op.add, Op.max)
         if t == 0:
             send(0, qn, sn, C - E)
-            dma("g", T.vin[:], T.v[:], [], [V("vin")])
-            iota(V("ones"), [[0, C]], 1, 0)
-            iota(V("tabi", C), [[1, ENDC - C]], C, 0)
-            quant("qe", "se", 256, 128, V("ff", 1, 513))
-        tt(V("sm", HEAD), V("ps1", 0, 128), V("maska", HEAD), Op.min)
-        if t > 0:
-            tt(lf, lev, iw, Op.add)
         else:
-            quant("qe", "se", 384, 128, V("ff", 0, 512))
-        scan(V("hold", HEAD), V("reset", HEAD), V("sm", HEAD), -1e29, Op.add, Op.max)
-        tt(V("sm", 0, HEAD), V("ps0", 0, HEAD), V("maska", 0, HEAD), Op.min)
-        jk, signs = [0], []
-
-        def slot(k, e, m):
-            o, s = V("m%d" % k, e, 64 * m, 4), V("hold", 16 * m + 15, 16 * m + 16)
-            j = V("junk", jk[0], jk[0] + 16 * m)
-            jk[0] += 16 * m
-            if m in ONACT:
-                act(j, V("ps2", 0, 16 * m), Fn.Sign, bias=s, scale=-1.0)
-                signs.append((o, j, m))
-                if m == ONACT[-1]:
-                    for o, j, m in signs:
-                        act(o, j, Fn.Relu, acc=V("rows", m, m + 1))
-            else:
-                ts(o, V("ps0", 0, 16 * m), s, Op.is_lt)
-                if m not in ONVEC:
-                    act(j, o, Fn.Copy, acc=V("rows", m, m + 1))
-
-        def count_tile(k):
-            wd = TILES[k][0]
-            quant("qm%d" % k, "sm%d" % k, 0, wd, V("m%d" % k))
-            if wd > 128:
-                mm(1, "qbd", "sbd", 0, "qm%d" % k, "sm%d" % k, 0, wd, start=k == 0, stop=TILES[k + 1][0] == 128)
-            mm(3, "qbd", "sbd", 0, "qm%d" % k, "sm%d" % k, 0, 128, start=k == 0, stop=k == len(TILES) - 1)
-
+            acc, bias, tf, toff = nw(2), nw(2), nw(8), nw(8, "wu")
+            act(bias, V("cf", K0, K0 + 2), Fn.Identity, bias=V("cg", UP - 1, UP))
+            for k in range(2):
+                act(V("junk2", k * UP, (k + 1) * UP), V("cg"), Fn.Sign, bias=sub(bias, k, k + 1), scale=-1.0, acc=sub(acc, k, k + 1))
+            for k in range(4):
+                lin(sub(tf, 2 * k, 2 * k + 2), acc, 2, 4 * (C - UP) + 2 * UP + k)
+            cp(toff, tf)
+            for j in range(4):
+                act(V("tt", j, 4 * E, 4), ind(V("xt"), sub(toff, 2 * j, 2 * j + 2)), Fn.Copy)
+            quant("qt%d" % (t - 1), "st%d" % (t - 1), 0, 128, V("tt"))
+            send(t, "qt%d" % (t - 1), "st%d" % (t - 1), 0)
+            lev, lf, lu = st["lev"], nw(), nw(NB, "wu")
+            tt(lf, lev, iw, Op.add)
+            cp(lu, lf)
+            thr = [lev] + [nw() for k in range(t)]
+            for k in range(1, t + 1):
+                act(thr[k], lev, Fn.Abs, bias=-float(C * k))
+            lin(V("tab", 0, C, F), V("tabi", 0, E), -4, -4 * BCOL[t])
+            lin(V("tab", C, 3 * C, C), V("tabi", 0, 2), 0, -4 * BCOL[t])
+            for k in range(t):
+                c = V("cp", k * C, (k + 1) * C - 1)
+                act(V("cp", k * C, (k + 1) * C), ind(V("tabl"), sub(off, k * NB, (k + 1) * NB)), Fn.Copy)
+                lin(V("cp", k * C + F - 1, (k + 1) * C, F), V("tabi", 0, E), -4, -4 * (BCOL[t] + 1))
+                scan(V("tab", (k + 1) * C + 1, (k + 2) * C), c, c, -4.0 * BCOL[t], Op.mult, Op.min)
+            tt(V("pk"), ind(V("tab", 0, (t + 1) * C), lu), V("hi"), Op.subtract)
         b1, b2, rk = nw(), nw(), nw()
+        jk = 0
+        wide = max(k for k, (wd, slots) in enumerate(TILES) if wd > 128)
         for k, (wd, slots) in enumerate(TILES):
             for e, m in enumerate(slots):
                 if m == "band":
-                    scan(V("hold", 0, HEAD), V("reset", 0, HEAD), V("sm", 0, HEAD), -1e29, Op.add, Op.max)
-                    continue
-                if k == 1 and e == 1:
-                    tt(V("m0", 3, 4 * C, 4), V("ps0", 0, C), V("hold"), Op.is_le)
-                slot(k, e, m)
-                if k == 0 and e == 2 and t > 0:
-                    cp(toff, tf)
-                    for j in range(4):
-                        act(V("tt", j, 4 * E, 4), ind(V("xt"), sub(toff, 2 * j, 2 * j + 2)), Fn.Copy)
-                if k > 1 and e == 0:
-                    count_tile(k - 1)
-                if k == 1 and e == 1:
-                    scan(V("seg"), V("segr"), V("m0", 3, 4 * C, 4), 0.0, Op.mult, Op.add)
-                if k == 1 and e == 3:
-                    count_tile(0)
+                    tt(V("m%d" % k, e, 4 * C, 4), V("ps0", 0, C), V("hold"), Op.is_le)
+                    scan(V("seg"), V("segr"), V("m%d" % k, e, 4 * C, 4), 0.0, Op.mult, Op.add)
                     tt(b1, bcw, V("seg", 15, C, 16), Op.subtract)
-                if k == 2 and e == 1 and t > 0:
-                    quant("qt%d" % (t - 1), "st%d" % (t - 1), 0, 128, V("tt"))
-                    send(t, "qt%d" % (t - 1), "st%d" % (t - 1), 0)
-        if t > 0:
-            cp(lu, lf)
-        else:
-            quant("qtri", "stri", 0, 128, tri)
-        count_tile(len(TILES) - 1)
-        if t == 0:
-            quant("qtru", "stru", 0, 128, tru)
-            lin(V("pk"), V("tabi", 0, C), 32772, 4 * (XCOL - 1))
-            lin(V("pk", 0, C, F), V("tabi", 0, E), 4 + 32768 * F, 4 * BCOL[0])
-        else:
-            def spread(k):
-                act(V("cp", k * C, (k + 1) * C), ind(V("tabi"), sub(off, k * NB, (k + 1) * NB)), Fn.Copy, scale=4.0)
-                lin(V("cp", k * C + F - 1, (k + 1) * C, F), V("tabi", 0, E), 4, 4 * (BCOL[t] + 1))
-                act(V("np_", k * C, (k + 1) * C), V("cp", k * C, (k + 1) * C), Fn.Relu, bias=1.0, scale=-1.0)
-
-            def nearest(k):
-                scan(V("tab", (k + 1) * C + 1, (k + 2) * C), V("np_", k * C, (k + 1) * C - 1), V("cp", k * C, (k + 1) * C - 1),
-                     4.0 * BCOL[t], Op.mult, Op.add)
-            spread(0)
-        for e, m in enumerate(ONVEC):
-            o, i = V("rows", m, m + 1), V("m5", e, 64 * m, 4)
-            op("v", lambda: g.vector.tensor_reduce(o[0], i[0], AxisListType.X, Op.add), [i], [o])
+                    continue
+                o, s, j = V("m%d" % k, e, 64 * m, 4), V("hold", 16 * m + 15, 16 * m + 16), V("junk", jk, jk + 16 * m)
+                jk += 16 * m
+                if m in ONACT:
+                    act(j, V("ps2", 0, 16 * m), Fn.Sign, bias=s, scale=-1.0)
+                    act(o, j, Fn.Relu, acc=V("rows", m, m + 1))
+                    continue
+                ts(o, V("ps0", 0, 16 * m), s, Op.is_lt)
+                if m in ONVEC:
+                    scan(V("rv", RS * (m + 1) - 8 * m, RS * (m + 1)), V("m%d" % k, e, 32 * m, 4), V("m%d" % k, 32 * m + e, 64 * m, 4),
+                         0.0, Op.add, Op.add)
+                else:
+                    act(j, o, Fn.Copy, acc=V("rows", m, m + 1))
+            quant("qm%d" % k, "sm%d" % k, 0, wd, V("m%d" % k, 0, 4 * wd))
+            if wd > 128:
+                mm(1, "qbd", "sbd", 0, "qm%d" % k, "sm%d" % k, 0, wd, start=k == 0, stop=k == wide)
+            mm(3, "qbd", "sbd", 0, "qm%d" % k, "sm%d" % k, 0, 128, start=k == 0, stop=k == len(TILES) - 1)
         scan(V("cw", 128), V("maskc", 128), V("ps1", 128, C), 0.0, Op.add, Op.min)
-        tt(b2, V("rows", 0, NB), b1, Op.subtract)
         scan(V("cw", 0, 128), V("maskc", 0, 128), V("ps3", 0, 128), 0.0, Op.add, Op.min)
-        if t > 0:
-            tt(rk, V("cw", 15, C, 16), b2, Op.subtract)
-        else:
-            quant("ql", "sl", 96, 128, V("tt"))
+        a = 0
+        for m in range(1, NB + 1):
+            if m == NB or (m > 1 and (m in ONVEC) != (m - 1 in ONVEC)):
+                rows = V("rv", RS * (a + 1) - 1, RS * m, RS) if m - 1 in ONVEC else V("rows", a, m)
+                tt(sub(b2, a, m), rows, sub(b1, a, m), Op.subtract)
+                a = m
         n = (t + 1) * NB
-        for k in range(t + 1):
-            o = V("ng", 8 * (1 + k * NB), 8 * (1 + (k + 1) * NB), 8)
-            if t == 0:
-                tt(o, V("cw", 15, C, 16), b2, Op.is_ge)
-                tt(rk, V("cw", 15, C, 16), b2, Op.subtract)
-            else:
-                tt(o, rk, thr[k], Op.is_ge)
+        cw = V("cw", 15, C, 16)
+        if t == 0:
+            tt(V("ng", 8, 8 * (1 + NB), 8), cw, b2, Op.is_ge)
+        tt(rk, cw, b2, Op.subtract)
+        for k in range(t + 1 if t else 0):
+            tt(V("ng", 8 * (1 + k * NB), 8 * (1 + (k + 1) * NB), 8), rk, thr[k], Op.is_ge)
         nn = max(128, 2 * n)
         quant("qn", "sn", 0, nn + 2, V("ng", 0, 4 * (nn + 2)))
         mm(3, "qtri", "stri", 0, "qn", "sn", 2, nn, stop=False)
         mm(3, "qtru", "stru", 0, "qn", "sn", 0, nn, start=False)
-        pr = nw(4 * NB)
+        pr, od, posu, sums = nw(4 * NB), nw(n), nw(NB, "wu"), nw(4 * NB)
         w0 = pr[3]
-        ts(V("w", w0, w0 + (t + 2) * NB, t + 2), rk, 0.0, Op.min)
         if t == 0:
-            quant("qv", "sv", 0, 128, V("vin"))
-            act(V("big", 4 * XCOL, 4 * (XCOL + C)), V("xin"), Fn.Copy, scale=0.5)
+            ts(V("w", w0 + 1, w0 + 2 * NB, 2), rk, 0.0, Op.min)
+            scan(V("w", w0, w0 + 2 * NB, 2), V("ps3", 0, 2 * n, 2), sub(zero, 0, n), 0.0, Op.add, Op.add)
+            scan(sub(sums, 0, 2 * NB), V("ng", 4, 4 + 8 * NB, 4), sub(pr, 0, 2 * NB), 0.0, Op.mult, Op.add)
         else:
-            nearest(0)
-            if t == 2:
-                spread(1)
+            ts(V("w", w0, w0 + (t + 2) * NB, t + 2), rk, 0.0, Op.min)
+            scan(od, V("ps3", 0, 2 * n, 2), sub(zero, 0, n), 0.0, Op.add, Op.add)
+            for k in range(t + 1):
+                tt(V("w", w0 + k + 1, w0 + (t + 2) * NB, t + 2), sub(od, k * NB, (k + 1) * NB),
+                   V("ng", 8 * (1 + k * NB), 8 * (1 + (k + 1) * NB), 8), Op.mult)
+            scan(sub(sums, 0, n + NB), sub(runs[t], 0, n + NB), sub(pr, 0, n + NB), 0.0, Op.mult, Op.add)
+        pos = V("w", sums[3] + t + 1, sums[3] + n + NB, t + 2)
+        ts(posu, pos, float(A), Op.add)
         for b in range(4):
             mm(4 + b, "qe", "se", 128 * b, "ql", "sl", LAND[t], 128)
-        od, posu, sums = nw(n), nw(NB, "wu"), nw(4 * NB)
-        scan(od, V("ps3", 0, 2 * n, 2), sub(zero, 0, n), 0.0, Op.add, Op.add)
-        if t == 1:
-            tt(V("pk"), ind(V("tab", 0, 2 * C), lu), V("hi"), Op.add)
-        for k in range(t + 1):
-            tt(V("w", w0 + k + 1, w0 + (t + 2) * NB, t + 2), sub(od, k * NB, (k + 1) * NB),
-               V("ng", 8 * (1 + k * NB), 8 * (1 + (k + 1) * NB), 8), Op.mult)
-        scan(sub(sums, 0, n + NB), sub(runs[t], 0, n + NB), sub(pr, 0, n + NB), 0.0, Op.mult, Op.add)
-        pos = V("w", sums[3] + t + 1, sums[3] + n + NB, t + 2)
-        if t == 2:
-            nearest(1)
-        ts(posu, pos, float(A), Op.add)
-        if t == 2:
-            tt(V("pk"), ind(V("tab"), lu), V("hi"), Op.add)
-        pb, s0, nl, cur = nw(), nw(), nw(), nw()
-        lin(pb, pos, 1, A + HCOL[t])
-        lin(s0, pos, -1e4, (B - 0.5) * 1e4)
-        ej = V("ej")
-        op("v", lambda: g.vector.tensor_copy(ej[0].indirect(posu[0]), T.pk[:]), [V("pk"), posu], [ej])
-        if not last:
-            act(V("go"), ind(V("tabi", 0, C), posu), Fn.Sign, bias=A - 0.5, scale=-1.0)
-        if t == 0:
-            act(V("hi"), V("tabi", 0, C), Fn.Copy, scale=32768.0)
-            lin(V("tab", 0, C), V("tabi", 0, C), 4, 4 * (XCOL - 1))
-            st["nl0"] = nl
-        if not last:
-            lin(V("tab", 0, C, F), V("tabi", 0, E), 4, 4 * BCOL[t + 1])
-            lin(V("tab", C, 3 * C, C), V("tabi", 0, 2), 0, 4 * BCOL[t + 1])
-        if t == 1:
-            s1, s2 = nw(), nw()
-            lin(s1, lev, -8, 4 * C)
-            lin(s2, lev, 8, -4 * C)
-        if last:
-            sel, lev3, lu3 = nw(), nw(), nw(NB, "wu")
-            act(sel, s0, Fn.Sign)
-            lin(lev3, lev, 2.0 / C, 1.25)
-        for b in range(4):
-            act(V("big", 4 * BCOL[t] + b, 4 * (BCOL[t] + E), 4), V("ps%d" % (4 + b), 0, E), Fn.Copy, scale=0.5)
-        tt(nl, pb, s0, Op.min)
-        if last:
-            tt(lev3, lev3, sel, Op.add)
-        scan(V("ew"), V("maskd"), V("ej", 0, NJ), 0.0, Op.add, Op.min)
+            if t == 0:
+                tt(V("zall", b, 4 * C, 4 * F), V("ps%d" % (4 + b), 0, E), V("xin", b, 4 * C, 4 * F), Op.add)
+            else:
+                act(V("big", 4 * BCOL[t] + b, 4 * (BCOL[t] + E), 4), V("ps%d" % (4 + b), 0, E), Fn.Copy, scale=0.5)
+        ej, pk = V("ej"), V("pk" if t else "pk0")
+        run("v", lambda posu=posu, pk=pk: g.vector.tensor_copy(ej[0].indirect(posu[0]), pk[0]), [pk, posu], [ej], 0.05 + 3.8 * CYC * C)
+        scan(V("ew"), V("maskd"), V("ej", 0, NJ), 0.0, Op.mult, Op.min)
         nq = NJ // 4
-        vi, lo_, hu, lou = nw(nq, "wi"), nw(nq, "wi"), nw(nq, "wu"), nw(nq, "wu")
-        xo = nw(4 * NB, "wu")
-
-        def xlist(k):
-            ts(sub(xo, k * NB, (k + 1) * NB), cur, 4.0, Op.mult, float(k - 4 * XCOL), Op.add)
-        tt(cur, nl, st["cur"], Op.max)
-        if last:
-            cp(lu3, lev3)
-        ts(vi, V("ew", 3, NJ, 4), col(C1), Op.add, col(C2 + t), Op.add)
-        ts(hu, V("ew", 3, NJ, 4), col(C1H), Op.add, 2.0 ** -13, Op.mult)
-        xlist(0)
-        ts(lo_, vi, 8191, Op.bitwise_and)
-        xlist(1)
-        xlist(2)
-        cp(lou, lo_)
-        for a, b in zip(ZCH, ZCH[1:]):
-            act(V("own", 16 * a, 16 * b), ind(V(xsrc), sub(hu, a, b)), Fn.Copy, scale=0.5)
-        for a, b in zip(ZCH, ZCH[1:]):
-            tt(V("zt", 16 * a, 16 * b), ind(V("big", 4 * BCOL[t], 4 * HCOL[t]), sub(lou, a, b)), V("own", 16 * a, 16 * b), Op.add)
-            if b == 32 and not last:
-                scan(V("cg"), V("go"), V("ones"), 0.0, Op.add, Op.add)
-            if b == nq:
-                xlist(3)
-                if not last:
-                    st["sel"] = nw()
-                    ts(st["sel"], pos, float(B), Op.is_lt, float(C), Op.mult)
-            if b == 32 or b == nq:
-                z0, q0, bank = (0, 0, 4) if b == 32 else (NJ - 128, 128, 0)
-                quant("qz", "sz", q0, 128, V("zt", 4 * z0, 4 * z0 + 512))
-                for k in range(4):
-                    mm(bank + k, "qw", "sw", 128 * k, "qz", "sz", q0, 128)
-        if last:
-            act(V("olv"), ind(V("tabi", 0, 16), lu3), Fn.Copy, scale=0.5)
-            dma("s", T.ol[:], T.olv[0:128:16, :], [V("olv")], [])
-        off = nw((t + 1) * NB, "wu")
+        ew, hu = V("ew", 3, NJ, 4), nw(nq, "wu")
         if t == 0:
-            cp(off, nl)
+            ts(hu, ew, dlo, Op.mult, col(C2), Op.add)
+            for a, b, who in Z0:
+                scaled(who, V("zt", 16 * a, 16 * b), ind(V("zall"), sub(hu, a, b)), 0.5)
+        else:
+            vi, lo_, lou = nw(nq, "wi"), nw(nq, "wi"), nw(nq, "wu")
+            ts(hu, ew, col(DH), Op.mult, col(TH), Op.add)
+            ts(vi, ew, dlo, Op.mult, col(C2 + t), Op.add)
+            ts(lo_, vi, KEY // 4 - 1, Op.bitwise_and)
+            cp(lou, lo_)
+            for a, b in zip(ZCH, ZCH[1:]):
+                act(V("own", 16 * a, 16 * b), ind(V(xsrc), sub(hu, a, b)), Fn.Copy, scale=0.5)
+                tt(V("zt", 16 * a, 16 * b), ind(V("big", 4 * BCOL[t], 4 * HCOL[t]), sub(lou, a, b)), V("own", 16 * a, 16 * b), Op.add)
+        q0 = 0
+        for j, (a, b, who) in enumerate(ZMM):
+            wd = max(128, b - a)
+            quant("qz", "sz", q0, wd, V("zt", 4 * (b - wd), 4 * b))
+            for k in range(4):
+                bank = (4 + 4 * j + k) % 8
+                mm(bank, "qw", "sw", 128 * k, "qz", "sz", q0, wd)
+                scaled(who[k], V("big", 4 * (HCOL[t] + a) + k, 4 * (HCOL[t] + b), 4), V("ps%d" % bank, wd - (b - a), wd), 2.0 ** -6)
+            q0 += wd
+        pb, s0, nl, cur, sel = nw(), nw(), nw(), nw(4 * NB), nw()
+        lin(pb, pos, 4, 4 * (A + HCOL[t] - XCOL))
+        lin(s0, pos, -1e5, (B - 0.5) * 1e5)
+        tt(nl, pb, s0, Op.min)
+        tt(sub(cur, 0, NB), nl, st["cur"], Op.max)
+        xo = nw(4 * NB, "wu")
+        for k in range(1, 4):
+            lin(sub(cur, k * NB, (k + 1) * NB), sub(cur, 0, NB), 1, k)
+        cp(xo, cur)
+        if not last:
+            act(V("go"), ind(V("tabi"), sub(posu, NB - UP // 16, NB)), Fn.Sign, bias=A - 0.5, scale=-1.0)
+            scan(V("cg"), V("go"), V("ones"), 0.0, Op.add, Op.add)
+            ts(sel, pos, float(B), Op.is_lt, float(C), Op.mult)
+            off = nw((t + 1) * NB, "wu")
+        if t == 0:
+            st["nl0"], st["lev"] = nl, sel
+            ts(off, nl, 0.25, Op.mult, float(XCOL - HCOL[0] + 1), Op.add)
         elif t == 1:
-            o1, o2, st["lev2"] = nw(), nw(2 * NB), nw()
+            s1, s2, o1, o2, st["lev"] = nw(), nw(), nw(), nw(2 * NB), nw()
+            lin(s1, lev, -100, 1e4)
+            lin(s2, lev, 100, -1e4)
             tt(o1, nl, s1, Op.min)
             tt(sub(o2, NB, 2 * NB), nl, s2, Op.min)
-            tt(st["lev2"], lev, st["sel"], Op.add)
             tt(sub(o2, 0, NB), o1, st["nl0"], Op.max)
-        for b in range(4):
-            act(V("big", 4 * HCOL[t] + b, 4 * (HCOL[t] + 128), 4), V("ps%d" % (4 + b), 0, 128), Fn.Copy, scale=2.0 ** -6)
-        for b in range(4):
-            o, i = V("big", 4 * (HCOL[t] + 128) + b, 4 * (HCOL[t] + NJ), 4), V("ps%d" % b, 256 - NJ, 128)
-            if b != 2:
-                ts(o, i, 2.0 ** -6, Op.mult)
-            else:
-                act(o, i, Fn.Copy, scale=2.0 ** -6)
-        if t == 1:
-            cp(off, o2)
+            ts(off, o2, 0.25, Op.mult, float(XCOL - HCOL[0] + 1), Op.add)
+            tt(st["lev"], lev, sel, Op.add)
+        else:
+            lev3, lu3 = nw(), nw(NB, "wu")
+            act(sel, s0, Fn.Sign)
+            lin(lev3, lev, 2.0 / C, 1.25)
+            tt(lev3, lev3, sel, Op.add)
+            cp(lu3, lev3)
+            act(V("olv"), ind(V("tabi", 0, 16), lu3), Fn.Copy, scale=0.5)
+            dma("s", T.ol[:], T.olv[0:128:16, :], [V("olv")], [])
         win = V("big", 4 * XCOL, 4 * (HCOL[t] + NJ))
-        pieces = FIN if last else [0, NB]
-        for j, (a, b) in enumerate(zip(pieces, pieces[1:])):
+        pieces = FIN if last else MID
+        for j, (a, b) in enumerate(pieces):
             for k in range(4):
-                o, i = V("xt", 64 * a + k, 64 * b, 4), ind(win, sub(xo, k * NB + a, k * NB + b))
-                if k < 2:
-                    ts(o, i, 2.0, Op.mult)
-                else:
-                    act(o, i, Fn.Copy, scale=2.0)
+                scaled(XWHO[k], V("xt", 64 * a + k, 64 * b, 4), ind(win, sub(xo, k * NB + a, k * NB + b)), 2.0)
             if last:
                 a, b = 16 * a, 16 * b
                 quant("qx", "sx", a, b - a, V("xt", 4 * a, 4 * b))
                 mm(j, "qv", "sv", 0, "qx", "sx", a, b - a)
                 dma("sa"[j], T.oc[:, 4 * a:4 * b], T.qx[:, a:b].bitcast(dt.uint8), [V("qx", a, b)], [])
+                scaled(YWHO[j], V("yb", a, b), V("ps%d" % j, 0, b - a), 1.0)
+                dma("s", T.y[:, a:b], T.yb[:, a:b], [V("yb", a, b)], [])
         xsrc = "xt"
-        st["cur"] = cur
+        st["cur"] = sub(cur, 0, NB)
 
     for k in range(4):
         dma("ag"[k % 2], T.osc[4 * k:4 * k + 4, :], T.sx[32 * k:32 * k + 4, :], [V("sx")], [])
-    for j, (a, b) in enumerate(zip(FIN, FIN[1:])):
-        a, b = 16 * a, 16 * b
-        cp(V("yb", a, b), V("ps%d" % j, 0, b - a))
-        dma("s", T.y[:, a:b], T.yb[:, a:b], [V("yb", a, b)], [])
-    for sem, n in final.items():
-        wait("g", sem, n)
+    issue()

@@ -5,7 +5,7 @@ NJ = A + B
 STEP = [1, 3, 2]
 NB = C // 16
 UP = C - (A - E)
-BCOL = [0, 68, 36]
+BCOL = [4, 68, 36]
 XCOL = 100
 HCOL = [452, 676, 900]
 ENDC = 1124
@@ -13,18 +13,24 @@ LAND = [64, 32, 0]
 KEY = 16384
 TILES = [(352, [21, 20, 19, "band"]), (288, [18, 17, 16, 15]), (224, [14, 13, 12, 11]),
          (160, [10, 9, 8, 7]), (128, [6, 5, 4, 3]), (128, [2, 1])]
-ONACT = [21, 20, 19, 18, 17, 16]
-ONVEC = list(range(9, 16))
-RS = 128
+NV = 0
+ONACT, ONVEC, ONSCA, RS = [21, 20, 19, 18, 17, 16], list(range(9, 16)), [], 168
+PAD = 128
+RUNS = [(14, 16), (0, 14)]
 HEAD = C - 128
-ZCH = [0, 8, 20, 32, 46, 56]
+ZCH = [0, 8, 20, 32, 44, 56]
 Z0 = [(0, 16, "v"), (16, 32, "a"), (32, 44, "v"), (44, 56, "a")]
-ZMM = [(0, 128, "aava"), (128, NJ, "vvav")]
+ZMM = [(0, 128, "****"), (128, NJ, "****")]
 MID = [(0, NB)]
 FIN = [(0, 14), (14, NB)]
-XWHO, YWHO = "vvaa", "vv"
-FAROFF, HOLD = 2.0 ** 96, 2.0 ** 24
-CYC, PECYC, VFIX, AFIX, WAKE, DMA, FAR, TURNS = 0.83e-3, 0.63e-3, 0.03, 0.09, 0.15, 1.5, 1.5, 8
+XWHO, YWHO = "****", "vv"
+FAROFF, HOLD = 2.0 ** 96, 2.0 ** 23
+CYC, PECYC, VFIX, AFIX, DMA, FAR, TURNS = 0.845e-3, 0.77e-3, 0.03, 0.075, 1.0, 2.5, 6
+TRIES = [(0.2, 0.03), (0.24, 0.05)]
+CASES = [((0.06, 0.24), 0.0, {"v": (1.0, -0.01), "a": (1.0, -0.03)}),
+         ((0.17, 0.07), 0.3, {"v": (1.03, 0.01), "a": (1.03, 0.015), "t": (0.92, 0.0)}),
+         ((0.1, 0.14), -0.2, {"v": (1.0, 0.01), "a": (1.0, 0.025), "t": (1.08, 0.0)}),
+         ((0.16, 0.27), 0.3, {"v": (1.0, -0.025), "a": (1.0, -0.03), "t": (1.08, 0.0), "g": (1.15, 0.0)})]
 
 BF, F32, I32, U16, Q4, U8 = "bfloat16", "float32", "int32", "uint16", "float8_e4m3fn_x4", "uint8"
 NGW = 134
@@ -37,12 +43,12 @@ def _sb(n, d):
 SCRATCH = {
     "xin": _sb(4 * C, BF), "uin": _sb(512, BF), "vin": _sb(512, BF), "xt": _sb(4 * C, BF), "zall": _sb(4 * C, BF),
     "big": _sb(4 * ENDC, BF), "own": _sb(4 * NJ, BF), "zt": _sb(4 * NJ, BF), "tt": _sb(512, BF), "ng": _sb(4 * NGW, BF),
-    "sm": _sb(C, F32), "hold": _sb(C, F32), "seg": _sb(C, BF), "junk": _sb(16 * 231, BF), "junk2": _sb(2 * UP, BF),
+    "sm": _sb(C, F32), "hold": _sb(C, F32), "seg": _sb(C, F32), "junk": _sb(16 * 231, BF), "junk2": _sb(2 * UP, BF),
     "cw": _sb(C, F32), "ej": _sb(C, F32), "ew": _sb(NJ, F32), "pk0": _sb(C, F32), "pk": _sb(C, F32), "tab": _sb(3 * C, F32),
     "cp": _sb(2 * C, F32), "go": _sb(UP, BF), "cg": _sb(UP, BF), "olv": _sb(C, F32), "yb": _sb(C, F32),
-    "rows": _sb(24, F32), "rv": _sb(RS * 17, BF), "w": _sb(2560, F32), "wi": _sb(512, I32), "wu": _sb(1024, U16),
-    "tabi": _sb(C, F32), "tabl": _sb(2 * NJ + 1, F32), "im16": _sb(C, BF), "im4": _sb(NJ, BF), "g128": _sb(128, BF), "d128": _sb(128, BF),
-    "maska": _sb(C, BF), "maskc": _sb(C, BF), "maskd": _sb(NJ, BF), "reset": _sb(C, BF), "segr": _sb(C, BF), "ones": _sb(UP, BF),
+    "rv": _sb(RS * NB, F32), "segb": _sb(C, BF), "rows": _sb(24, F32), "holdb": _sb(C, F32), "w": _sb(2560, F32), "wi": _sb(512, I32), "wu": _sb(1024, U16),
+    "tabi": _sb(C, F32), "tabl": _sb(2 * NJ + 1, F32), "im16": _sb(C, BF), "im4": _sb(NJ, BF),
+    "maska": _sb(C, BF), "maskc": _sb(C, BF), "maskd": _sb(NJ, BF), "reset": _sb(C, BF), "segr": _sb(C, BF), "ones": _sb(512, BF), "d128": _sb(128, BF), "g128": _sb(128, BF),
     "hi": _sb(C, F32), "bd": _sb(512, BF), "tri": _sb(512, BF), "tru": _sb(512, BF), "ff": _sb(516, BF),
     "ci": _sb(64, I32), "cf": _sb(512, F32), "cu": _sb(8, U16),
     "qu": _sb(128, Q4), "su": _sb(128, U8), "qu2": _sb(128, Q4), "su2": _sb(128, U8), "qv": _sb(128, Q4), "sv": _sb(128, U8),
@@ -51,16 +57,29 @@ SCRATCH = {
     "qt0": _sb(128, Q4), "st0": _sb(128, U8), "qt1": _sb(128, Q4), "st1": _sb(128, U8),
     "ql": _sb(224, Q4), "sl": _sb(224, U8), "qbd": _sb(128, Q4), "sbd": _sb(128, U8),
     "qtri": _sb(128, Q4), "stri": _sb(128, U8), "qtru": _sb(128, Q4), "stru": _sb(128, U8),
-    "qe": _sb(512, Q4), "se": _sb(512, U8),
+    "qe": _sb(512, Q4), "se": _sb(512, U8), "qo": _sb(128, Q4), "so": _sb(128, U8),
 }
 for _k in range(len(TILES)):
     SCRATCH["m%d" % _k] = _sb(4 * C, BF)
-    SCRATCH["qm%d" % _k] = _sb(C, Q4)
-    SCRATCH["sm%d" % _k] = _sb(C, U8)
+    SCRATCH["qm%d" % _k] = _sb(PAD + C, Q4)
+    SCRATCH["sm%d" % _k] = _sb(PAD + C, U8)
 for _k in range(8):
     SCRATCH["ps%d" % _k] = ("psum", [128, 512], F32)
 
-NDMA = 24
+DEALT = {}
+HWHO, FIRST, AHEAD = "*", 0, True
+OCQ, YQ, OSQ = "**", "**", "***g"
+SLACK = 0.8
+ISSUE = 0.18
+SHAKES, SHAKE, SPAN = 6000, 0.7, 0.8
+INORD, BDG = 4, False
+WARM, SEED = 0.0, 2
+RATE, GATHER = 250.0, 1.08e-3
+ZADD = True
+FARHOLD, GHOLD, ZEARLY = (2.2, 0.9), 1.8, False
+XONE, OUTONE, VLATE = False, False, 0
+NDMA = 44
+ZDMA = True
 SEMAPHORES = ["g", "v", "a", "t"] + ["d%d" % k for k in range(NDMA)] + ["arr0", "arr1", "arr2", "out0", "out1", "out2"]
 
 
@@ -98,7 +117,7 @@ def rank_program(g, core, T, topo):
         for (name, cols), wr in regs:
             bank = name.startswith("ps")
             for c2, k, w2 in uses.get(name, []):
-                if (wr or w2 or (bank and calls[k]["q"] != q)) and cols & c2:
+                if (wr or w2 or (bank and (calls[k]["q"] != q or q == "*"))) and cols & c2:
                     need[k] = need.get(k, False) or not (chain and bank and calls[k]["q"] == q)
         for (name, cols), wr in regs:
             old = uses.get(name, [])
@@ -110,40 +129,87 @@ def rank_program(g, core, T, topo):
 
     def issue():
         n = len(calls)
-        busy = [c["busy"] for c in calls]
+        ways = [c["busy"] if c["q"] == "*" else {c["q"]: c["busy"]} for c in calls]
+        busy = [min(w.values()) for w in ways]
+        lean = [0.0] * n
         before, behind = [[] for c in calls], [[] for c in calls]
         for i, c in enumerate(calls):
             for k, w in c["need"].items():
-                gap = calls[k]["late"] + WAKE if w else 0.0
-                before[i].append((k, gap))
-                behind[k].append((i, gap))
+                gap = calls[k]["late"] if w else 0.0
+                before[i].append((k, gap, w))
+                behind[k].append((i, gap, w))
 
-        def deal(order, links, tail):
-            end, slots = [0.0] * n, {q: [] for q in "gvatsx"}
+        def deal(order, links, tail, wake, spare, due):
+            start, end, who, slots = [0.0] * n, [0.0] * n, [None] * n, {q: [] for q in "gvatsx"}
             for i in order:
-                at = max([end[k] + gap for k, gap in links[i]] + [tail * calls[i]["late"]])
-                row, j = slots[calls[i]["q"]], 0
-                while j < len(row) and row[j][0] < at + busy[i]:
-                    at = max(at, row[j][1])
-                    j += 1
-                row.insert(j, (at, at + busy[i]))
-                end[i] = at + busy[i]
-            return end
+                free = max([end[k] + gap + (wake if w else 0.0) for k, gap, w in links[i]] + [tail * calls[i]["late"]])
+                fits = []
+                for q, d in ways[i].items():
+                    at, row = free, slots[q]
+                    j = len(row)
+                    while j and row[j - 1][1] > at:
+                        j -= 1
+                    while j < len(row) and row[j][0] < at + d:
+                        at = max(at, row[j][1])
+                        j += 1
+                    fits.append((max(at + d, due[i]) + (spare + lean[i] if q == "v" else 0.0), at + d, q, at, j))
+                end[i], who[i], start[i], j = min(fits)[1:]
+                slots[who[i]].insert(j, (start[i], end[i]))
+            return start, end, who
 
-        way = [0.0] * n
-        for i in range(n - 1, -1, -1):
-            way[i] = busy[i] + max([way[k] + gap for k, gap in behind[i]] + [calls[i]["late"]])
-        best = None
-        for turn in range(TURNS):
-            end = deal(sorted(range(n), key=lambda i: (-way[i], i)), before, 0)
-            span = max(end[i] + calls[i]["late"] for i in range(n))
-            if best is None or span < best[0]:
-                best = (span, end)
-            way = deal(sorted(range(n), key=lambda i: (-end[i], -i)), behind, 1)
+        def replay(order, who, wake, slow, more):
+            end, free = [0.0] * n, {q: 0.0 for q in "gvatsx"}
+            for i in order:
+                at = max([free[who[i]]] + [end[k] + gap + ((wake[who[k] == who[i]] + (slow if gap > 0.5 else 0.0)) if w else 0.0)
+                                           for k, gap, w in before[i]])
+                end[i] = free[who[i]] = at + ways[i][who[i]] * more.get(who[i], (1.0, 0.0))[0] + more.get(who[i], (1.0, 0.0))[1]
+            return max(end[i] + calls[i]["late"] for i in range(n))
+
+        best = DEALT.get("best")
+        for wake, spare in [] if best else TRIES:
+            way = [0.0] * n
+            for i in range(n - 1, -1, -1):
+                way[i] = busy[i] + max([way[k] + gap + (wake if w else 0.0) for k, gap, w in behind[i]] + [calls[i]["late"]])
+            due = [0.0] * n
+            for turn in range(TURNS):
+                start, end, who = deal(sorted(range(n), key=lambda i: (-way[i], i)), before, 0, wake, spare, due)
+                order = sorted(range(n), key=lambda i: (start[i], end[i], i))
+                span = sum(replay(order, who, *case) for case in CASES)
+                if best is None or span < best[0]:
+                    best = (span, start, end, who, wake, spare, turn)
+                    keep = (way, due)
+                top_ = max(end)
+                back, way = deal(sorted(range(n), key=lambda i: (-end[i], -start[i], -i)), behind, 1, wake, spare,
+                                 [top_ - a - SLACK for a in start])[:2]
+                due = [max(way) - a - SLACK for a in back]
+        seed, kept = [SEED], best
+
+        def chance():
+            seed[0] = (seed[0] * 1103515245 + 12345) % 2 ** 31
+            return seed[0] / 2 ** 31 - 0.5
+
+        for turn in range(0 if DEALT else SHAKES):
+            mid, way, old = (chance() + 0.5) * max(best[2]), list(keep[0]), list(lean)
+            for i in range(n):
+                if abs(best[1][i] - mid) < SPAN:
+                    way[i] += SHAKE * chance()
+                    lean[i] = 0.4 * chance() if chance() > 0.2 else lean[i]
+                way[i] = min([way[i]] + [way[k] - 1e-6 for k, gap, w in before[i]])
+            start, end, who = deal(sorted(range(n), key=lambda i: (-way[i], i)), before, 0, best[4], best[5], keep[1])
+            order = sorted(range(n), key=lambda i: (start[i], end[i], i))
+            span = sum(replay(order, who, *case) for case in CASES)
+            if span <= best[0] + WARM * (1 - turn / SHAKES) * (chance() + 0.5):
+                best, keep = (span, start, end, who) + best[4:], (way, keep[1])
+                kept = min(kept, best, key=lambda b: b[0])
+            else:
+                lean[:] = old
+        best = DEALT["best"] = kept
         count, known, seen, mark, final = {}, {q: {} for q in queue}, {}, {}, {}
-        for i in sorted(range(n), key=lambda i: (best[1][i] - busy[i], best[1][i], i)):
+        for i in sorted(range(n), key=lambda i: (best[1][i], best[2][i], i)):
             c = calls[i]
-            q = c["q"]
+            q = best[3][i]
+            if c["q"] == "*":
+                c["sem"], c["fn"] = q if c["sem"] == "*" else c["sem"], c["fn"][q]
             count[c["sem"]] = count.get(c["sem"], 0) + c["inc"]
             mark[i] = (c["sem"], count[c["sem"]])
             final[c["sem"]] = count[c["sem"]]
@@ -166,14 +232,19 @@ def rank_program(g, core, T, topo):
                 g.wait_ge(T.sem[sem], m)
 
     def run(q, fn, reads, writes, busy, chain=False):
-        return op(q, lambda s: fn().then_inc(s, 1), reads, writes, busy, chain, late=0.06 if q == "t" else 0.0)
+        return op(q, lambda s: fn().then_inc(s, 1), reads, writes, busy, chain, late=0.07 if q == "t" else 0.0)
 
     ndma = [0]
 
     def dma(q, out, in_, reads, writes, after=(), **kw):
         ndma[0] += 1
-        return op(q, lambda s: queue[q].dma_start(out, in_, **kw).then_inc(s, 16), reads, writes, 0.6 if q == "g" else 0.05,
-                  sem="d%d" % (ndma[0] - 1), inc=16, late=DMA, after=after)
+        x = (writes + reads)[0]
+        kb = 0.128 * x[4] * {BF: 2, U8: 1}.get(SCRATCH[x[2]][2], 4) * (2 if kw else 1)
+        if q == "*":
+            fn = {k: lambda s, k=k: queue[k].dma_start(out, in_).then_inc(s, 16) for k in "sa"}
+            return op(q, fn, reads, writes, {"s": ISSUE, "a": ISSUE}, sem="d%d" % (ndma[0] - 1), inc=16, late=DMA + kb / RATE, after=after)
+        return op(q, lambda s: queue[q].dma_start(out, in_, **kw).then_inc(s, 16), reads, writes, (GHOLD if kw else 0.9) if q == "g" else ISSUE,
+                  sem="d%d" % (ndma[0] - 1), inc=16, late=DMA + kb / RATE, after=after)
 
     def sc(x):
         return x[0] if isinstance(x, tuple) else x
@@ -183,10 +254,13 @@ def rank_program(g, core, T, topo):
 
     def vec(out, *ins, k=1.0):
         if ins and ins[0][5] is None:
-            return 0.05 + 1.56 * CYC * out[4]
+            return 0.05 + GATHER * out[4]
         if k == 1.0 and all(x[5] for x in (out,) + ins):
             k = 0.5
         return VFIX + CYC * max(64, k * (ins[0][4] if ins else out[4]))
+
+    def sca(out, in_):
+        return 0.065 + GATHER * out[4] if in_[5] is None else AFIX + CYC * out[4]
 
     def ts(out, in0, s1, op0, s2=None, op1=None):
         if op1 is None:
@@ -215,26 +289,43 @@ def rank_program(g, core, T, topo):
             kw["scale"] = sc(scale)
         if acc is not None:
             kw["accum_out"] = acc[0]
-        busy = 0.065 + 1.56 * CYC * out[4] if in_[5] is None else AFIX + CYC * out[4]
-        run("a", lambda: g.scalar.activation(out[0], in_[0], fn, **kw), [in_] + cols_of(bias, scale), [out] + cols_of(acc), busy)
+        run("a", lambda: g.scalar.activation(out[0], in_[0], fn, **kw), [in_] + cols_of(bias, scale), [out] + cols_of(acc),
+            sca(out, in_) + (0.02 if acc else 0.0))
 
-    def lin(out, in_, scale, bias):
-        act(out, in_, Fn.Identity, bias=float(bias), scale=float(scale))
+    def lin(out, in_, scale, bias=0.0, q="*"):
+        scale, bias = [x if isinstance(x, tuple) else float(x) for x in (scale, bias)]
+        if q == "v":
+            return ts(out, in_, scale, Op.mult, bias, Op.add)
+        if q == "a":
+            return act(out, in_, Fn.Identity, bias=bias, scale=scale)
+        fn = {"v": lambda s: g.vector.tensor_scalar(out[0], in_[0], sc(scale), sc(bias), Op.mult, Op.add).then_inc(s, 1),
+              "a": lambda s: g.scalar.activation(out[0], in_[0], Fn.Identity, bias=sc(bias), scale=sc(scale)).then_inc(s, 1)}
+        op("*", fn, [in_] + cols_of(scale, bias), [out], {"v": vec(out, in_), "a": sca(out, in_)})
+
+    def count(sums, total, row, lo, hi, junk, q):
+        fn = {"v": lambda s: g.vector.tensor_tensor_scan(sums[0], lo[0], hi[0], 0.0, Op.add, Op.add).then_inc(s, 1),
+              "a": lambda s: g.scalar.activation(junk[0], row[0], Fn.Copy, accum_out=total[0]).then_inc(s, 1)}
+        busy = {"v": vec(sums, lo), "a": sca(junk, row) + 0.02}
+        if q == "*":
+            op(q, fn, [row], [sums, junk], busy)
+        else:
+            op(q, fn[q], [row], [sums, junk], busy[q])
 
     def scaled(q, out, in_, c):
-        if q == "v":
-            ts(out, in_, c, Op.mult)
-        else:
-            act(out, in_, Fn.Copy, scale=c)
+        lin(out, in_, c, 0.0, q)
 
     def quant(qn, sn, a, n, in_):
         q, s = V(qn, a, a + n), V(sn, a, a + n)
-        run("v", lambda: g.vector.quantize_mx(q[0], s[0], in_[0]), [in_], [q, s], 0.012 + 0.88e-3 * n)
+        run("v", lambda: g.vector.quantize_mx(q[0], s[0], in_[0]), [in_], [q, s], 0.013 + 1.06 * CYC * n)
 
-    def mm(bank, wq, ws, wa, xq, xs, xa, n, start=True, stop=True):
+    def mm(bank, wq, ws, wa, xq, xs, xa, n, start=True, stop=True, free=None):
         o = V("ps%d" % bank, 0, n)
         a, b, c, d = V(wq, wa, wa + 128), V(ws, wa, wa + 128), V(xq, xa, xa + n), V(xs, xa, xa + n)
-        run("t", lambda: g.tensor.matmul_mx(o[0], a[0], b[0], c[0], d[0], start, stop), [a, b, c, d], [o], PECYC * (n + 16), chain=not start)
+        me = run("t", lambda: g.tensor.matmul_mx(o[0], a[0], b[0], c[0], d[0], start, stop), [a, b, c, d], [o], PECYC * (n + 16), chain=not start)
+        if free is not None:
+            for k in free:
+                calls[me]["need"].pop(k, None)
+            free.append(me)
 
     def iota(out, pattern, base, cm, small=True):
         busy = 0.13 + 2 * CYC * out[4]
@@ -242,6 +333,9 @@ def rank_program(g, core, T, topo):
             run("g", lambda: g.iota(out[0], pattern, base, cm, allow_small_or_imprecise_dtypes=True), [], [out], busy)
         else:
             run("g", lambda: g.iota(out[0], pattern, base, cm), [], [out], busy)
+
+    def select(out, in_, pattern, o, base, cm):
+        run("g", lambda: g.affine_select(out[0], in_[0], pattern, o, 0.0, base, cm), [in_], [out], 0.17 + 2 * CYC * out[4])
 
     def send(t, qn, sn, a):
         dst = T.cores[(rank + STEP[t]) % n_ranks]
@@ -256,7 +350,7 @@ def rank_program(g, core, T, topo):
         def both(sem):
             g.remote_dma(lq[0].bitcast(dt.uint8), q[0].bitcast(dt.uint8), arr, sem, pid, rid, masks[0])
             g.remote_dma(ls[0], s[0], arr, sem, pid, rid, masks[1])
-        k = op("g", both, [q, s], [], 0.6, sem="out%d" % t, inc=2 * half, late=DMA)
+        k = op("g", both, [q, s], [], FARHOLD[min(t, 1)], sem="out%d" % t, inc=2 * half, late=1.0)
         op("x", None, [], [lq, ls], 0.0, sem="arr%d" % t, inc=2 * (len(topo.engines(src, core)) // 2), late=FAR, after=[k])
 
     top = {"w": 0, "wi": 0, "wu": 0, "cf": 16, "ci": 8}
@@ -271,38 +365,58 @@ def rank_program(g, core, T, topo):
 
     cut = 4 * HEAD
     dma("s", T.uin[:], T.u[:], [], [V("uin")])
-    d1 = dma("a", T.xin[:, cut:], T.x[:, cut:], [], [V("xin", cut)])
-    d2 = dma("s", T.xin[:, :cut], T.x[:, :cut], [], [V("xin", 0, cut)])
-    dma("s", T.zall[:, 4:], T.x[:, :4 * C - 4], [], [V("zall")], after=[d1, d2])
-    dma("g", T.zall[:, 4:], T.xin[:, 4:], [V("xin")], [V("zall")], accum_op=Op.add)
-    dma("s", T.qw[:].bitcast(dt.uint8), T.wc[:], [], [V("qw")], after=[d1, d2])
-    dma("s", T.sw[:], T.ws[:], [], [V("sw")], after=[d1, d2])
-    dma("s", T.vin[:], T.v[:], [], [V("vin")], after=[d1, d2])
+    if XONE:
+        d1 = d2 = dma("a", T.xin[:], T.x[:], [], [V("xin")])
+    else:
+        d1 = dma("a", T.xin[:, cut:], T.x[:, cut:], [], [V("xin", cut)])
+        d2 = dma("s", T.xin[:, :cut], T.x[:, :cut], [], [V("xin", 0, cut)])
+        calls[d2]["need"][d1 - 1] = False
+    if ZADD:
+        k = dma("s", T.zall[:, 4:], T.x[:, :4 * C - 4], [], [V("zall")], after=[] if ZEARLY else [d1, d2])
+        calls[k]["need"].setdefault(d2, False)
+        calls[k]["late"] += 1.5 * ZEARLY
+        dma("g", T.zall[:, 4:], T.xin[:, 4:], [V("xin")], [V("zall")], accum_op=Op.add)
+    added = len(calls) - 1
+    for out, in_, name in ((T.qw[:].bitcast(dt.uint8), T.wc[:], "qw"), (T.sw[:], T.ws[:], "sw")):
+        calls[dma("s", out, in_, [], [V(name)], after=[added - 1] if ZEARLY else [d1, d2])]["need"].setdefault(added - 1, False)
+    dma("s", T.vin[:], T.v[:], [], [V("vin")], after=[added])
 
-    RC, GC, AC, TC, DH, BC0, TH, C2, K0 = 0, 1, 2, 3, 5, 6, 4, 7, 10
-    iota(V("im16"), [[0, NB], [1, 16]], 0, 0)
+    RC, AC, TC, DH, BC0, TH, C2, K0 = 0, 1, 2, 5, 6, 4, 7, 10
     iota(V("ci", 0, 1), [[0, 1]], 0, 1, False)
     uo = nw(8, "ci")
     iota(uo, [[16, 8]], 0, 0, False)
-    iota(V("g128"), [[1, 8], [0, 16]], 0, 0)
     iota(V("d128"), [[1, 128]], 0, -1)
+    iota(V("im16"), [[0, NB], [1, 16]], 0, 0)
+    firsts = len(calls) - 4
+    for k in range(1, INORD):
+        calls[firsts + k]["need"][firsts + k - 1] = False
     m16 = nw(NB, "cf")
     iota(m16, [[16, NB]], 0, 0)
     iota(V("im4"), [[0, NJ // 4], [1, 4]], 0, 0)
-    iota(V("pk0"), [[-4, C]], -4, 0)
     iota(V("tabi"), [[1, C]], 0, 0)
     iota(V("tabl"), [[-4, 2 * NJ + 1]], -4 * (HCOL[0] - 1), 0)
     iota(V("tabl", 0, 1), [[0, 1]], 1, 0)
     iota(V("hi"), [[KEY, C]], 0, 0)
     iota(V("tab", 0, C), [[-4, C]], -4 * (XCOL - 1), 0)
-    iota(V("ones"), [[0, UP]], 1, 0)
+
+    def zeros(out):
+        src = V("ng", 0, out[4])
+        if ZDMA:
+            dma("s", out[0], src[0], [src], [out], after=[d1, d2])
+        else:
+            fn = {"v": lambda s: g.vector.memset(out[0], 0.0).then_inc(s, 1),
+                  "a": lambda s: g.scalar.activation(out[0], src[0], Fn.Copy).then_inc(s, 1)}
+            op("*", fn, [src], [out], {"v": vec(out), "a": sca(out, src)})
 
     low = [min(16 * m for m in slots if m != "band") for wd, slots in TILES]
     zero = nw(3 * NB, "cf")
-    ms(V("ff"), 0.0)
     ms(V("ng"), 0.0)
-    ms(V("rows"), 0.0)
-    ms(V("rv", RS - 1, RS), 0.0)
+    iota(V("ones", 0, UP), [[0, UP]], 1, 0)
+    if NV:
+        ends = nw(NB, "wu")
+        ts(ends, m16, 15.0, Op.add)
+    else:
+        iota(V("rv", RS - 1, RS), [[0, 1]], 0, 0)
     ms(zero, 0.0)
     runs = [None] + [nw((k + 2) * NB, "cf") for k in range(1, R)]
     for k in range(1, R):
@@ -312,46 +426,58 @@ def rank_program(g, core, T, topo):
         a = 4 * low[k] if len(slots) == 4 else 0
         while a < 4 * wd:
             n = min(512, 4 * wd - a)
-            act(V("m%d" % k, a, a + n), V("ng", 0, n), Fn.Copy)
+            zeros(V("m%d" % k, a, a + n))
             a += n
-    act(V("tt"), V("ng", 0, 512), Fn.Copy)
+    zeros(V("tt"))
     p = V("ci", 0, 1)
     ts(V("ci", 2, 3), p, 15, Op.bitwise_and)
-    ts(V("ci", 3, 4), p, 4, Op.arith_shift_right)
-    ts(V("ci", 4, 5), p, 2, Op.arith_shift_right, 3, Op.bitwise_and)
-    ts(V("ci", 5, 6), p, 3, Op.bitwise_and)
-    cp(V("cf", 0, 4), V("ci", 2, 6))
-    ts(V("reset"), V("im16"), 0.0, Op.is_equal, -2 * FAROFF, Op.mult)
-    ts(V("segr"), V("im16"), 0.0, Op.not_equal)
+    ts(V("ci", 3, 4), p, 2, Op.arith_shift_right, 3, Op.bitwise_and)
+    ts(V("ci", 4, 5), p, 3, Op.bitwise_and)
+    cp(V("cf", 0, 3), V("ci", 2, 5))
+    act(V("segr"), V("im16"), Fn.Sign)
+    lin(V("reset"), V("segr"), 2 * FAROFF, -2 * FAROFF)
     ts(V("maska"), V("im16"), col(RC), Op.not_equal, -FAROFF, Op.mult)
     lin(V("maskc"), V("maska"), 66560.0 / FAROFF, 65536.0)
-    for t in range(4):
-        ts(V("bd", t, 512, 4), V("g128"), col(GC), Op.is_equal)
     tri, tru, bd = V("tri"), V("tru"), V("bd")
-    run("g", lambda: g.affine_select(tri[0], bd[0], [[1, 128], [0, 4]], Op.is_gt, 0.0, 0, -1), [bd], [tri], 1.02)
-    run("g", lambda: g.affine_select(tru[0], bd[0], [[-1, 128], [0, 4]], Op.is_ge, 0.0, 0, 1), [bd], [tru], 1.02)
+    act(V("ff"), V("ng", 0, 516), Fn.Copy)
+    act(V("d128"), V("d128"), Fn.Abs)
+    act(V("ff", 3, 515, 4), V("d128"), Fn.Relu, bias=1.0, scale=-1.0)
+    if BDG:
+        select(tri, V("ones", 0, 512), [[-16, 8], [0, 64]], Op.is_ge, 0, 1)
+        calls[-1]["need"][firsts + 3] = False
+        select(bd, tri, [[16, 8], [0, 64]], Op.is_ge, 15, -1)
+        calls.append(calls.pop())
+    else:
+        iota(V("g128"), [[16, 8], [0, 16]], 8, -1)
+        act(V("g128"), V("g128"), Fn.Abs, bias=-0.5)
+        act(V("g128"), V("g128"), Fn.Sign, bias=8.0, scale=-1.0)
+        for t in range(4):
+            act(V("bd", t, 512, 4), V("g128"), Fn.Relu)
+    select(tri, bd, [[1, 128], [0, 4]], Op.is_gt, 0, -1)
+    select(tru, bd, [[-1, 128], [0, 4]], Op.is_ge, 0, 1)
     cp(V("cu"), uo)
     quant("qbd", "sbd", 0, 128, bd)
     quant("qtri", "stri", 0, 128, tri)
     quant("qtru", "stru", 0, 128, tru)
-    ts(V("ff", 3, 515, 4), V("d128"), 0.0, Op.is_equal)
     for b in range(4):
         quant("qe", "se", 128 * b, 128, V("ff", 3 - b, 515 - b))
-    quant("ql", "sl", 96, 128, V("tt"))
-    bcw, iw, cur0, e4, m4, d4 = nw(NB, "cf"), nw(NB, "cf"), nw(NB, "cf"), nw(4, "cf"), nw(4, "cf"), nw(4, "cf")
-    ts(V("maskd"), V("im4"), col(AC), Op.not_equal, HOLD, Op.mult)
-    ts(e4, V("im4", 0, 4), col(AC), Op.is_equal, -1.0, Op.mult)
-    ts(m4, V("im4", 0, 4), col(AC), Op.not_equal, 1.0 / HOLD, Op.mult)
-    scan(d4, m4, e4, 0.0, Op.mult, Op.add)
-    dlo = sub(d4, 3, 4)
-    lin(col(DH), dlo, 4.0 / KEY, 0)
-    lin(col(TH), col(TC), 1, -0.4)
+    pads = [("qm%d" % k, "sm%d" % k, 0, PAD) for k, (wd, slots) in enumerate(TILES) if min(NV if m == "band" else m for m in slots) < NV]
+    for qn, sn, a, n in pads + [("ql", "sl", 96, 128)]:
+        quant(qn, sn, a, n, V("ng", 0, 512))
+    bcw, iw, cur0 = nw(NB, "cf"), nw(NB, "cf"), nw(NB, "cf")
+    act(V("maskd"), V("im4"), Fn.Abs, bias=col(AC), scale=-1.0)
+    act(V("maskd"), V("maskd"), Fn.Sign)
+    lin(V("maskd"), V("maskd"), 17 * HOLD, -16 * HOLD, "a")
     lin(col(BC0), col(RC), -1025, 15 * 1025 - A)
-    act(iw, m16, Fn.Identity, bias=col(RC))
-    act(bcw, m16, Fn.Identity, bias=col(BC0))
+    lin(iw, m16, 1.0, col(RC))
+    lin(bcw, m16, 1.0, col(BC0))
     lin(cur0, iw, 4, 0)
+    lin(col(DH), col(AC), -4 * HOLD / KEY, 12 * HOLD / KEY - 0.4)
+    lin(col(TH), col(TC), 1, col(DH))
     for k in range(R):
-        lin(col(C2 + k), col(TC), 1, -4 * BCOL[k] if k else -4)
+        lin(col(C2 + k), col(AC), -HOLD, 3 * HOLD - 4 * BCOL[k])
+    lin(V("pk0"), V("tabi"), -4 - KEY, -4 * (XCOL - 1))
+    lin(V("pk0", 0, C, F), V("tabi", 0, E), -4 - KEY * F, -4 * BCOL[0])
     for k in range(2):
         lin(col(K0 + k), col(RC), 2, 32 * k + 1 - 2 * E)
     quant("qu", "su", 0, 128, V("uin"))
@@ -375,24 +501,24 @@ def rank_program(g, core, T, topo):
         tt(V("sm", HEAD), V("ps1", 0, 128), V("maska", HEAD), Op.add)
         scan(V("hold", HEAD), V("reset", HEAD), V("sm", HEAD), -FAROFF, Op.add, Op.max)
         tt(V("sm", 0, HEAD), V("ps0", 0, HEAD), V("maska", 0, HEAD), Op.add)
+        if FIRST:
+            calls[-1]["need"].setdefault(len(calls) - 1 - FIRST, False)
         scan(V("hold", 0, HEAD), V("reset", 0, HEAD), V("sm", 0, HEAD), -FAROFF, Op.add, Op.max)
         if t == 0:
             send(0, qn, sn, C - E)
         else:
             acc, bias, tf, toff = nw(2), nw(2), nw(8), nw(8, "wu")
-            act(bias, V("cf", K0, K0 + 2), Fn.Identity, bias=V("cg", UP - 1, UP))
+            lin(bias, V("cf", K0, K0 + 2), 1.0, V("cg", UP - 1, UP))
             for k in range(2):
                 act(V("junk2", k * UP, (k + 1) * UP), V("cg"), Fn.Sign, bias=sub(bias, k, k + 1), scale=-1.0, acc=sub(acc, k, k + 1))
-            for k in range(4):
-                lin(sub(tf, 2 * k, 2 * k + 2), acc, 2, 4 * (C - UP) + 2 * UP + k)
-            cp(toff, tf)
+            for k in range(2):
+                lin(V("w", tf[3] + k, tf[3] + 8, 2), V("im4", 0, 4), 0.5, sub(acc, k, k + 1))
+            ts(toff, tf, 2.0, Op.mult, float(4 * (C - UP) + 2 * UP), Op.add)
             for j in range(4):
                 act(V("tt", j, 4 * E, 4), ind(V("xt"), sub(toff, 2 * j, 2 * j + 2)), Fn.Copy)
             quant("qt%d" % (t - 1), "st%d" % (t - 1), 0, 128, V("tt"))
             send(t, "qt%d" % (t - 1), "st%d" % (t - 1), 0)
-            lev, lf, lu = st["lev"], nw(), nw(NB, "wu")
-            tt(lf, lev, iw, Op.add)
-            cp(lu, lf)
+            lev = st["lev"]
             thr = [lev] + [nw() for k in range(t)]
             for k in range(1, t + 1):
                 act(thr[k], lev, Fn.Abs, bias=-float(C * k))
@@ -400,44 +526,52 @@ def rank_program(g, core, T, topo):
             lin(V("tab", C, 3 * C, C), V("tabi", 0, 2), 0, -4 * BCOL[t])
             for k in range(t):
                 c = V("cp", k * C, (k + 1) * C - 1)
-                act(V("cp", k * C, (k + 1) * C), ind(V("tabl"), sub(off, k * NB, (k + 1) * NB)), Fn.Copy)
+                lin(V("cp", k * C, (k + 1) * C), ind(V("tabl"), sub(off, k * NB, (k + 1) * NB)), 1.0)
                 lin(V("cp", k * C + F - 1, (k + 1) * C, F), V("tabi", 0, E), -4, -4 * (BCOL[t] + 1))
                 scan(V("tab", (k + 1) * C + 1, (k + 2) * C), c, c, -4.0 * BCOL[t], Op.mult, Op.min)
             tt(V("pk"), ind(V("tab", 0, (t + 1) * C), lu), V("hi"), Op.subtract)
         b1, b2, rk = nw(), nw(), nw()
         jk = 0
-        wide = max(k for k, (wd, slots) in enumerate(TILES) if wd > 128)
+        adds = {1: [], 3: [], 4: []}
+        if NV:
+            lin(V("holdb", 0, 16 * NV), ind(V("hold", 0, 16 * NV), sub(ends, 0, NV)), 1.0, 0.0, HWHO)
         for k, (wd, slots) in enumerate(TILES):
+            qm, sm = "qm%d" % k, "sm%d" % k
             for e, m in enumerate(slots):
                 if m == "band":
                     tt(V("m%d" % k, e, 4 * C, 4), V("ps0", 0, C), V("hold"), Op.is_le)
-                    scan(V("seg"), V("segr"), V("m%d" % k, e, 4 * C, 4), 0.0, Op.mult, Op.add)
-                    tt(b1, bcw, V("seg", 15, C, 16), Op.subtract)
+                    scan(V("segb"), V("segr"), V("m%d" % k, e, 4 * C, 4), 0.0, Op.mult, Op.add)
+                    tt(b1, bcw, V("segb", 15, C, 16), Op.subtract)
                     continue
                 o, s, j = V("m%d" % k, e, 64 * m, 4), V("hold", 16 * m + 15, 16 * m + 16), V("junk", jk, jk + 16 * m)
+                if m < NV:
+                    d = 16 * (NV - m)
+                    tt(o, V("ps0", 0, 16 * m), V("holdb", d, 16 * NV), Op.is_lt)
+                    adds[4].append(("qe", "se", 128 * e, qm, sm, PAD - d, 128))
+                    continue
                 jk += 16 * m
+                rows = V("rv", RS * (m + 1) - 1, RS * (m + 1))
                 if m in ONACT:
                     act(j, V("ps2", 0, 16 * m), Fn.Sign, bias=s, scale=-1.0)
-                    act(o, j, Fn.Relu, acc=V("rows", m, m + 1))
+                    act(o, j, Fn.Relu, acc=rows)
                     continue
                 ts(o, V("ps0", 0, 16 * m), s, Op.is_lt)
-                if m in ONVEC:
-                    scan(V("rv", RS * (m + 1) - 8 * m, RS * (m + 1)), V("m%d" % k, e, 32 * m, 4), V("m%d" % k, 32 * m + e, 64 * m, 4),
-                         0.0, Op.add, Op.add)
-                else:
-                    act(j, o, Fn.Copy, acc=V("rows", m, m + 1))
-            quant("qm%d" % k, "sm%d" % k, 0, wd, V("m%d" % k, 0, 4 * wd))
+                count(V("rv", RS * (m + 1) - 8 * m, RS * (m + 1)), rows, o, V("m%d" % k, e, 32 * m, 4),
+                      V("m%d" % k, 32 * m + e, 64 * m, 4), j, "v" if m in ONVEC else "a" if m in ONSCA else "*")
+            quant(qm, sm, PAD, wd, V("m%d" % k, 0, 4 * wd))
             if wd > 128:
-                mm(1, "qbd", "sbd", 0, "qm%d" % k, "sm%d" % k, 0, wd, start=k == 0, stop=k == wide)
-            mm(3, "qbd", "sbd", 0, "qm%d" % k, "sm%d" % k, 0, 128, start=k == 0, stop=k == len(TILES) - 1)
+                adds[1].append(("qbd", "sbd", 0, qm, sm, PAD, wd))
+            adds[3].append(("qbd", "sbd", 0, qm, sm, PAD, 128))
+        for bank, items in adds.items():
+            free = []
+            for k, item in enumerate(items):
+                mm(bank, *item, start=k == 0, stop=k == len(items) - 1, free=free if 0 < k < len(items) - 1 else None)
+        if NV:
+            scan(V("seg", 0, 16 * NV), V("segr", 0, 16 * NV), V("ps4", 0, 16 * NV), 0.0, Op.mult, Op.add)
+            tt(sub(b2, 0, NV), V("seg", 15, 16 * NV, 16), sub(b1, 0, NV), Op.subtract)
+        tt(sub(b2, NV, NB), V("rv", RS * (NV + 1) - 1, None, RS), sub(b1, NV, NB), Op.subtract)
         scan(V("cw", 128), V("maskc", 128), V("ps1", 128, C), 0.0, Op.add, Op.min)
         scan(V("cw", 0, 128), V("maskc", 0, 128), V("ps3", 0, 128), 0.0, Op.add, Op.min)
-        a = 0
-        for m in range(1, NB + 1):
-            if m == NB or (m > 1 and (m in ONVEC) != (m - 1 in ONVEC)):
-                rows = V("rv", RS * (a + 1) - 1, RS * m, RS) if m - 1 in ONVEC else V("rows", a, m)
-                tt(sub(b2, a, m), rows, sub(b1, a, m), Op.subtract)
-                a = m
         n = (t + 1) * NB
         cw = V("cw", 15, C, 16)
         if t == 0:
@@ -466,28 +600,30 @@ def rank_program(g, core, T, topo):
         ts(posu, pos, float(A), Op.add)
         for b in range(4):
             mm(4 + b, "qe", "se", 128 * b, "ql", "sl", LAND[t], 128)
-            if t == 0:
+            if t == 0 and ZADD:
                 tt(V("zall", b, 4 * C, 4 * F), V("ps%d" % (4 + b), 0, E), V("xin", b, 4 * C, 4 * F), Op.add)
             else:
-                act(V("big", 4 * BCOL[t] + b, 4 * (BCOL[t] + E), 4), V("ps%d" % (4 + b), 0, E), Fn.Copy, scale=0.5)
+                lin(V("big", 4 * BCOL[t] + b, 4 * (BCOL[t] + E), 4), V("ps%d" % (4 + b), 0, E), 0.5)
         ej, pk = V("ej"), V("pk" if t else "pk0")
-        run("v", lambda posu=posu, pk=pk: g.vector.tensor_copy(ej[0].indirect(posu[0]), pk[0]), [pk, posu], [ej], 0.05 + 3.8 * CYC * C)
-        scan(V("ew"), V("maskd"), V("ej", 0, NJ), 0.0, Op.mult, Op.min)
+        run("v", lambda posu=posu, pk=pk: g.vector.tensor_copy(ej[0].indirect(posu[0]), pk[0]), [pk, posu], [ej], 0.05 + 2 * GATHER * C)
+        scan(V("ew"), V("maskd"), V("ej", 0, NJ), 0.0, Op.add, Op.max)
         nq = NJ // 4
         ew, hu = V("ew", 3, NJ, 4), nw(nq, "wu")
-        if t == 0:
-            ts(hu, ew, dlo, Op.mult, col(C2), Op.add)
+        ts(hu, ew, -4.0 / KEY, Op.mult, col(TH), Op.add)
+        if t == 0 and ZADD:
             for a, b, who in Z0:
                 scaled(who, V("zt", 16 * a, 16 * b), ind(V("zall"), sub(hu, a, b)), 0.5)
         else:
             vi, lo_, lou = nw(nq, "wi"), nw(nq, "wi"), nw(nq, "wu")
-            ts(hu, ew, col(DH), Op.mult, col(TH), Op.add)
-            ts(vi, ew, dlo, Op.mult, col(C2 + t), Op.add)
+            ts(vi, ew, -1.0, Op.mult, col(C2 + t), Op.add)
             ts(lo_, vi, KEY // 4 - 1, Op.bitwise_and)
-            cp(lou, lo_)
+            ts(lou, lo_, col(TC), Op.add)
             for a, b in zip(ZCH, ZCH[1:]):
                 act(V("own", 16 * a, 16 * b), ind(V(xsrc), sub(hu, a, b)), Fn.Copy, scale=0.5)
                 tt(V("zt", 16 * a, 16 * b), ind(V("big", 4 * BCOL[t], 4 * HCOL[t]), sub(lou, a, b)), V("own", 16 * a, 16 * b), Op.add)
+                if a and AHEAD:
+                    for k in (1, 2):
+                        calls[-k]["need"].setdefault(len(calls) - k - 2, False)
         q0 = 0
         for j, (a, b, who) in enumerate(ZMM):
             wd = max(128, b - a)
@@ -497,23 +633,25 @@ def rank_program(g, core, T, topo):
                 mm(bank, "qw", "sw", 128 * k, "qz", "sz", q0, wd)
                 scaled(who[k], V("big", 4 * (HCOL[t] + a) + k, 4 * (HCOL[t] + b), 4), V("ps%d" % bank, wd - (b - a), wd), 2.0 ** -6)
             q0 += wd
-        pb, s0, nl, cur, sel = nw(), nw(), nw(), nw(4 * NB), nw()
+        nlist = (5 if last else 6 + t) * NB
+        pb, s0, nl, cur, sel, xo = nw(), nw(), nw(), nw(nlist), nw(), nw(nlist, "wu")
         lin(pb, pos, 4, 4 * (A + HCOL[t] - XCOL))
         lin(s0, pos, -1e5, (B - 0.5) * 1e5)
         tt(nl, pb, s0, Op.min)
         tt(sub(cur, 0, NB), nl, st["cur"], Op.max)
-        xo = nw(4 * NB, "wu")
         for k in range(1, 4):
             lin(sub(cur, k * NB, (k + 1) * NB), sub(cur, 0, NB), 1, k)
-        cp(xo, cur)
+        act(sel, s0, Fn.Sign)
+        lf, of = sub(cur, 4 * NB, 5 * NB), sub(cur, 5 * NB, nlist)
+        lu, off = sub(xo, 4 * NB, 5 * NB), sub(xo, 5 * NB, nlist)
         if not last:
             act(V("go"), ind(V("tabi"), sub(posu, NB - UP // 16, NB)), Fn.Sign, bias=A - 0.5, scale=-1.0)
-            scan(V("cg"), V("go"), V("ones"), 0.0, Op.add, Op.add)
-            ts(sel, pos, float(B), Op.is_lt, float(C), Op.mult)
-            off = nw((t + 1) * NB, "wu")
+            scan(V("cg"), V("go"), V("ones", 0, UP), 0.0, Op.add, Op.add)
+            lin(sel, sel, C / 2, C / 2)
         if t == 0:
             st["nl0"], st["lev"] = nl, sel
-            ts(off, nl, 0.25, Op.mult, float(XCOL - HCOL[0] + 1), Op.add)
+            lin(of, nl, 0.25, XCOL - HCOL[0] + 1)
+            tt(lf, sel, iw, Op.add)
         elif t == 1:
             s1, s2, o1, o2, st["lev"] = nw(), nw(), nw(), nw(2 * NB), nw()
             lin(s1, lev, -100, 1e4)
@@ -521,15 +659,15 @@ def rank_program(g, core, T, topo):
             tt(o1, nl, s1, Op.min)
             tt(sub(o2, NB, 2 * NB), nl, s2, Op.min)
             tt(sub(o2, 0, NB), o1, st["nl0"], Op.max)
-            ts(off, o2, 0.25, Op.mult, float(XCOL - HCOL[0] + 1), Op.add)
+            lin(of, o2, 0.25, XCOL - HCOL[0] + 1)
             tt(st["lev"], lev, sel, Op.add)
+            tt(lf, st["lev"], iw, Op.add)
         else:
-            lev3, lu3 = nw(), nw(NB, "wu")
-            act(sel, s0, Fn.Sign)
-            lin(lev3, lev, 2.0 / C, 1.25)
-            tt(lev3, lev3, sel, Op.add)
-            cp(lu3, lev3)
-            act(V("olv"), ind(V("tabi", 0, 16), lu3), Fn.Copy, scale=0.5)
+            lin(lf, lev, 2.0 / C, 1.25)
+            tt(lf, lf, sel, Op.add)
+        cp(xo, cur)
+        if last:
+            act(V("olv"), ind(V("tabi", 0, 16), lu), Fn.Copy, scale=0.5)
             dma("s", T.ol[:], T.olv[0:128:16, :], [V("olv")], [])
         win = V("big", 4 * XCOL, 4 * (HCOL[t] + NJ))
         pieces = FIN if last else MID
@@ -540,12 +678,16 @@ def rank_program(g, core, T, topo):
                 a, b = 16 * a, 16 * b
                 quant("qx", "sx", a, b - a, V("xt", 4 * a, 4 * b))
                 mm(j, "qv", "sv", 0, "qx", "sx", a, b - a)
-                dma("sa"[j], T.oc[:, 4 * a:4 * b], T.qx[:, a:b].bitcast(dt.uint8), [V("qx", a, b)], [])
                 scaled(YWHO[j], V("yb", a, b), V("ps%d" % j, 0, b - a), 1.0)
-                dma("s", T.y[:, a:b], T.yb[:, a:b], [V("yb", a, b)], [])
+                if not OUTONE:
+                    dma(OCQ[j], T.oc[:, 4 * a:4 * b], T.qx[:, a:b].bitcast(dt.uint8), [V("qx", a, b)], [])
+                    dma(YQ[j], T.y[:, a:b], T.yb[:, a:b], [V("yb", a, b)], [])
+        if last and OUTONE:
+            dma(OCQ[0], T.oc[:], T.qx[:].bitcast(dt.uint8), [V("qx")], [])
+            dma(YQ[0], T.y[:], T.yb[:], [V("yb")], [])
         xsrc = "xt"
         st["cur"] = sub(cur, 0, NB)
 
     for k in range(4):
-        dma("ag"[k % 2], T.osc[4 * k:4 * k + 4, :], T.sx[32 * k:32 * k + 4, :], [V("sx")], [])
+        dma(OSQ[k], T.osc[4 * k:4 * k + 4, :], T.sx[32 * k:32 * k + 4, :], [V("sx", 0, 8)] + [V("sx")], [])
     issue()

from concourse.mybir import dt, AluOpType as Op, ActivationFunctionType as Fn

C, A, B, E, F, R = 352, 160, 64, 32, 11, 3
NJ = A + B
STEP = [1, 3, 2]
NB = C // 16
UP = C - (A - E)
BCOL = [4, 68, 36]
XCOL = 100
HCOL = [452, 676, 900]
ENDC = 1124
LAND = [64, 32, 0]
KEY = 16384
TILES = [(352, [21, 20, 19, "band"]), (288, [18, 17, 16, 15]), (224, [14, 13, 12, 11]),
         (160, [10, 9, 8, 7]), (128, [6, 5, 4, 3]), (128, [2, 1])]
NV = 0
ONACT, ONVEC, ONSCA, RS = [21, 20, 19, 18, 17, 16], list(range(9, 16)), [], 168
PAD = 128
RUNS = [(14, 16), (0, 14)]
HEAD = C - 128
ZCH = [0, 8, 20, 32, 44, 56]
Z0 = [(0, 16, "v"), (16, 32, "a"), (32, 44, "v"), (44, 56, "a")]
ZMM = [(0, 128, "****"), (128, NJ, "****")]
MID = [(0, NB)]
FIN = [(0, 14), (14, NB)]
XWHO, YWHO = "****", "vv"
FAROFF, HOLD = 2.0 ** 96, 2.0 ** 23
CYC, PECYC, VFIX, AFIX, DMA, FAR, TURNS = 0.845e-3, 0.77e-3, 0.03, 0.075, 1.0, 2.5, 6
TRIES = [(0.2, 0.03), (0.24, 0.05)]
CASES = [((0.06, 0.24), 0.0, {"v": (1.0, -0.01), "a": (1.0, -0.03)}),
         ((0.17, 0.07), 0.3, {"v": (1.03, 0.01), "a": (1.03, 0.015), "t": (0.92, 0.0)}),
         ((0.1, 0.14), -0.2, {"v": (1.0, 0.01), "a": (1.0, 0.025), "t": (1.08, 0.0)}),
         ((0.16, 0.27), 0.3, {"v": (1.0, -0.025), "a": (1.0, -0.03), "t": (1.08, 0.0), "g": (1.15, 0.0)})]

BF, F32, I32, U16, Q4, U8 = "bfloat16", "float32", "int32", "uint16", "float8_e4m3fn_x4", "uint8"
NGW = 134


def _sb(n, d):
    return ("sbuf", [128, n], d)


SCRATCH = {
    "xin": _sb(4 * C, BF), "uin": _sb(512, BF), "vin": _sb(512, BF), "xt": _sb(4 * C, BF), "zall": _sb(4 * C, BF),
    "big": _sb(4 * ENDC, BF), "own": _sb(4 * NJ, BF), "zt": _sb(4 * NJ, BF), "tt": _sb(512, BF), "ng": _sb(4 * NGW, BF),
    "sm": _sb(C, F32), "hold": _sb(C, F32), "seg": _sb(C, F32), "junk": _sb(16 * 231, BF), "junk2": _sb(2 * UP, BF),
    "cw": _sb(C, F32), "ej": _sb(C, F32), "ew": _sb(NJ, F32), "pk0": _sb(C, F32), "pk": _sb(C, F32), "tab": _sb(3 * C, F32),
    "cp": _sb(2 * C, F32), "go": _sb(UP, BF), "cg": _sb(UP, BF), "olv": _sb(C, F32), "yb": _sb(C, F32),
    "rv": _sb(RS * NB, F32), "segb": _sb(C, BF), "rows": _sb(24, F32), "holdb": _sb(C, F32), "w": _sb(2560, F32), "wi": _sb(512, I32), "wu": _sb(1024, U16),
    "tabi": _sb(C, F32), "tabl": _sb(2 * NJ + 1, F32), "im16": _sb(C, BF), "im4": _sb(NJ, BF),
    "maska": _sb(C, BF), "maskc": _sb(C, BF), "maskd": _sb(NJ, BF), "reset": _sb(C, BF), "segr": _sb(C, BF), "ones": _sb(512, BF), "d128": _sb(128, BF), "g128": _sb(128, BF),
    "hi": _sb(C, F32), "bd": _sb(512, BF), "tri": _sb(512, BF), "tru": _sb(512, BF), "ff": _sb(516, BF),
    "ci": _sb(64, I32), "cf": _sb(512, F32), "cu": _sb(8, U16),
    "qu": _sb(128, Q4), "su": _sb(128, U8), "qu2": _sb(128, Q4), "su2": _sb(128, U8), "qv": _sb(128, Q4), "sv": _sb(128, U8),
    "qw": _sb(512, Q4), "sw": _sb(512, U8), "qx0": _sb(C, Q4), "sx0": _sb(C, U8), "qx": _sb(C, Q4), "sx": _sb(C, U8),
    "qz": _sb(256, Q4), "sz": _sb(256, U8), "qn": _sb(NGW, Q4), "sn": _sb(NGW, U8),
    "qt0": _sb(128, Q4), "st0": _sb(128, U8), "qt1": _sb(128, Q4), "st1": _sb(128, U8),
    "ql": _sb(224, Q4), "sl": _sb(224, U8), "qbd": _sb(128, Q4), "sbd": _sb(128, U8),
    "qtri": _sb(128, Q4), "stri": _sb(128, U8), "qtru": _sb(128, Q4), "stru": _sb(128, U8),
    "qe": _sb(512, Q4), "se": _sb(512, U8), "qo": _sb(128, Q4), "so": _sb(128, U8),
}
for _k in range(len(TILES)):
    SCRATCH["m%d" % _k] = _sb(4 * C, BF)
    SCRATCH["qm%d" % _k] = _sb(PAD + C, Q4)
    SCRATCH["sm%d" % _k] = _sb(PAD + C, U8)
for _k in range(8):
    SCRATCH["ps%d" % _k] = ("psum", [128, 512], F32)

DEALT = {}
HWHO, FIRST, AHEAD = "*", 0, True
OCQ, YQ, OSQ = "**", "**", "***g"
SLACK = 0.8
ISSUE = 0.18
SHAKES, SHAKE, SPAN = 6000, 0.7, 0.8
INORD, BDG = 4, False
WARM, SEED = 0.0, 2
RATE, GATHER = 250.0, 1.08e-3
ZADD = True
FARHOLD, GHOLD, ZEARLY = (2.2, 0.9), 1.8, False
XONE, OUTONE, VLATE = False, False, 0
NDMA = 44
ZDMA = True
SEMAPHORES = ["g", "v", "a", "t"] + ["d%d" % k for k in range(NDMA)] + ["arr0", "arr1", "arr2", "out0", "out1", "out2"]


def rank_program(g, core, T, topo):
    rank = T.rank_of(core)
    if rank is None:
        return
    n_ranks = len(T.cores)
    queue = {"g": g, "v": g.vector, "a": g.scalar, "t": g.tensor, "s": g.sync}
    calls = []
    uses = {}

    def V(name, a=0, b=None, s=1):
        width = SCRATCH[name][1][1]
        b = width if b is None else b
        if name.startswith("ps"):
            cols = 1
        elif s == 1:
            cols = ((1 << (b - a)) - 1) << a
        else:
            cols = sum(1 << c for c in range(a, b, s))
        ap = T[name][:, a:b] if s == 1 else T[name][:, a:b:s]
        return (ap, [(name, cols)], name, a, len(range(a, b, s)), SCRATCH[name][2] in (BF, U16))

    def sub(v, a, b):
        return V(v[2], v[3] + a, v[3] + b)

    def ind(win, off):
        return (win[0].indirect(off[0]), win[1] + off[1], None, 0, 16 * off[4], None)

    def op(q, fn, reads, writes, busy, chain=False, sem=None, inc=1, late=0.0, after=()):
        me = len(calls)
        need = {k: True for k in after}
        regs = [(r, False) for x in reads for r in x[1]] + [(r, True) for x in writes for r in x[1]]
        for (name, cols), wr in regs:
            bank = name.startswith("ps")
            for c2, k, w2 in uses.get(name, []):
                if (wr or w2 or (bank and (calls[k]["q"] != q or q == "*"))) and cols & c2:
                    need[k] = need.get(k, False) or not (chain and bank and calls[k]["q"] == q)
        for (name, cols), wr in regs:
            old = uses.get(name, [])
            if wr and not chain:
                old = [u for u in old if u[0] & ~cols or u[1] == me]
            uses[name] = old + [(cols, me, wr)]
        calls.append({"q": q, "fn": fn, "need": need, "sem": sem or q, "inc": inc, "busy": busy, "late": late})
        return me

    def issue():
        n = len(calls)
        ways = [c["busy"] if c["q"] == "*" else {c["q"]: c["busy"]} for c in calls]
        busy = [min(w.values()) for w in ways]
        lean = [0.0] * n
        before, behind = [[] for c in calls], [[] for c in calls]
        for i, c in enumerate(calls):
            for k, w in c["need"].items():
                gap = calls[k]["late"] if w else 0.0
                before[i].append((k, gap, w))
                behind[k].append((i, gap, w))

        def deal(order, links, tail, wake, spare, due):
            start, end, who, slots = [0.0] * n, [0.0] * n, [None] * n, {q: [] for q in "gvatsx"}
            for i in order:
                free = max([end[k] + gap + (wake if w else 0.0) for k, gap, w in links[i]] + [tail * calls[i]["late"]])
                fits = []
                for q, d in ways[i].items():
                    at, row = free, slots[q]
                    j = len(row)
                    while j and row[j - 1][1] > at:
                        j -= 1
                    while j < len(row) and row[j][0] < at + d:
                        at = max(at, row[j][1])
                        j += 1
                    fits.append((max(at + d, due[i]) + (spare + lean[i] if q == "v" else 0.0), at + d, q, at, j))
                end[i], who[i], start[i], j = min(fits)[1:]
                slots[who[i]].insert(j, (start[i], end[i]))
            return start, end, who

        def replay(order, who, wake, slow, more):
            end, free = [0.0] * n, {q: 0.0 for q in "gvatsx"}
            for i in order:
                at = max([free[who[i]]] + [end[k] + gap + ((wake[who[k] == who[i]] + (slow if gap > 0.5 else 0.0)) if w else 0.0)
                                           for k, gap, w in before[i]])
                end[i] = free[who[i]] = at + ways[i][who[i]] * more.get(who[i], (1.0, 0.0))[0] + more.get(who[i], (1.0, 0.0))[1]
            return max(end[i] + calls[i]["late"] for i in range(n))

        best = DEALT.get("best")
        for wake, spare in [] if best else TRIES:
            way = [0.0] * n
            for i in range(n - 1, -1, -1):
                way[i] = busy[i] + max([way[k] + gap + (wake if w else 0.0) for k, gap, w in behind[i]] + [calls[i]["late"]])
            due = [0.0] * n
            for turn in range(TURNS):
                start, end, who = deal(sorted(range(n), key=lambda i: (-way[i], i)), before, 0, wake, spare, due)
                order = sorted(range(n), key=lambda i: (start[i], end[i], i))
                span = sum(replay(order, who, *case) for case in CASES)
                if best is None or span < best[0]:
                    best = (span, start, end, who, wake, spare, turn)
                    keep = (way, due)
                top_ = max(end)
                back, way = deal(sorted(range(n), key=lambda i: (-end[i], -start[i], -i)), behind, 1, wake, spare,
                                 [top_ - a - SLACK for a in start])[:2]
                due = [max(way) - a - SLACK for a in back]
        seed, kept = [SEED], best

        def chance():
            seed[0] = (seed[0] * 1103515245 + 12345) % 2 ** 31
            return seed[0] / 2 ** 31 - 0.5

        for turn in range(0 if DEALT else SHAKES):
            mid, way, old = (chance() + 0.5) * max(best[2]), list(keep[0]), list(lean)
            for i in range(n):
                if abs(best[1][i] - mid) < SPAN:
                    way[i] += SHAKE * chance()
                    lean[i] = 0.4 * chance() if chance() > 0.2 else lean[i]
                way[i] = min([way[i]] + [way[k] - 1e-6 for k, gap, w in before[i]])
            start, end, who = deal(sorted(range(n), key=lambda i: (-way[i], i)), before, 0, best[4], best[5], keep[1])
            order = sorted(range(n), key=lambda i: (start[i], end[i], i))
            span = sum(replay(order, who, *case) for case in CASES)
            if span <= best[0] + WARM * (1 - turn / SHAKES) * (chance() + 0.5):
                best, keep = (span, start, end, who) + best[4:], (way, keep[1])
                kept = min(kept, best, key=lambda b: b[0])
            else:
                lean[:] = old
        best = DEALT["best"] = kept
        count, known, seen, mark, final = {}, {q: {} for q in queue}, {}, {}, {}
        for i in sorted(range(n), key=lambda i: (best[1][i], best[2][i], i)):
            c = calls[i]
            q = best[3][i]
            if c["q"] == "*":
                c["sem"], c["fn"] = q if c["sem"] == "*" else c["sem"], c["fn"][q]
            count[c["sem"]] = count.get(c["sem"], 0) + c["inc"]
            mark[i] = (c["sem"], count[c["sem"]])
            final[c["sem"]] = count[c["sem"]]
            if q == "x":
                continue
            want = {}
            for k, w in c["need"].items():
                if w:
                    want[mark[k][0]] = max(want.get(mark[k][0], 0), mark[k][1])
            for sem in sorted(want, key=lambda k: k == q):
                if known[q].get(sem, 0) < want[sem]:
                    queue[q].wait_ge(T.sem[sem], want[sem])
                    known[q][sem] = want[sem]
                    for k, m in seen.get((sem, want[sem]), {}).items():
                        known[q][k] = max(known[q].get(k, 0), m)
            seen[mark[i]] = dict(known[q])
            c["fn"](T.sem[c["sem"]])
        for sem, m in final.items():
            if known["g"].get(sem, 0) < m:
                g.wait_ge(T.sem[sem], m)

    def run(q, fn, reads, writes, busy, chain=False):
        return op(q, lambda s: fn().then_inc(s, 1), reads, writes, busy, chain, late=0.07 if q == "t" else 0.0)

    ndma = [0]

    def dma(q, out, in_, reads, writes, after=(), **kw):
        ndma[0] += 1
        x = (writes + reads)[0]
        kb = 0.128 * x[4] * {BF: 2, U8: 1}.get(SCRATCH[x[2]][2], 4) * (2 if kw else 1)
        if q == "*":
            fn = {k: lambda s, k=k: queue[k].dma_start(out, in_).then_inc(s, 16) for k in "sa"}
            return op(q, fn, reads, writes, {"s": ISSUE, "a": ISSUE}, sem="d%d" % (ndma[0] - 1), inc=16, late=DMA + kb / RATE, after=after)
        return op(q, lambda s: queue[q].dma_start(out, in_, **kw).then_inc(s, 16), reads, writes, (GHOLD if kw else 0.9) if q == "g" else ISSUE,
                  sem="d%d" % (ndma[0] - 1), inc=16, late=DMA + kb / RATE, after=after)

    def sc(x):
        return x[0] if isinstance(x, tuple) else x

    def cols_of(*xs):
        return [x for x in xs if isinstance(x, tuple)]

    def vec(out, *ins, k=1.0):
        if ins and ins[0][5] is None:
            return 0.05 + GATHER * out[4]
        if k == 1.0 and all(x[5] for x in (out,) + ins):
            k = 0.5
        return VFIX + CYC * max(64, k * (ins[0][4] if ins else out[4]))

    def sca(out, in_):
        return 0.065 + GATHER * out[4] if in_[5] is None else AFIX + CYC * out[4]

    def ts(out, in0, s1, op0, s2=None, op1=None):
        if op1 is None:
            run("v", lambda: g.vector.tensor_scalar(out[0], in0[0], sc(s1), None, op0), [in0] + cols_of(s1), [out], vec(out, in0))
        else:
            run("v", lambda: g.vector.tensor_scalar(out[0], in0[0], sc(s1), sc(s2), op0, op1), [in0] + cols_of(s1, s2), [out], vec(out, in0))

    def tt(out, in0, in1, o):
        k = 1.001 if (in0[2] or "").startswith("ps") else 2.0
        run("v", lambda: g.vector.tensor_tensor(out[0], in0[0], in1[0], o), [in0, in1], [out], vec(out, in0, in1, k=k))

    def cp(out, in_):
        run("v", lambda: g.vector.tensor_copy(out[0], in_[0]), [in_], [out], vec(out, in_))

    def ms(out, c):
        run("v", lambda: g.vector.memset(out[0], c), [], [out], vec(out))

    def scan(out, d0, d1, init, o0, o1):
        run("v", lambda: g.vector.tensor_tensor_scan(out[0], d0[0], d1[0], init, o0, o1), [d0, d1], [out], vec(out, d0, d1))

    def act(out, in_, fn, bias=None, scale=None, acc=None):
        kw = {}
        if bias is not None:
            kw["bias"] = sc(bias)
        if scale is not None:
            kw["scale"] = sc(scale)
        if acc is not None:
            kw["accum_out"] = acc[0]
        run("a", lambda: g.scalar.activation(out[0], in_[0], fn, **kw), [in_] + cols_of(bias, scale), [out] + cols_of(acc),
            sca(out, in_) + (0.02 if acc else 0.0))

    def lin(out, in_, scale, bias=0.0, q="*"):
        scale, bias = [x if isinstance(x, tuple) else float(x) for x in (scale, bias)]
        if q == "v":
            return ts(out, in_, scale, Op.mult, bias, Op.add)
        if q == "a":
            return act(out, in_, Fn.Identity, bias=bias, scale=scale)
        fn = {"v": lambda s: g.vector.tensor_scalar(out[0], in_[0], sc(scale), sc(bias), Op.mult, Op.add).then_inc(s, 1),
              "a": lambda s: g.scalar.activation(out[0], in_[0], Fn.Identity, bias=sc(bias), scale=sc(scale)).then_inc(s, 1)}
        op("*", fn, [in_] + cols_of(scale, bias), [out], {"v": vec(out, in_), "a": sca(out, in_)})

    def count(sums, total, row, lo, hi, junk, q):
        fn = {"v": lambda s: g.vector.tensor_tensor_scan(sums[0], lo[0], hi[0], 0.0, Op.add, Op.add).then_inc(s, 1),
              "a": lambda s: g.scalar.activation(junk[0], row[0], Fn.Copy, accum_out=total[0]).then_inc(s, 1)}
        busy = {"v": vec(sums, lo), "a": sca(junk, row) + 0.02}
        if q == "*":
            op(q, fn, [row], [sums, junk], busy)
        else:
            op(q, fn[q], [row], [sums, junk], busy[q])

    def scaled(q, out, in_, c):
        lin(out, in_, c, 0.0, q)

    def quant(qn, sn, a, n, in_):
        q, s = V(qn, a, a + n), V(sn, a, a + n)
        run("v", lambda: g.vector.quantize_mx(q[0], s[0], in_[0]), [in_], [q, s], 0.013 + 1.06 * CYC * n)

    def mm(bank, wq, ws, wa, xq, xs, xa, n, start=True, stop=True, free=None):
        o = V("ps%d" % bank, 0, n)
        a, b, c, d = V(wq, wa, wa + 128), V(ws, wa, wa + 128), V(xq, xa, xa + n), V(xs, xa, xa + n)
        me = run("t", lambda: g.tensor.matmul_mx(o[0], a[0], b[0], c[0], d[0], start, stop), [a, b, c, d], [o], PECYC * (n + 16), chain=not start)
        if free is not None:
            for k in free:
                calls[me]["need"].pop(k, None)
            free.append(me)

    def iota(out, pattern, base, cm, small=True):
        busy = 0.13 + 2 * CYC * out[4]
        if small:
            run("g", lambda: g.iota(out[0], pattern, base, cm, allow_small_or_imprecise_dtypes=True), [], [out], busy)
        else:
            run("g", lambda: g.iota(out[0], pattern, base, cm), [], [out], busy)

    def select(out, in_, pattern, o, base, cm):
        run("g", lambda: g.affine_select(out[0], in_[0], pattern, o, 0.0, base, cm), [in_], [out], 0.17 + 2 * CYC * out[4])

    def send(t, qn, sn, a):
        dst = T.cores[(rank + STEP[t]) % n_ranks]
        src = T.cores[(rank - STEP[t]) % n_ranks]
        rid, pid = topo.addr(dst, core)
        eng = topo.engines(core, dst)
        half = len(eng) // 2
        masks = [sum(1 << e for e in eng[:half]), sum(1 << e for e in eng[half:2 * half])]
        q, s = V(qn, a, a + E), V(sn, a, a + E)
        lq, ls, arr = V("ql", LAND[t], LAND[t] + E), V("sl", LAND[t], LAND[t] + E), T.sem["arr%d" % t]

        def both(sem):
            g.remote_dma(lq[0].bitcast(dt.uint8), q[0].bitcast(dt.uint8), arr, sem, pid, rid, masks[0])
            g.remote_dma(ls[0], s[0], arr, sem, pid, rid, masks[1])
        k = op("g", both, [q, s], [], FARHOLD[min(t, 1)], sem="out%d" % t, inc=2 * half, late=1.0)
        op("x", None, [], [lq, ls], 0.0, sem="arr%d" % t, inc=2 * (len(topo.engines(src, core)) // 2), late=FAR, after=[k])

    top = {"w": 0, "wi": 0, "wu": 0, "cf": 16, "ci": 8}

    def nw(n=NB, name="w"):
        a = top[name]
        top[name] = a + n + n % 2
        return V(name, a, a + n)

    def col(k):
        return V("cf", k, k + 1)

    cut = 4 * HEAD
    dma("s", T.uin[:], T.u[:], [], [V("uin")])
    if XONE:
        d1 = d2 = dma("a", T.xin[:], T.x[:], [], [V("xin")])
    else:
        d1 = dma("a", T.xin[:, cut:], T.x[:, cut:], [], [V("xin", cut)])
        d2 = dma("s", T.xin[:, :cut], T.x[:, :cut], [], [V("xin", 0, cut)])
        calls[d2]["need"][d1 - 1] = False
    if ZADD:
        k = dma("s", T.zall[:, 4:], T.x[:, :4 * C - 4], [], [V("zall")], after=[] if ZEARLY else [d1, d2])
        calls[k]["need"].setdefault(d2, False)
        calls[k]["late"] += 1.5 * ZEARLY
        dma("g", T.zall[:, 4:], T.xin[:, 4:], [V("xin")], [V("zall")], accum_op=Op.add)
    added = len(calls) - 1
    for out, in_, name in ((T.qw[:].bitcast(dt.uint8), T.wc[:], "qw"), (T.sw[:], T.ws[:], "sw")):
        calls[dma("s", out, in_, [], [V(name)], after=[added - 1] if ZEARLY else [d1, d2])]["need"].setdefault(added - 1, False)
    dma("s", T.vin[:], T.v[:], [], [V("vin")], after=[added])

    RC, AC, TC, DH, BC0, TH, C2, K0 = 0, 1, 2, 5, 6, 4, 7, 10
    iota(V("ci", 0, 1), [[0, 1]], 0, 1, False)
    uo = nw(8, "ci")
    iota(uo, [[16, 8]], 0, 0, False)
    iota(V("d128"), [[1, 128]], 0, -1)
    iota(V("im16"), [[0, NB], [1, 16]], 0, 0)
    firsts = len(calls) - 4
    for k in range(1, INORD):
        calls[firsts + k]["need"][firsts + k - 1] = False
    m16 = nw(NB, "cf")
    iota(m16, [[16, NB]], 0, 0)
    iota(V("im4"), [[0, NJ // 4], [1, 4]], 0, 0)
    iota(V("tabi"), [[1, C]], 0, 0)
    iota(V("tabl"), [[-4, 2 * NJ + 1]], -4 * (HCOL[0] - 1), 0)
    iota(V("tabl", 0, 1), [[0, 1]], 1, 0)
    iota(V("hi"), [[KEY, C]], 0, 0)
    iota(V("tab", 0, C), [[-4, C]], -4 * (XCOL - 1), 0)

    def zeros(out):
        src = V("ng", 0, out[4])
        if ZDMA:
            dma("s", out[0], src[0], [src], [out], after=[d1, d2])
        else:
            fn = {"v": lambda s: g.vector.memset(out[0], 0.0).then_inc(s, 1),
                  "a": lambda s: g.scalar.activation(out[0], src[0], Fn.Copy).then_inc(s, 1)}
            op("*", fn, [src], [out], {"v": vec(out), "a": sca(out, src)})

    low = [min(16 * m for m in slots if m != "band") for wd, slots in TILES]
    zero = nw(3 * NB, "cf")
    ms(V("ng"), 0.0)
    iota(V("ones", 0, UP), [[0, UP]], 1, 0)
    if NV:
        ends = nw(NB, "wu")
        ts(ends, m16, 15.0, Op.add)
    else:
        iota(V("rv", RS - 1, RS), [[0, 1]], 0, 0)
    ms(zero, 0.0)
    runs = [None] + [nw((k + 2) * NB, "cf") for k in range(1, R)]
    for k in range(1, R):
        iota(runs[k], [[0, (k + 2) * NB]], 1, 0)
        iota(V("cf", runs[k][3], runs[k][3] + (k + 2) * NB, k + 2), [[0, NB]], 0, 0)
    for k, (wd, slots) in enumerate(TILES):
        a = 4 * low[k] if len(slots) == 4 else 0
        while a < 4 * wd:
            n = min(512, 4 * wd - a)
            zeros(V("m%d" % k, a, a + n))
            a += n
    zeros(V("tt"))
    p = V("ci", 0, 1)
    ts(V("ci", 2, 3), p, 15, Op.bitwise_and)
    ts(V("ci", 3, 4), p, 2, Op.arith_shift_right, 3, Op.bitwise_and)
    ts(V("ci", 4, 5), p, 3, Op.bitwise_and)
    cp(V("cf", 0, 3), V("ci", 2, 5))
    act(V("segr"), V("im16"), Fn.Sign)
    lin(V("reset"), V("segr"), 2 * FAROFF, -2 * FAROFF)
    ts(V("maska"), V("im16"), col(RC), Op.not_equal, -FAROFF, Op.mult)
    lin(V("maskc"), V("maska"), 66560.0 / FAROFF, 65536.0)
    tri, tru, bd = V("tri"), V("tru"), V("bd")
    act(V("ff"), V("ng", 0, 516), Fn.Copy)
    act(V("d128"), V("d128"), Fn.Abs)
    act(V("ff", 3, 515, 4), V("d128"), Fn.Relu, bias=1.0, scale=-1.0)
    if BDG:
        select(tri, V("ones", 0, 512), [[-16, 8], [0, 64]], Op.is_ge, 0, 1)
        calls[-1]["need"][firsts + 3] = False
        select(bd, tri, [[16, 8], [0, 64]], Op.is_ge, 15, -1)
        calls.append(calls.pop())
    else:
        iota(V("g128"), [[16, 8], [0, 16]], 8, -1)
        act(V("g128"), V("g128"), Fn.Abs, bias=-0.5)
        act(V("g128"), V("g128"), Fn.Sign, bias=8.0, scale=-1.0)
        for t in range(4):
            act(V("bd", t, 512, 4), V("g128"), Fn.Relu)
    select(tri, bd, [[1, 128], [0, 4]], Op.is_gt, 0, -1)
    select(tru, bd, [[-1, 128], [0, 4]], Op.is_ge, 0, 1)
    cp(V("cu"), uo)
    quant("qbd", "sbd", 0, 128, bd)
    quant("qtri", "stri", 0, 128, tri)
    quant("qtru", "stru", 0, 128, tru)
    for b in range(4):
        quant("qe", "se", 128 * b, 128, V("ff", 3 - b, 515 - b))
    pads = [("qm%d" % k, "sm%d" % k, 0, PAD) for k, (wd, slots) in enumerate(TILES) if min(NV if m == "band" else m for m in slots) < NV]
    for qn, sn, a, n in pads + [("ql", "sl", 96, 128)]:
        quant(qn, sn, a, n, V("ng", 0, 512))
    bcw, iw, cur0 = nw(NB, "cf"), nw(NB, "cf"), nw(NB, "cf")
    act(V("maskd"), V("im4"), Fn.Abs, bias=col(AC), scale=-1.0)
    act(V("maskd"), V("maskd"), Fn.Sign)
    lin(V("maskd"), V("maskd"), 17 * HOLD, -16 * HOLD, "a")
    lin(col(BC0), col(RC), -1025, 15 * 1025 - A)
    lin(iw, m16, 1.0, col(RC))
    lin(bcw, m16, 1.0, col(BC0))
    lin(cur0, iw, 4, 0)
    lin(col(DH), col(AC), -4 * HOLD / KEY, 12 * HOLD / KEY - 0.4)
    lin(col(TH), col(TC), 1, col(DH))
    for k in range(R):
        lin(col(C2 + k), col(AC), -HOLD, 3 * HOLD - 4 * BCOL[k])
    lin(V("pk0"), V("tabi"), -4 - KEY, -4 * (XCOL - 1))
    lin(V("pk0", 0, C, F), V("tabi", 0, E), -4 - KEY * F, -4 * BCOL[0])
    for k in range(2):
        lin(col(K0 + k), col(RC), 2, 32 * k + 1 - 2 * E)
    quant("qu", "su", 0, 128, V("uin"))
    q2, q1, cu = V("qu2"), V("qu"), V("cu")
    run("v", lambda: g.vector.tensor_copy(q2[0].bitcast(dt.uint32), q1[0].bitcast(dt.uint32).indirect(cu[0])), [q1, cu], [q2], 0.22)
    act(V("su2"), ind(V("su"), cu), Fn.Copy)
    quant("qv", "sv", 0, 128, V("vin"))
    act(V("big", 4 * XCOL, 4 * (XCOL + C)), V("xin"), Fn.Copy, scale=0.5)

    st = {"cur": cur0}
    xsrc = "xin"

    for t in range(R):
        last = t == R - 1
        qn, sn = ("qx0", "sx0") if t == 0 else ("qx", "sx")
        quant(qn, sn, HEAD, 128, V(xsrc, 4 * HEAD))
        mm(1, "qu2", "su2", 0, qn, sn, HEAD, 128)
        quant(qn, sn, 0, HEAD, V(xsrc, 0, 4 * HEAD))
        mm(0, "qu2", "su2", 0, qn, sn, 0, C)
        mm(2, "qu2", "su2", 0, qn, sn, 0, C)
        tt(V("sm", HEAD), V("ps1", 0, 128), V("maska", HEAD), Op.add)
        scan(V("hold", HEAD), V("reset", HEAD), V("sm", HEAD), -FAROFF, Op.add, Op.max)
        tt(V("sm", 0, HEAD), V("ps0", 0, HEAD), V("maska", 0, HEAD), Op.add)
        if FIRST:
            calls[-1]["need"].setdefault(len(calls) - 1 - FIRST, False)
        scan(V("hold", 0, HEAD), V("reset", 0, HEAD), V("sm", 0, HEAD), -FAROFF, Op.add, Op.max)
        if t == 0:
            send(0, qn, sn, C - E)
        else:
            acc, bias, tf, toff = nw(2), nw(2), nw(8), nw(8, "wu")
            lin(bias, V("cf", K0, K0 + 2), 1.0, V("cg", UP - 1, UP))
            for k in range(2):
                act(V("junk2", k * UP, (k + 1) * UP), V("cg"), Fn.Sign, bias=sub(bias, k, k + 1), scale=-1.0, acc=sub(acc, k, k + 1))
            for k in range(2):
                lin(V("w", tf[3] + k, tf[3] + 8, 2), V("im4", 0, 4), 0.5, sub(acc, k, k + 1))
            ts(toff, tf, 2.0, Op.mult, float(4 * (C - UP) + 2 * UP), Op.add)
            for j in range(4):
                act(V("tt", j, 4 * E, 4), ind(V("xt"), sub(toff, 2 * j, 2 * j + 2)), Fn.Copy)
            quant("qt%d" % (t - 1), "st%d" % (t - 1), 0, 128, V("tt"))
            send(t, "qt%d" % (t - 1), "st%d" % (t - 1), 0)
            lev = st["lev"]
            thr = [lev] + [nw() for k in range(t)]
            for k in range(1, t + 1):
                act(thr[k], lev, Fn.Abs, bias=-float(C * k))
            lin(V("tab", 0, C, F), V("tabi", 0, E), -4, -4 * BCOL[t])
            lin(V("tab", C, 3 * C, C), V("tabi", 0, 2), 0, -4 * BCOL[t])
            for k in range(t):
                c = V("cp", k * C, (k + 1) * C - 1)
                lin(V("cp", k * C, (k + 1) * C), ind(V("tabl"), sub(off, k * NB, (k + 1) * NB)), 1.0)
                lin(V("cp", k * C + F - 1, (k + 1) * C, F), V("tabi", 0, E), -4, -4 * (BCOL[t] + 1))
                scan(V("tab", (k + 1) * C + 1, (k + 2) * C), c, c, -4.0 * BCOL[t], Op.mult, Op.min)
            tt(V("pk"), ind(V("tab", 0, (t + 1) * C), lu), V("hi"), Op.subtract)
        b1, b2, rk = nw(), nw(), nw()
        jk = 0
        adds = {1: [], 3: [], 4: []}
        if NV:
            lin(V("holdb", 0, 16 * NV), ind(V("hold", 0, 16 * NV), sub(ends, 0, NV)), 1.0, 0.0, HWHO)
        for k, (wd, slots) in enumerate(TILES):
            qm, sm = "qm%d" % k, "sm%d" % k
            for e, m in enumerate(slots):
                if m == "band":
                    tt(V("m%d" % k, e, 4 * C, 4), V("ps0", 0, C), V("hold"), Op.is_le)
                    scan(V("segb"), V("segr"), V("m%d" % k, e, 4 * C, 4), 0.0, Op.mult, Op.add)
                    tt(b1, bcw, V("segb", 15, C, 16), Op.subtract)
                    continue
                o, s, j = V("m%d" % k, e, 64 * m, 4), V("hold", 16 * m + 15, 16 * m + 16), V("junk", jk, jk + 16 * m)
                if m < NV:
                    d = 16 * (NV - m)
                    tt(o, V("ps0", 0, 16 * m), V("holdb", d, 16 * NV), Op.is_lt)
                    adds[4].append(("qe", "se", 128 * e, qm, sm, PAD - d, 128))
                    continue
                jk += 16 * m
                rows = V("rv", RS * (m + 1) - 1, RS * (m + 1))
                if m in ONACT:
                    act(j, V("ps2", 0, 16 * m), Fn.Sign, bias=s, scale=-1.0)
                    act(o, j, Fn.Relu, acc=rows)
                    continue
                ts(o, V("ps0", 0, 16 * m), s, Op.is_lt)
                count(V("rv", RS * (m + 1) - 8 * m, RS * (m + 1)), rows, o, V("m%d" % k, e, 32 * m, 4),
                      V("m%d" % k, 32 * m + e, 64 * m, 4), j, "v" if m in ONVEC else "a" if m in ONSCA else "*")
            quant(qm, sm, PAD, wd, V("m%d" % k, 0, 4 * wd))
            if wd > 128:
                adds[1].append(("qbd", "sbd", 0, qm, sm, PAD, wd))
            adds[3].append(("qbd", "sbd", 0, qm, sm, PAD, 128))
        for bank, items in adds.items():
            free = []
            for k, item in enumerate(items):
                mm(bank, *item, start=k == 0, stop=k == len(items) - 1, free=free if 0 < k < len(items) - 1 else None)
        if NV:
            scan(V("seg", 0, 16 * NV), V("segr", 0, 16 * NV), V("ps4", 0, 16 * NV), 0.0, Op.mult, Op.add)
            tt(sub(b2, 0, NV), V("seg", 15, 16 * NV, 16), sub(b1, 0, NV), Op.subtract)
        tt(sub(b2, NV, NB), V("rv", RS * (NV + 1) - 1, None, RS), sub(b1, NV, NB), Op.subtract)
        scan(V("cw", 128), V("maskc", 128), V("ps1", 128, C), 0.0, Op.add, Op.min)
        scan(V("cw", 0, 128), V("maskc", 0, 128), V("ps3", 0, 128), 0.0, Op.add, Op.min)
        n = (t + 1) * NB
        cw = V("cw", 15, C, 16)
        if t == 0:
            tt(V("ng", 8, 8 * (1 + NB), 8), cw, b2, Op.is_ge)
        tt(rk, cw, b2, Op.subtract)
        for k in range(t + 1 if t else 0):
            tt(V("ng", 8 * (1 + k * NB), 8 * (1 + (k + 1) * NB), 8), rk, thr[k], Op.is_ge)
        nn = max(128, 2 * n)
        quant("qn", "sn", 0, nn + 2, V("ng", 0, 4 * (nn + 2)))
        mm(3, "qtri", "stri", 0, "qn", "sn", 2, nn, stop=False)
        mm(3, "qtru", "stru", 0, "qn", "sn", 0, nn, start=False)
        pr, od, posu, sums = nw(4 * NB), nw(n), nw(NB, "wu"), nw(4 * NB)
        w0 = pr[3]
        if t == 0:
            ts(V("w", w0 + 1, w0 + 2 * NB, 2), rk, 0.0, Op.min)
            scan(V("w", w0, w0 + 2 * NB, 2), V("ps3", 0, 2 * n, 2), sub(zero, 0, n), 0.0, Op.add, Op.add)
            scan(sub(sums, 0, 2 * NB), V("ng", 4, 4 + 8 * NB, 4), sub(pr, 0, 2 * NB), 0.0, Op.mult, Op.add)
        else:
            ts(V("w", w0, w0 + (t + 2) * NB, t + 2), rk, 0.0, Op.min)
            scan(od, V("ps3", 0, 2 * n, 2), sub(zero, 0, n), 0.0, Op.add, Op.add)
            for k in range(t + 1):
                tt(V("w", w0 + k + 1, w0 + (t + 2) * NB, t + 2), sub(od, k * NB, (k + 1) * NB),
                   V("ng", 8 * (1 + k * NB), 8 * (1 + (k + 1) * NB), 8), Op.mult)
            scan(sub(sums, 0, n + NB), sub(runs[t], 0, n + NB), sub(pr, 0, n + NB), 0.0, Op.mult, Op.add)
        pos = V("w", sums[3] + t + 1, sums[3] + n + NB, t + 2)
        ts(posu, pos, float(A), Op.add)
        for b in range(4):
            mm(4 + b, "qe", "se", 128 * b, "ql", "sl", LAND[t], 128)
            if t == 0 and ZADD:
                tt(V("zall", b, 4 * C, 4 * F), V("ps%d" % (4 + b), 0, E), V("xin", b, 4 * C, 4 * F), Op.add)
            else:
                lin(V("big", 4 * BCOL[t] + b, 4 * (BCOL[t] + E), 4), V("ps%d" % (4 + b), 0, E), 0.5)
        ej, pk = V("ej"), V("pk" if t else "pk0")
        run("v", lambda posu=posu, pk=pk: g.vector.tensor_copy(ej[0].indirect(posu[0]), pk[0]), [pk, posu], [ej], 0.05 + 2 * GATHER * C)
        scan(V("ew"), V("maskd"), V("ej", 0, NJ), 0.0, Op.add, Op.max)
        nq = NJ // 4
        ew, hu = V("ew", 3, NJ, 4), nw(nq, "wu")
        ts(hu, ew, -4.0 / KEY, Op.mult, col(TH), Op.add)
        if t == 0 and ZADD:
            for a, b, who in Z0:
                scaled(who, V("zt", 16 * a, 16 * b), ind(V("zall"), sub(hu, a, b)), 0.5)
        else:
            vi, lo_, lou = nw(nq, "wi"), nw(nq, "wi"), nw(nq, "wu")
            ts(vi, ew, -1.0, Op.mult, col(C2 + t), Op.add)
            ts(lo_, vi, KEY // 4 - 1, Op.bitwise_and)
            ts(lou, lo_, col(TC), Op.add)
            for a, b in zip(ZCH, ZCH[1:]):
                act(V("own", 16 * a, 16 * b), ind(V(xsrc), sub(hu, a, b)), Fn.Copy, scale=0.5)
                tt(V("zt", 16 * a, 16 * b), ind(V("big", 4 * BCOL[t], 4 * HCOL[t]), sub(lou, a, b)), V("own", 16 * a, 16 * b), Op.add)
                if a and AHEAD:
                    for k in (1, 2):
                        calls[-k]["need"].setdefault(len(calls) - k - 2, False)
        q0 = 0
        for j, (a, b, who) in enumerate(ZMM):
            wd = max(128, b - a)
            quant("qz", "sz", q0, wd, V("zt", 4 * (b - wd), 4 * b))
            for k in range(4):
                bank = (4 + 4 * j + k) % 8
                mm(bank, "qw", "sw", 128 * k, "qz", "sz", q0, wd)
                scaled(who[k], V("big", 4 * (HCOL[t] + a) + k, 4 * (HCOL[t] + b), 4), V("ps%d" % bank, wd - (b - a), wd), 2.0 ** -6)
            q0 += wd
        nlist = (5 if last else 6 + t) * NB
        pb, s0, nl, cur, sel, xo = nw(), nw(), nw(), nw(nlist), nw(), nw(nlist, "wu")
        lin(pb, pos, 4, 4 * (A + HCOL[t] - XCOL))
        lin(s0, pos, -1e5, (B - 0.5) * 1e5)
        tt(nl, pb, s0, Op.min)
        tt(sub(cur, 0, NB), nl, st["cur"], Op.max)
        for k in range(1, 4):
            lin(sub(cur, k * NB, (k + 1) * NB), sub(cur, 0, NB), 1, k)
        act(sel, s0, Fn.Sign)
        lf, of = sub(cur, 4 * NB, 5 * NB), sub(cur, 5 * NB, nlist)
        lu, off = sub(xo, 4 * NB, 5 * NB), sub(xo, 5 * NB, nlist)
        if not last:
            act(V("go"), ind(V("tabi"), sub(posu, NB - UP // 16, NB)), Fn.Sign, bias=A - 0.5, scale=-1.0)
            scan(V("cg"), V("go"), V("ones", 0, UP), 0.0, Op.add, Op.add)
            lin(sel, sel, C / 2, C / 2)
        if t == 0:
            st["nl0"], st["lev"] = nl, sel
            lin(of, nl, 0.25, XCOL - HCOL[0] + 1)
            tt(lf, sel, iw, Op.add)
        elif t == 1:
            s1, s2, o1, o2, st["lev"] = nw(), nw(), nw(), nw(2 * NB), nw()
            lin(s1, lev, -100, 1e4)
            lin(s2, lev, 100, -1e4)
            tt(o1, nl, s1, Op.min)
            tt(sub(o2, NB, 2 * NB), nl, s2, Op.min)
            tt(sub(o2, 0, NB), o1, st["nl0"], Op.max)
            lin(of, o2, 0.25, XCOL - HCOL[0] + 1)
            tt(st["lev"], lev, sel, Op.add)
            tt(lf, st["lev"], iw, Op.add)
        else:
            lin(lf, lev, 2.0 / C, 1.25)
            tt(lf, lf, sel, Op.add)
        cp(xo, cur)
        if last:
            act(V("olv"), ind(V("tabi", 0, 16), lu), Fn.Copy, scale=0.5)
            dma("s", T.ol[:], T.olv[0:128:16, :], [V("olv")], [])
        win = V("big", 4 * XCOL, 4 * (HCOL[t] + NJ))
        pieces = FIN if last else MID
        for j, (a, b) in enumerate(pieces):
            for k in range(4):
                scaled(XWHO[k], V("xt", 64 * a + k, 64 * b, 4), ind(win, sub(xo, k * NB + a, k * NB + b)), 2.0)
            if last:
                a, b = 16 * a, 16 * b
                quant("qx", "sx", a, b - a, V("xt", 4 * a, 4 * b))
                mm(j, "qv", "sv", 0, "qx", "sx", a, b - a)
                scaled(YWHO[j], V("yb", a, b), V("ps%d" % j, 0, b - a), 1.0)
                if not OUTONE:
                    dma(OCQ[j], T.oc[:, 4 * a:4 * b], T.qx[:, a:b].bitcast(dt.uint8), [V("qx", a, b)], [])
                    dma(YQ[j], T.y[:, a:b], T.yb[:, a:b], [V("yb", a, b)], [])
        if last and OUTONE:
            dma(OCQ[0], T.oc[:], T.qx[:].bitcast(dt.uint8), [V("qx")], [])
            dma(YQ[0], T.y[:], T.yb[:], [V("yb")], [])
        xsrc = "xt"
        st["cur"] = sub(cur, 0, NB)

    for k in range(4):
        dma(OSQ[k], T.osc[4 * k:4 * k + 4, :], T.sx[32 * k:32 * k + 4, :], [V("sx", 0, 8)] + [V("sx")], [])
    issue()
